import numpy as np, ml_dtypes
CORES = [78,86,94,102,110,118]
N = 6
BF = ml_dtypes.bfloat16
V, M, L, P, TV, HS = 4096, 1024, 256, 16, 5, (1, 2, 3, 5, 8)
def pushed(ls, s, n):
    return np.take_along_axis(ls.reshape(N, 8, 16 * M), (s & 15) * M + (((s * s >> 5) + s + 77 * n) & (M - 1)), 2)
def parts(rng):
    kd = rng.permutation(np.arange(V) & 3); pool = np.argsort(kd, kind="stable").reshape(4, V >> 2)
    own = np.where(rng.random((N, 8, V)) < 0.02, rng.integers(0, 4, (N, 8, V)), kd); proto = rng.integers(0, 16, (N, 8, 16, 4))
    x = np.clip(np.take_along_axis(proto, own[:, :, None], 3) + rng.integers(-1, 2, (N, 8, 16, V)), 0, 15)
    ls = rng.integers(0, V, (N, 8, 16, M)); s = rng.integers(0, 4096, (N, 8, L))
    n = np.where(rng.random((N, 8, L)) < 0.5, rng.integers(15, 17, (N, 8, L)), rng.integers(0, 17, (N, 8, L)))
    return kd, pool, x, ls, s, n, rng.integers(10, 30, (N, 8)), rng.integers(0, 256, (N, 8, 16))
def spell(rng, ls, s, n, kd, pool, p):
    a = kd[pushed(ls, s, n)]; b = (a + rng.integers(1, 4, a.shape)) & 3; j = np.arange(1, 17)[:, None]; sh = (N, 8, 16, L)
    k = np.where(j % np.maximum(p, 1)[:, :, None] == 0, a[:, :, None], b[:, :, None])
    cut = np.maximum(2 * p, rng.integers(0, 17, p.shape))[:, :, None]
    k = np.where((p[:, :, None] == 0) | (j >= cut), rng.integers(0, 4, sh), k)
    return pool[k, rng.integers(0, V >> 2, sh)]
def two(a, b, p):
    j = np.arange(1, 17)[:, None]; q = np.where(p == 0, 99, p)[:, :, None]
    return np.where(j % q == 0, a[:, :, None], b[:, :, None])
def pack(x, ls, w, s, n, th, wt):
    w = np.where(np.arange(16)[:, None] < n[:, :, None, :], w, 0)
    return {"x": np.ascontiguousarray(x.reshape(N, 128, V)).astype(np.float32).astype(BF), "ls": np.ascontiguousarray(ls.reshape(N, 128, M)).astype(np.int32),
            "wd": np.ascontiguousarray(w.reshape(N, 128, L)).astype(np.int32), "nl": n.astype(np.int32), "sd": s.astype(np.int32),
            "th": np.ascontiguousarray(th.reshape(N, 8, 1)).astype(np.int32), "wt": np.ascontiguousarray(wt.reshape(N, 128, 1)).astype(np.int32)}
def setup_inputs(rng):
    kd, pool, x, ls, s, n, th, wt = parts(rng); p = rng.choice(np.array((0, 0) + HS), (N, 8, L))
    return pack(x, ls, spell(rng, ls, s, n, kd, pool, p), s, n, th, wt)
def setup_inputs_corners(rng):
    kd, pool, x, ls, s, n, th, wt = parts(rng); sh = (N, 8, L)
    ls = np.where(rng.random(ls.shape) < 0.2, rng.choice(np.array([0, V - 1]), ls.shape), ls)
    edge = np.array(sorted({0, 1, 15, 16} | {2 * h - 2 for h in HS} | {2 * h - 1 for h in HS})); p = rng.choice(np.array(HS), sh); u = rng.random(sh)
    n = np.where(u < 0.4, 2 * p - 2, np.where(u < 0.7, 2 * p - 1, rng.choice(edge, sh)))
    n[0, 0] = 0; n[N - 1, 7] = 16; n[:, 3] = rng.choice(np.array([0, 16]), (N, L))
    s = np.where(rng.random(sh) < 0.3, rng.choice(np.array([0, 15, 16, 4095]), sh), s)
    th = rng.choice(np.array([0, 1, 20, 240]), (N, 8)); wt = rng.choice(np.array([0, 1, 255]), (N, 8, 16))
    p[N - 1, 7] = 8; th[N - 1, 7] = 0
    c = int(rng.integers(1, N - 1))
    x[c] = 8 * (np.arange(V) & 1) + rng.integers(0, 3, (8, 16, V)); th[c] = 8; th[c - 1] = 240
    ls[c - 1] |= 1; ls[c] -= ls[c] & 1
    n[c - 1] = 0; n[c] = np.maximum(n[c], 1); n[c, 7, L - 1] = 0
    a = pushed(ls, s, n); u = rng.integers(0, 4, sh); own = P * np.arange(L) + rng.integers(0, P, sh)
    b = np.where(u == 0, 0, np.where(u == 1, V - 1, np.where(u == 2, own, rng.integers(0, V, sh))))
    w = two(a, b, p); w[c, :, 0] = a[c]
    return pack(x, ls, w, s, n, th, wt)
def setup_inputs_ties(rng):
    kd, pool, x, ls, s, n, th, wt = parts(rng); sh = (N, 8, L); half = V >> 3
    th = rng.integers(16, 61, (N, 8)); val = np.stack([0 * th, th, th + 1, 2 * th + 1], -1)
    loose = np.ones(V, np.int64); loose[pool[:, :half]] = 0
    e = val[:, :, kd] + loose * rng.integers(0, 17, (N, 8, V)); x = (e[:, :, None] + np.arange(16)[:, None]) >> 4
    ls = np.where(rng.random(ls.shape) < 0.8, pool[rng.integers(0, 4, ls.shape), rng.integers(0, half, ls.shape)], ls)
    p = rng.choice(np.array(HS), sh); a = kd[pushed(ls, s, n)]; b = np.array([3, 3, 0, 0])[a]
    c = np.where(rng.random(sh) < 0.6, np.array([1, 0, 3, 2])[a], np.array([2, 3, 0, 1])[a])
    k = np.where(np.arange(1, 17)[:, None] == p[:, :, None], c[:, :, None], two(a, b, p))
    return pack(x, ls, pool[k, rng.integers(0, half, k.shape)], s, n, th, wt)
def setup_inputs_again(rng):
    kd, pool, x, ls, s, n, th, wt = parts(rng)
    few = np.concatenate([np.arange(4 * P), V - 4 * P + np.arange(4 * P)])
    x = np.clip(rng.integers(0, 16, (N, 8, 16, 1)) + rng.integers(-3, 4, (N, 8, 16, V)), 0, 15); th = rng.integers(24, 44, (N, 8))
    ls = few[rng.integers(0, 8 * P, ls.shape)]; w = few[rng.integers(0, 8 * P, (N, 8, 16, L))]
    q = int(rng.integers(0, N)); n[q] = np.maximum(n[q], 1); w[q, :, 0] = pushed(ls, s, n)[q]
    return pack(x, ls, w, s, n, th, wt)
def setup_inputs_spread(rng):
    sh = (N, 8, L)
    x = np.minimum((np.exp2(4 * rng.random((N, 8, 1, V))) * rng.random((N, 8, 16, V))).astype(np.int64), 15)
    ls = np.minimum((V * rng.random((N, 8, 16, M)) * np.sqrt(rng.random((N, 8, 16, M)))).astype(np.int64), V - 1)
    w = np.minimum((np.exp2(np.log2(V) * rng.random((N, 8, 16, L)))).astype(np.int64), V - 1)
    s = np.where(rng.random(sh) < 0.5, rng.integers(0, 4096, sh), np.minimum(np.exp2(12 * rng.random(sh)).astype(np.int64), 4095))
    wt = np.minimum(np.exp2(8 * rng.random((N, 8, 16))).astype(np.int64) - 1, 255)
    return pack(x, ls, w, s, rng.integers(0, 17, sh), rng.integers(0, 241, (N, 8)), wt)
def setup_inputs_ends(rng):
    sh = (N, 8, L)
    u = rng.integers(0, 3, (N, 8, 1, V)); x = 15 * np.where(u == 2, rng.integers(0, 2, (N, 8, 16, V)), u)
    x[:, 1:7:2, :, 0] = 0; x[:, 1:7:2, :, V - 1] = 15; x[:, 7, :, 0] = 0; x[:, 7, :, V - 1] = 15; x[:, 0, :, 0] = 15; x[:, 0, :, V - 1] = 0
    ls = (V - 1) * rng.integers(0, 2, (N, 8, 16, M)); s = 4095 * rng.integers(0, 2, sh); n = 16 * (rng.random(sh) < 0.75).astype(np.int64)
    th = 240 * rng.integers(0, 2, (N, 8)); th[:, 7] = 0; th[:, 6] = 240
    wt = 255 * rng.integers(0, 2, (N, 8, 16)); wt[:, 7] = 255; wt[:, 0] = 0
    p = rng.choice(np.array((0,) + HS), sh)
    for i, k in ((0, 0), (1, 8), (7, 0), (10, 8), (L - 2, 8), (L - 1, 0)):
        s[:, 7, i] = 4095; n[:, 7, i] = 16; p[:, 7, i] = k
    ls[:, 7, 15, ((4095 * 4095 >> 5) + 4095 + 77 * 16) & (M - 1)] = V - 1
    a = pushed(ls, s, n)
    return pack(x, ls, two(a, V - 1 - a, p), s, n, th, wt)
def check_inputs(d):
    bad = []
    for k, lo, hi in (("x", 0, 15), ("ls", 0, V - 1), ("wd", 0, V - 1), ("nl", 0, 16), ("sd", 0, 4095), ("th", 0, 240), ("wt", 0, 255)):
        v = np.asarray(d[k]).astype(np.float64)
        if not np.all((v >= lo) & (v <= hi)): bad.append("range of " + k)
        if not np.all(v == np.floor(v)): bad.append("whole numbers in " + k)
    w = np.asarray(d["wd"]).reshape(N, 8, 16, L); n = np.asarray(d["nl"]).reshape(N, 8, 1, L)
    if np.any((np.arange(16)[:, None] >= n) & (w != 0)): bad.append("empty rows of wd")
    return bad
def reference(x, ls, wd, nl, sd, th, wt):
    X = x.astype(np.float32).astype(np.int32).reshape(N, 8, 16, V); tab = ls.astype(np.int64).reshape(N, 8, 16 * M)
    w = wd.astype(np.int64).reshape(N, 8, 16, L); n = nl.astype(np.int64); s = sd.astype(np.int64)
    lim = th.astype(np.int64).reshape(N, 8, 1, 1); wgt = wt.astype(np.int64).reshape(N, 8, 16, 1)
    A = np.zeros(N, np.int64); row = np.arange(16)[:, None]
    for t in range(TV):
        new = np.take_along_axis(tab, (s & 15) * M + (((s * s >> 5) + s + 77 * n) & (M - 1)), 2)
        w = np.concatenate([new[:, :, None], w[:, :, :15]], axis=2); n = np.minimum(n + 1, 16)
        G = np.take_along_axis(X, w.reshape(N, 8, 1, 16 * L), 3).reshape(N, 8, 16, 16, L)
        bound = lim + (A & 15).reshape(N, 1, 1, 1); h = np.zeros((N, 8, L), np.int64)
        for k in HS:
            D = np.add.reduce(np.abs(G[:, :, :, :k] - G[:, :, :, k:2 * k]), axis=2)
            h = np.where((h == 0) & (2 * k <= n) & np.all(D <= bound, axis=2), k, h)
        hit = h > 0
        z = np.maximum.reduce(np.where(row < h[:, :, None, None, :], G, 0), axis=3)
        tot = np.add.reduce(wgt * np.where(hit[:, :, None], z, G[:, :, :, 0]), axis=2)
        s = np.where(hit, tot + h, 5 * s + tot) & 4095
        at = row + h[:, :, None, :]
        w = np.where(at < 16, np.take_along_axis(w, np.minimum(at, 15), 2), 0); n = n - h
        col = np.roll(P * np.arange(L) + (s & (P - 1)), 1, axis=0)[:, :, None]
        old = np.take_along_axis(X, col, 3)
        val = np.where(np.roll(hit, 1, axis=0)[:, :, None], (old + np.roll(z, 1, axis=0)) >> 1, old)
        np.put_along_axis(X, col, val.astype(np.int32), 3)
        A = np.add.reduce(hit.astype(np.int64).reshape(N, 8 * L), axis=1)
        if t < TV - 1:
            by = 1 + (t + 1) // N - t // N
            w, n, s = [np.roll(np.roll(v, 1, axis=0), by, axis=1) for v in (w, n, s)]
    return {"yx": X.reshape(N, 128, V).astype(np.float32).astype(BF), "yw": w.reshape(N, 128, L).astype(np.float32), "yn": n.astype(np.float32), "ys": s.astype(np.float32)}

@@ -1,0 +1,628 @@
+from concourse.mybir import AluOpType as A, AxisListType, ActivationFunctionType as F
+
+HS = (8, 5, 3, 2, 1)
+BASE = {8: 1, 5: 9, 3: 14, 2: 17, 1: 19}
+SLOT = {1: 0, 2: 1, 3: 2, 5: 4, 8: 7, 0: 5}
+TV = 5
+MAXED = (1, 2, 3)
+PAIRS = [(h, j) for h in (5, 3, 2, 1) for j in range(h)]
+
+SCRATCH = {
+    "X": ("sbuf", [128, 8192], "bfloat16"), "LS": ("sbuf", [128, 1024], "int32"), "LSN": ("sbuf", [128, 1024], "int32"),
+    "SH": ("sbuf", [128, 2048], "float32"), "GL": ("sbuf", [128, 2048], "bfloat16"), "GH": ("sbuf", [128, 2048], "bfloat16"),
+    "D8": ("sbuf", [128, 2048], "bfloat16"), "DL": ("sbuf", [128, 11 * 256], "bfloat16"), "ZC": ("sbuf", [128, 2048], "bfloat16"),
+    "ZR": ("sbuf", [128, 2048], "bfloat16"), "NEG": ("sbuf", [128, 256], "bfloat16"),
+    "M1S": ("sbuf", [128, 5 * 288], "bfloat16"), "M1R": ("sbuf", [128, 5 * 288], "bfloat16"),
+    "MLS": ("sbuf", [128, 5 * 16], "uint16"), "MLR": ("sbuf", [128, 5 * 16], "uint16"),
+    "MNS": ("sbuf", [128, 5 * 32], "float32"), "MNR": ("sbuf", [128, 5 * 32], "float32"),
+    "W2": ("sbuf", [128, 5 * 256], "float32"), "W2R": ("sbuf", [128, 5 * 256], "float32"),
+    "LF": ("sbuf", [128, 5 * 256], "float32"), "LFR": ("sbuf", [128, 5 * 256], "float32"),
+    "IDB": ("sbuf", [128, 128], "bfloat16"), "NIB": ("sbuf", [128, 128], "bfloat16"), "IDF": ("sbuf", [128, 128], "float32"),
+    "ONE": ("sbuf", [128, 128], "bfloat16"), "ONEF": ("sbuf", [128, 128], "float32"), "ROW0": ("sbuf", [128, 128], "float32"),
+    "RA": ("sbuf", [128, 512], "float32"), "ME": ("sbuf", [128, 288], "float32"),
+    "KB": ("sbuf", [128, 8], "bfloat16"), "KF": ("sbuf", [128, 8], "float32"), "K256": ("sbuf", [128, 8], "bfloat16"),
+    "K2": ("sbuf", [128, 8], "bfloat16"), "KN": ("sbuf", [128, 8], "bfloat16"), "WTB": ("sbuf", [128, 8], "bfloat16"),
+    "CP": ("sbuf", [128, 1280], "bfloat16"), "DB": ("sbuf", [128, 160], "bfloat16"), "RB": ("sbuf", [128, 160], "bfloat16"),
+    "D0": ("sbuf", [128, 160], "bfloat16"), "C2": ("sbuf", [128, 160], "bfloat16"), "THR": ("sbuf", [128, 320], "float32"),
+    "E": ("sbuf", [128, 320], "bfloat16"), "SC2": ("sbuf", [128, 320], "bfloat16"),
+    "EK": ("sbuf", [128, 288], "bfloat16"), "EC": ("sbuf", [128, 288], "float32"), "RS": ("sbuf", [128, 288], "bfloat16"),
+    "EV": ("sbuf", [128, 256], "bfloat16"), "EL": ("sbuf", [128, 256], "float32"),
+    "LS9": ("sbuf", [128, 18], "uint16"), "LK9": ("sbuf", [128, 18], "uint16"), "LU": ("sbuf", [128, 16], "uint16"), "ROT": ("sbuf", [128, 2], "uint16"),
+    "BI": ("sbuf", [128, 16], "float32"), "B8": ("sbuf", [128, 16], "bfloat16"), "B16": ("sbuf", [128, 16], "bfloat16"),
+    "II": ("sbuf", [128, 128], "int32"), "IM": ("sbuf", [128, 288], "int32"), "IG": ("sbuf", [128, 8], "int32"), "I20": ("sbuf", [128, 160], "int32"),
+    "IP": ("sbuf", [128, 4], "int32"), "IK": ("sbuf", [128, 16], "int32"), "I9": ("sbuf", [128, 18], "int32"), "IU": ("sbuf", [128, 16], "int32"),
+    "P15": ("sbuf", [128, 1], "float32"), "PB": ("sbuf", [128, 2], "float32"), "P15I": ("sbuf", [128, 4], "int32"),
+    "SDI": ("sbuf", [8, 256], "int32"), "NLI": ("sbuf", [8, 256], "int32"), "SDF": ("sbuf", [8, 256], "float32"), "NLF": ("sbuf", [8, 256], "float32"),
+    "WTI": ("sbuf", [128, 1], "int32"), "WTF": ("sbuf", [128, 1], "float32"), "THI": ("sbuf", [128, 1], "int32"), "THF": ("sbuf", [128, 1], "float32"),
+    "WI": ("sbuf", [128, 256], "int32"), "LH": ("sbuf", [128, 256], "uint16"), "L1": ("sbuf", [128, 16], "uint16"), "L2": ("sbuf", [128, 16], "uint16"),
+    "LLU": ("sbuf", [128, 16], "uint16"), "CL": ("sbuf", [128, 16], "uint16"), "KBI": ("sbuf", [128, 16], "int32"),
+    "N0": ("sbuf", [128, 16], "float32"), "N1": ("sbuf", [128, 16], "float32"), "NP": ("sbuf", [128, 16], "float32"),
+    "NH": ("sbuf", [128, 16], "float32"), "H": ("sbuf", [128, 16], "float32"), "H1": ("sbuf", [128, 16], "float32"),
+    "S5": ("sbuf", [128, 16], "float32"), "AD": ("sbuf", [128, 16], "float32"), "DU": ("sbuf", [128, 16], "int32"),
+    "SUM": ("sbuf", [128, 16], "int32"), "V15": ("sbuf", [128, 16], "int32"), "VV": ("sbuf", [128, 16], "int32"), "SI": ("sbuf", [128, 16], "int32"),
+    "S15": ("sbuf", [128, 16], "int32"), "T1": ("sbuf", [128, 16], "int32"), "T2": ("sbuf", [128, 16], "int32"), "U": ("sbuf", [128, 16], "int32"), "CI": ("sbuf", [128, 16], "int32"),
+    "MK": ("sbuf", [128, 256], "float32"), "MM": ("sbuf", [128, 256], "float32"), "LW": ("sbuf", [128, 16], "float32"),
+    "XT": ("sbuf", [128, 256], "bfloat16"), "XU": ("sbuf", [128, 256], "bfloat16"),
+    "NS": ("sbuf", [128, 1], "float32"), "AI": ("sbuf", [128, 1], "int32"), "BC": ("sbuf", [128, 1], "float32"), "AJ": ("sbuf", [128, 1], "int32"),
+    "YW": ("sbuf", [128, 256], "float32"), "YN": ("sbuf", [8, 256], "float32"), "YS": ("sbuf", [8, 256], "float32"), "SF": ("sbuf", [128, 16], "float32"),
+    "PG": ("psum", [128, 2048], "float32"), "B4": ("psum", [128, 512], "float32"), "B5": ("psum", [128, 512], "float32"),
+    "PD0": ("psum", [128, 512], "float32"), "PD1": ("psum", [128, 512], "float32"),
+}
+_ARR = ["%s%d" % (n, t) for n in ("M1", "ML", "MN", "W2", "LF") for t in range(TV)] + ["LS"]
+_DMA = ["small", "sm2", "ls", "wd", "x", "sh", "sh2", "oyx", "oyw", "oyn"]
+SEMAPHORES = ["qv", "qa", "qp", "qg", "loc"] + ["r" + n for n in _ARR] + ["d" + n for n in _DMA]
+
+
+def rank_program(g, core, T, topo):
+    rank = T.rank_of(core)
+    if rank is None:
+        return
+    N = len(T.cores)
+    nxt, nx2, prv = T.cores[(rank + 1) % N], T.cores[(rank + 2) % N], T.cores[(rank - 1) % N]
+    V, P, S = g.vector, g.tensor, g.scalar
+    Q = {"v": V, "a": S, "p": P, "g": g, "s": g.sync}
+
+    tot = {}
+    known = {q: {} for q in Q}
+    lastw, readers, banks, ops = {}, {}, {}, []
+
+    def need(q, deps):
+        for o in sorted(deps, reverse=True):
+            sem, val, snap, dma = ops[o]
+            if known[q].get(sem, 0) >= val:
+                continue
+            if dma:
+                val = tot[sem]
+            Q[q].wait_ge(T.sem[sem], val)
+            for s_, v_ in snap.items():
+                known[q][s_] = max(known[q].get(s_, 0), v_)
+            known[q][sem] = val
+
+    def deps_of(q, r, w, b):
+        d = set()
+        for k in r:
+            d.update(lastw.get(k, ()))
+        for k in w:
+            d.update(lastw.get(k, ()))
+            d.update(readers.get(k, ()))
+        for k in b:
+            d.update(o for q_, o in banks.get(k, {}).items() if q_ != q)
+        return d
+
+    def note(q, sem, inc, r, w, b, dma=False):
+        tot[sem] = tot.get(sem, 0) + inc
+        o = len(ops)
+        ops.append((sem, tot[sem], dict(known[q]) if q else {}, dma))
+        for k in w:
+            lastw[k] = [o]
+            readers[k] = []
+        for k in r:
+            readers.setdefault(k, []).append(o)
+        for k in b:
+            banks.setdefault(k, {})[q] = o
+        return o
+
+    def run(q, fn, *a, r="", w="", b="", **k):
+        r, w, b = r.split(), w.split(), b.split()
+        need(q, deps_of(q, r, w, b))
+        sem = "q" + q
+        fn(*a, **k).then_inc(T.sem[sem], 1)
+        note(q, sem, 1, r, w, b)
+
+    def v(fn, *a, **k):
+        run("v", fn, *a, **k)
+
+    def act(out, in_, func=F.Copy, r="", w="", b="", **k):
+        run("a", S.activation, out, in_, func, r=r, w=w, b=b, **k)
+
+    def mm(out, l, rh, start=True, stop=True, r="", w="", b=""):
+        r, w, b = r.split(), w.split(), b.split()
+        need("p", deps_of("p", r, [], b))
+        P.matmul(out, l, rh, start, stop).then_inc(T.sem.qp, 1)
+        note("p", "qp", 1, r, w, b)
+
+    def dma(sem, out, in_, r="", w=""):
+        r, w = r.split(), w.split()
+        need("s", deps_of("s", r, w, []))
+        g.sync.dma_start(out, in_).then_inc(T.sem["d" + sem], 16)
+        note("s", "d" + sem, 16, r, w, [], True)
+
+    def send(name, dst, out, in_, r=""):
+        r = r.split()
+        need("g", deps_of("g", r, [], []))
+        rid, pid = topo.addr(dst)[:2]
+        g.remote_dma(out, in_, T.sem["r" + name], T.sem.loc, pid, rid, topo.mask(core, dst))
+        note("g", "loc", len(topo.engines(core, dst)), [], [], [])
+
+    def arrive(name, src, key):
+        n = len(topo.engines(src, core))
+        tot["r" + name] = n
+        lastw[key] = [len(ops)]
+        ops.append(("r" + name, n, {}, False))
+
+    p2 = T.cores[(rank - 2) % N]
+    for t in range(TV):
+        arrive("M1%d" % t, prv, "M1R%d" % t)
+        arrive("ML%d" % t, prv, "MLR%d" % t)
+        if t < 4:
+            arrive("MN%d" % t, prv, "MNR%d" % t)
+            arrive("W2%d" % t, prv, "W2R%d" % t)
+        arrive("LF%d" % t, prv if t in (0, 4) else p2, "LFR%d" % t)
+    arrive("LS", nxt, "LSN")
+
+    v(V.memset, T.THI[:], 0, w="THI")
+    dma("small", T.SDI[:], T.sd[:], w="SDI")
+    dma("small", T.NLI[:], T.nl[:], w="NLI")
+    dma("wd", T.WI[1:128, :], T.wd[0:127, :], w="WIa")
+    dma("wd", T.WI[0:1, :], T.wd[0:1, :], w="WIb")
+    dma("sm2", T.THI[0:128:16, :], T.th[:], w="THI")
+    dma("sm2", T.WTI[:], T.wt[:], w="WTI")
+    dma("x", T.X[:, 0:4096], T.x[:], w="XA XB")
+    dma("ls", T.LS[:], T.ls[:], w="LS")
+
+    def iota(out, pat, base, cm, key):
+        run("g", g.iota, out, pat, base, cm, w=key)
+    iota(T.II[:], [[-1, 128]], 0, 1, "II")
+    iota(T.IG[:], [[-16, 8]], 0, 1, "IG")
+    iota(T.IP[:], [[0, 4]], 0, 1, "IP")
+    iota(T.I9[:, 1:9], [[1, 8]], 0, 0, "I9a")
+    iota(T.I9[:, 10:18], [[1, 8]], 8, 0, "I9b")
+    iota(T.I9[:, 0:1], [[1, 1]], 7, 0, "I9c")
+    iota(T.I9[:, 9:10], [[1, 1]], 15, 0, "I9d")
+    iota(T.IM[:], [[0, 18], [-1, 16]], 0, 1, "IM")
+    iota(T.IU[:], [[1, 16]], 0, 0, "IU")
+    iota(T.IK[:], [[16, 16]], 0, 0, "IK")
+    iota(T.I20[:], [[-16, 8], [0, 20]], 0, 1, "I20")
+    v(V.memset, T.ZR[:], 1.0, w="ZR")
+    act(T.CP[:], T.ZR[:, 0:1280], scale=0.0, r="ZR", w="CP")
+    for c in (4096, 6144):
+        act(T.X[:, c:c + 2048], T.ZR[:], scale=0.0, r="ZR", w="XD")
+    d0k = "D0 " + " ".join("D0%d" % q_ for q_ in (0, 1, 9, 14, 17, 19))
+    c2k = "C2 C20 C28 C213 C216 C218"
+
+    def consts_scan():
+        v(V.memset, T.D0[:], 1.0, w="D0")
+        v(V.memset, T.C2[:], 0.0, w="C2")
+        for q_ in (0, 1, 9, 14, 17, 19):
+            v(V.memset, T.D0[:, q_:160:20], 0.0, r="D0", w="D0%d" % q_)
+        for q_, c in ((0, -2.0), (8, 3.0), (13, 2.0), (16, 1.0), (18, 1.0)):
+            v(V.memset, T.C2[:, q_:160:20], c, r="C2", w="C2%d" % q_)
+
+    v(V.tensor_scalar, T.IDF[:], T.II[:], 0, None, A.is_equal, r="II", w="IDF")
+    v(V.tensor_scalar, T.P15I[:, 1:2], T.IP[:, 0:1], 3, 1, A.arith_shift_right, A.bitwise_and, r="IP", w="P15b")
+    v(V.tensor_copy, T.PB[:, 1:2], T.P15I[:, 1:2], r="P15b", w="PB1")
+    v(V.tensor_scalar, T.PB[:, 0:1], T.P15I[:, 1:2], -1, 1, A.mult, A.add, r="P15b", w="PB0")
+    for b_ in range(2):
+        for w_ in range(2):
+            c = 128 * (2 * b_ + w_)
+            v(V.tensor_scalar, T.RA[:, c:c + 128], T.II[:], 8 * (b_ - w_), T.PB[:, b_:b_ + 1], A.is_equal, A.mult, r="II PB%d" % b_, w="RA%d%d" % (b_, w_))
+    v(V.tensor_copy, T.SDF[:], T.SDI[:], r="SDI", w="SDF")
+    v(V.tensor_copy, T.NLF[:], T.NLI[:], r="NLI", w="NLF")
+    for hf in range(2):
+        mm(T.B4[:, 8 * hf:8 * hf + 8], T.SDF[:, 128 * hf:128 * hf + 128], T.IDF[0:8, 0:8], r="SDF IDF", w="B4sd", b="B4")
+    for hf in range(2):
+        mm(T.B4[:, 16 + 8 * hf:24 + 8 * hf], T.NLF[:, 128 * hf:128 * hf + 128], T.IDF[0:8, 0:8], r="NLF IDF", w="B4sd", b="B4")
+    v(V.memset, T.ROW0[:], 0.0, w="ROW0")
+    v(V.tensor_scalar, T.IG[:], T.IG[:], 4, None, A.arith_shift_right, r="IG", w="IG")
+    v(V.tensor_scalar, T.KB[:], T.IG[:], 0, None, A.is_equal, r="IG", w="KB")
+    v(V.tensor_scalar, T.KF[:], T.IG[:], 0, None, A.is_equal, r="IG", w="KF")
+    v(V.tensor_scalar, T.IM[:], T.IM[:], 15, None, A.bitwise_and, r="IM", w="IM")
+    v(V.tensor_scalar, T.ME[:], T.IM[:], 0, None, A.is_equal, r="IM", w="ME")
+    v(V.tensor_copy, T.LS9[:], T.I9[:], r="I9a I9b I9c I9d", w="LS9")
+    v(V.tensor_scalar, T.LK9[:], T.I9[:], 20, 19, A.mult, A.add, r="I9a I9b I9c I9d", w="LK9")
+    v(V.tensor_copy, T.LU[:], T.IU[:], r="IU", w="LU")
+    v(V.tensor_copy, T.SI[:], T.B4[:, 0:16], r="B4sd", w="SI", b="B4")
+    v(V.tensor_copy, T.N0[:], T.B4[:, 16:32], r="B4sd", w="N0", b="B4")
+    v(V.tensor_scalar, T.P15I[:, 0:1], T.IP[:, 0:1], 15, None, A.bitwise_and, r="IP", w="P15I")
+    v(V.tensor_copy, T.P15[:], T.P15I[:, 0:1], r="P15I", w="P15")
+    v(V.tensor_copy, T.IDB[:], T.IDF[:], r="IDF", w="IDB")
+
+    def push1(ncol, nkey, first=None):
+        if not first:
+            v(V.tensor_tensor, T.T1[:], T.SI[:], T.SI[:], A.mult, r="SI", w="T1")
+            v(V.tensor_scalar, T.U[:], ncol, 77, None, A.mult, r=nkey, w="U")
+        v(V.tensor_scalar, T.S15[:], T.SI[:], 15, None, A.bitwise_and, r="SI", w="S15")
+        if first:
+            first()
+        v(V.tensor_scalar, T.T2[:], T.T1[:], 5, None, A.arith_shift_right, r="T1", w="T2")
+        v(V.tensor_tensor, T.U[:], T.U[:], T.SI[:], A.add, r="U SI", w="U")
+        v(V.tensor_tensor, T.T1[:], T.T2[:], T.U[:], A.add, r="T2 U", w="T1")
+        v(V.tensor_scalar, T.CI[:], T.T1[:], 1023, None, A.bitwise_and, r="T1", w="CI")
+        v(V.tensor_tensor, T.EC[:], T.CI[:].indirect(T.LS9[:]), T.ME[:], A.mult, r="CI LS9 ME", w="EC")
+        v(V.tensor_copy, T.RS[:], T.S15[:].indirect(T.LS9[:]), r="S15 LS9", w="RS")
+
+    def push2(sl):
+        for hf in range(2):
+            mm(T.PG[:, 8 * hf:8 * hf + 8], T.EC[:, 144 * hf + sl:144 * hf + sl + 128], T.KF[:], r="EC KF", w="pC", b="PG0")
+        for hf in range(2):
+            mm(T.PG[:, 512 + 128 * hf:640 + 128 * hf], T.RS[:, 144 * hf + sl:144 * hf + sl + 128], T.IDB[:], r="RS IDB", w="pR", b="PG1")
+
+    def push2a():
+        v(V.tensor_copy, T.CL[:], T.PG[:, 0:16], r="pC", w="CL", b="PG0")
+        v(V.tensor_scalar, T.MK[:], T.PG[:, 512:768], T.P15[:], None, A.is_equal, r="pR P15", w="MK", b="PG1")
+
+    def push2b(ls):
+        v(V.tensor_tensor, T.MM[:], T[ls][:].indirect(T.CL[:]), T.MK[:], A.mult, r=ls + " CL MK", w="MM")
+
+    lwb = {0: (T.B5, 16, "B5"), 1: (T.PG, 1024, "PG2")}
+
+    def push2w(k_=1):
+        B, c, bk = lwb[k_]
+        for hf in range(2):
+            mm(B[:, c + 8 * hf:c + 8 + 8 * hf], T.MM[:, 128 * hf:128 * hf + 128], T.KF[:], r="MM KF", w="pW", b=bk)
+
+    def push2f():
+        mm(T.B5[:, 256:512], T.ROW0[:], T.MM[:], r="MM ROW0", w="pF", b="B5")
+
+    def push3(k_=1):
+        B, c, bk = lwb[k_]
+        v(V.tensor_copy, T.LW[:], B[:, c:c + 16], r="pW", w="LW", b=bk)
+
+    def push3f(t):
+        act(T.LF[:, 256 * t:256 * t + 256], T.B5[:, 256:512], r="pF", w="LF%d" % t, b="B5")
+
+    def push4():
+        v(V.tensor_tensor, T.EL[:], T.LW[:].indirect(T.LU[:]), T.ME[:, 0:256], A.mult, r="LW LU ME", w="EL")
+        for hf in range(2):
+            mm(T.B5[:, 8 * hf:8 * hf + 8], T.EL[:, 128 * hf:128 * hf + 128], T.KF[:], r="EL KF", w="pL", b="B5")
+
+    v(V.tensor_copy, T.W2[:, 0:256], T.WI[:], r="WIa WIb", w="W20")
+    push1(T.N0[:], "N0")
+
+    def rearr(t, b_):
+        w2 = 256 * t
+        out, bk = (T.B4[:, 128:256], "B4") if b_ == 0 else (T.PG[:, 1792:1920], "PG3")
+        for w_ in range(2):
+            c = 128 * (2 * b_ + w_)
+            mm(out, T.RA[:, c:c + 128], T.W2[:, w2 + w_:w2 + 256:2], w_ == 0, w_ == 1, r="W2%d RA%d%d" % (t, b_, w_), w="pH%d" % b_, b=bk)
+
+    def lists(b_):
+        src, bk = (T.B4[:, 128:256], "B4") if b_ == 0 else (T.PG[:, 1792:1920], "PG3")
+        v(V.tensor_copy, T.LH[:, 128 * b_:128 * b_ + 128], src, r="pH%d" % b_, w="LH%d" % b_, b=bk)
+
+    rearr(0, 0)
+    rearr(0, 1)
+    push2(16)
+    lists(0)
+    act(T.KN[:], T.KB[:], scale=-1.0, r="KB", w="KN")
+    act(T.K2[:], T.KB[:], scale=2.0, r="KB", w="K2")
+    act(T.NIB[:], T.IDB[:], scale=-1.0, r="IDB", w="NIB")
+    act(T.ROW0[:, 0:128:16], T.KF[:], r="KF", w="ROW0")
+    cpk = ["CP"] * 5
+    for k_ in (1, 2, 3, 0, 4):
+        rr = k_ % 4
+        for h in HS[k_ // 4:]:
+            for j in (rr, rr - h):
+                if 0 <= j < h:
+                    key, c = "CP%d%d" % (k_, h), 160 * k_ + BASE[h] + j
+                    act(T.CP[:, c:160 * k_ + 160:20], T.KN[:], r="KN CP", w=key)
+                    cpk[k_] += " " + key
+    act(T.SH[:, 768:1024], T.W2[:, 0:256], scale=0.0, r="W20", w="SH3")
+    act(T.SH[:, 1536:1792], T.W2[:, 0:256], scale=0.0, r="W20", w="SH6")
+    act(T.ONEF[:], T.IDF[:], F.Identity, scale=0.0, bias=1.0, r="IDF", w="ONEF")
+    act(T.NEG[:], T.W2[:, 0:256], F.Identity, scale=0.0, bias=-128.0, r="W20", w="NEG")
+    push2a()
+    send("LS", prv, T.LSN[:], T.LS[:], r="LS")
+
+    def first0():
+        lists(1)
+
+    v(V.tensor_copy, T.THF[:], T.THI[:], r="THI", w="THF")
+    v(V.tensor_scalar, T.DB[:], T.I20[:], 0, None, A.is_equal, r="I20", w="DB")
+    v(V.tensor_scalar, T.BC[:], T.THF[:], -1, None, A.mult, r="THF", w="BC")
+
+    shk = "SH3 SH6 SHf SHg " + " ".join("SA%d SB%d" % (h, h) for h in (8, 5, 3, 2, 1, 0))
+
+    def n1(ncol, nkey):
+        v(V.tensor_scalar, T.N1[:], ncol, 1, 16, A.add, A.min, r=nkey, w="N1")
+
+    def thr():
+        for h in HS:
+            e = BASE[h] + h - 1
+            v(V.tensor_scalar, T.THR[:, e:320:20], T.N1[:], 0.5 - 2 * h, 0.0, A.add, A.min, r="N1 THR", w="THR%d" % e)
+    thk = "THR THR0 " + " ".join("THR%d" % (BASE[h] + h - 1) for h in HS)
+
+    def bound():
+        v(V.tensor_scalar, T.RB[:], T.DB[:], T.BC[:], None, A.mult, r="DB BC", w="RB")
+
+    def build_sh(t):
+        for h in (8, 5, 3, 2, 1, 0):
+            c, d = 256 * SLOT[h], 17 - h
+            dma("sh", T.SH[d:128, c:c + 256], T.W2R[0:128 - d, 256 * t:256 * t + 256], r="W2R%d" % t, w="SA%d" % h)
+            dma("sh", T.SH[0:d, c:c + 256], T.W2R[128 - d:128, 256 * t:256 * t + 256], r="W2R%d" % t, w="SB%d" % h)
+        dma("sh2", T.SH[17:128:16, 1280:1536], T.LFR[0:112:16, 256 * t:256 * t + 256], r="LFR%d SA0 SB0" % t, w="SHf")
+        dma("sh2", T.SH[1:2, 1280:1536], T.LFR[112:113, 256 * t:256 * t + 256], r="LFR%d SA0 SB0" % t, w="SHg")
+
+    def idx(h, j):
+        return PAIRS.index((h, j))
+
+    def pd(hf, lo, hi):
+        return (T.PD0 if hf == 0 else T.PD1)[:, lo:hi]
+
+    def place(hf, h, j):
+        return (T.PD0 if hf == 0 else T.PD1)[:, BASE[h] + j:160:20]
+
+    def bulk(t, mid, hole):
+        PGK = "PG0 PG1 PG2 PG3"
+        v(V.tensor_copy, T.GL[:, 1024:1536], T.X[:, 0:4096].indirect(T.LH[:, 64:96]), r="XA XB LH0", w="GLd R0d")
+        for c, k_ in ((0, "c"), (512, "a"), (1536, "b")):
+            act(T.GL[:, c:c + 512], T.X[:, 0:4096].indirect(T.LH[:, c // 16:c // 16 + 32]), r="XA XB LH0", w="GL%s R0%s" % (k_, k_))
+        for b_ in range(2):
+            if b_ == 1:
+                mid()
+            c, k_ = 512 * b_, "a" if b_ else "c"
+            mm(T.PG[:, c:c + 512], T.IDB[:], T.GL[:, c:c + 512], r="IDB GL%s R0%s" % (k_, k_), w="pg", b="PG%d" % b_)
+            c, k_ = 1024 + 512 * b_, "b" if b_ else "d"
+            for j in range(1, 6):
+                mm(T.PG[:, c + j:c + 512:8], T.IDB[:], T.GL[:, c + j:c + 512:8], r="IDB GL%s" % k_, w="pg", b="PG%d" % (2 + b_))
+        act(T.GH[:, 0:1024], T.X[:, 0:4096].indirect(T.LH[:, 128:192]), r="XA XB LH1", w="GHa")
+        act(T.GH[:, 1024:2048], T.X[:, 0:4096].indirect(T.LH[:, 192:256]), r="XA XB LH1", w="GHb")
+        hole()
+
+        def low(hf, j):
+            gl = T.GL[:, 1024 * hf + j:1024 * hf + 1024:8]
+            key = ("R0" if j == 0 else "GL") + "ab"[hf]
+            if j < 4:
+                k_ = 4 if hf == 1 and j == 0 else j
+                mm(pd(hf, 0, 160), gl, T.CP[:, 160 * k_:160 * k_ + 160], False, False, r=key + " " + cpk[k_], w="pd%d" % hf, b="PD%d" % hf)
+                return
+            for h in HS:
+                if h > j and not (h == 8 and hf == 1):
+                    mm(place(hf, h, j), gl, T.KN[:], False, False, r=key + " KN", w="pd%d" % hf, b="PD%d" % hf)
+
+        def high(hf, rr):
+            for h in HS:
+                j = rr - h
+                if 0 <= j < h and not (h == 8 and hf == 1 and j not in MAXED):
+                    src, key = (T.GL, "GL") if rr < 8 else (T.GH, "GH")
+                    o = 1024 * hf + rr % 8
+                    mm(place(hf, h, j), src[:, o:1024 * hf + 1024:8], T.KN[:], False, False, r=key + "ab"[hf] + " KN", w="pd%d" % hf, b="PD%d" % hf)
+
+        def add(hf, h, j, last=False):
+            o = place(hf, h, j)
+            if h == 8:
+                if hf == 0:
+                    mm(o, T.D8[:, j:1024:8], T.K2[:], False, last, r="K2 D8a D8b" + (" D8j" if j == 0 else ""), w="pd0", b="PD0")
+                else:
+                    mm(o, T.D8[:, 1024 + 128 * j:1152 + 128 * j], T.K2[:] if j in MAXED else T.KB[:], False, last,
+                       r="K2 D8y%d" % j if j in MAXED else "KB D8x%d" % min(j, 4), w="pd1", b="PD1")
+            else:
+                c = 256 * idx(h, j) + 128 * hf
+                mm(o, T.DL[:, c:c + 128], T.K2[:], False, last, r="K2 DL%d%d" % (h, j), w="pd%d" % hf, b="PD%d" % hf)
+
+        def pair(h, j):
+            c = 256 * idx(h, j)
+            if j == 0:
+                i0, i1, key = T.PG[:, h:2048:8], T.GL[:, 0:2048:8], "R0a R0b"
+            elif j + h < 8:
+                i0, i1, key = T.PG[:, j:2048:8], T.GL[:, j + h:2048:8], "GLa GLb"
+            else:
+                i0, i1, key = T.PG[:, j:2048:8], T.GH[:, j + h - 8:2048:8], "GHa GHb"
+            v(V.tensor_tensor, T.DL[:, c:c + 256], i0, i1, A.max, r="pg " + key, w="DL%d%d" % (h, j), b=PGK)
+
+        def sizes(js, B, bk):
+            n = 128 * len(js)
+            for q_, j in enumerate(js):
+                mm(B[:, 128 * q_:128 * q_ + 128], T.IDB[:], T.GL[:, 1024 + j:2048:8], True, False, r="IDB %sb" % ("R0" if j == 0 else "GL"), b=bk)
+                mm(B[:, 128 * q_:128 * q_ + 128], T.NIB[:], T.GH[:, 1024 + j:2048:8], False, True, r="NIB GHb", w="pB" + bk, b=bk)
+            act(T.D8[:, 1024 + 128 * js[0]:1024 + 128 * js[0] + n], B[:, 0:n], F.Abs, r="pB" + bk, w="D8x%d" % js[0], b=bk)
+
+        def row0():
+            act(T.GL[:, 0:2048:8], T.X[:, 0:4096].indirect(T.LLU[:]), r="XA XB LLU GLa GLb", w="R0a R0b R0c R0d")
+
+        early = ((2, 1), (3, 1), (3, 2), (5, 1), (5, 2))
+        for h, j in early:
+            pair(h, j)
+        v(V.tensor_tensor, T.D8[:, 0:512], T.PG[:, 0:512], T.GH[:, 0:512], A.max, r="pg GHa", w="D8a", b="PG0")
+        if t > 0:
+            v(V.tensor_copy, T.LLU[:], T.MNR[:, 32 * (t - 1) + 16:32 * t], r="MNR%d" % (t - 1), w="LLU")
+            v(V.tensor_scalar, T.S5[:], T.MNR[:, 32 * (t - 1):32 * (t - 1) + 16], 5, None, A.mult, r="MNR%d" % (t - 1), w="S5")
+            row0()
+        else:
+            push2b("LS")
+        for hf in range(2):
+            if hf == 1:
+                if t == 0:
+                    push2w(0)
+                    push3(0)
+                    push4()
+                v(V.tensor_tensor, T.D8[:, 512:1024], T.PG[:, 512:1024], T.GH[:, 512:1024], A.max, r="pg GHa", w="D8b", b="PG1")
+            mm(pd(hf, 0, 160), T.ONE[:], T.RB[:], True, False, r="ONE RB", w="pd%d" % hf, b="PD%d" % hf)
+            for rr in range(1, 8):
+                low(hf, rr)
+                if rr > 3:
+                    high(hf, rr)
+        if t == 0:
+            v(V.tensor_copy, T.LLU[:], T.B5[:, 0:16], r="pL", w="LLU", b="B5")
+            row0()
+        sizes((4, 5, 6, 7), T.B4, "B4")
+        sizes((0,), T.B5, "B5")
+        for j in MAXED:
+            v(V.tensor_tensor, T.D8[:, 1024 + 128 * j:1152 + 128 * j], T.PG[:, 1024 + j:2048:8], T.GH[:, 1024 + j:2048:8], A.max, r="pg GHb", w="D8y%d" % j, b="PG2 PG3")
+        for rr in range(8, 16):
+            high(0, rr)
+        for h, j in early:
+            for hf in range(2):
+                add(hf, h, j)
+        for j in range(1, 8):
+            add(0, 8, j)
+        for rr in (8, 9) + tuple(8 + j for j in MAXED if j > 1):
+            high(1, rr)
+        for h, j in ((5, 3), (5, 4)):
+            pair(h, j)
+            for hf in range(2):
+                add(hf, h, j)
+        for hf in range(2):
+            low(hf, 0)
+        v(V.tensor_tensor, T.D8[:, 0:1024:8], T.GL[:, 0:1024:8], T.GH[:, 0:1024:8], A.max, r="R0a GHa D8a D8b", w="D8j")
+        add(0, 8, 0)
+        for j in range(1, 8):
+            add(1, 8, j)
+        add(1, 8, 0)
+        for h in (5, 3, 2, 1):
+            pair(h, 0)
+            for hf in range(2):
+                add(hf, h, 0, h == 1)
+        if t == 0:
+            push2f()
+            push3f(0)
+            send("LF0", nxt, T.LFR[:, 0:256], T.LF[:, 0:256], r="LF0")
+        v(V.tensor_tensor_scan, T.ZC[:], T.ZR[:], T.GL[:], 0.0, A.mult, A.max, r="ZR GLa GLb R0a R0b", w="ZC")
+        act(T.ZC[:, 5:2048:8], T.GL[:, 0:2048:8], r="R0a R0b ZC", w="ZC5")
+
+    def decode(t):
+        last = t == TV - 1
+        rs = 16 if last else 0
+        m1 = 288 * t
+        halves = ((0, T.B4, "B4", 0), (1, T.B5, "B5", 160))
+        for hf, B, bk, c in halves:
+            v(V.tensor_tensor_scan, B[:, 0:160], T.D0[:], pd(hf, 0, 160), 0.0, A.mult, A.max, r="pd%d %s" % (hf, d0k), w="s1%d" % hf, b="PD%d %s" % (hf, bk))
+        for hf, B, bk, c in halves:
+            v(V.tensor_tensor, T.E[:, c:c + 160], B[:, 0:160], T.THR[:, c:c + 160], A.is_gt, r="s1%d %s" % (hf, thk), w="E%d" % hf, b=bk)
+        for hf, B, bk, c in halves:
+            v(V.tensor_tensor_scan, T.SC2[:, c:c + 160], T.E[:, c:c + 160], T.C2[:], 0.0, A.mult, A.add, r="E%d %s" % (hf, c2k), w="SC%d" % hf)
+        v(V.tensor_tensor, T.EK[:], T.SC2[:].indirect(T.LK9[:]), T.ME[:], A.mult, r="SC0 SC1 LK9 ME", w="EK")
+        mm(T.PG[:, 0:16], T.IDB[:], T.B8[:], True, False, r="IDB B8", w="p1", b="PG0")
+        for hf in range(2):
+            mm(T.PG[:, 8 * hf:8 * hf + 8], T.EK[:, 144 * hf + 16:144 * hf + 144], T.KB[:], False, hf == 1, r="EK KB", w="p1", b="PG0")
+        for hf in range(2):
+            mm(T.PG[:, 512 + 8 * hf:520 + 8 * hf], T.EK[:, 144 * hf + rs:144 * hf + rs + 128], T.K256[:], r="EK K256", w="p2", b="PG1")
+        kap = T.SC2[:, 19:320:20]
+        v(V.tensor_scalar, T.NH[:], kap, 5, None, A.is_equal, r="SC0 SC1", w="NH")
+        v(V.tensor_scalar, T.DU[:], T.NH[:], 4096, None, A.mult, r="NH", w="DU")
+        v(V.tensor_scalar, T.H1[:], T.NH[:], -6, 1, A.mult, A.add, r="NH", w="H1")
+        v(V.tensor_tensor, T.S5[:], T.S5[:], T.NH[:], A.mult, r="S5 NH", w="S5")
+        v(V.tensor_copy, T.L1[:], T.PG[:, 0:16], r="p1", w="L1", b="PG0")
+        v(V.tensor_tensor, T.H[:], T.H1[:], kap, A.add, r="H1 SC0 SC1", w="H")
+        v(V.tensor_copy, T.M1S[:, m1:m1 + 128], T.ZC[:].indirect(T.L1[:, 0:8]), r="ZC ZC5 L1", w="Za")
+        act(T.M1S[:, m1 + 128:m1 + 256], T.ZC[:].indirect(T.L1[:, 8:16]), r="ZC ZC5 L1", w="Zb")
+        act(T.M1S[:, m1 + 256:m1 + 272], T.PG[:, 512:528], r="p2", w="Zc", b="PG1")
+        for hf in range(2):
+            mm(T.PG[:, 1024 + 8 * hf:1032 + 8 * hf], T.M1S[:, m1 + 128 * hf:m1 + 128 * hf + 128], T.WTB[:], r="Z%s WTB" % "ab"[hf], w="pt", b="PG2")
+        mm(T.PG[:, 1536:1552], T.IDB[:], T.B16[:], True, False, r="IDB B16", w="p3", b="PG3")
+        v(V.tensor_tensor, T.AD[:], T.S5[:], T.H[:], A.add, r="S5 H", w="AD")
+        v(V.tensor_tensor, T.NP[:], T.N1[:], T.H[:], A.subtract, r="N1 H", w="NP")
+        v(V.tensor_tensor, T.SUM[:], T.PG[:, 1024:1040], T.AD[:], A.add, r="pt AD", w="SUM", b="PG2")
+        if last:
+            v(V.tensor_copy, T.M1S[:, m1 + 272:m1 + 288], T.NP[:], r="NP", w="Zd")
+        else:
+            v(V.tensor_copy, T.M1S[:, m1 + 272:m1 + 288], T.NP[:].indirect(T.ROT[:, 0:1]), r="NP ROT", w="Zd")
+        v(V.tensor_scalar, T.V15[:], T.SUM[:], 15, None, A.bitwise_and, r="SUM", w="V15")
+        v(V.tensor_tensor, T.VV[:], T.V15[:], T.DU[:], A.max, r="V15 DU", w="VV")
+        v(V.tensor_tensor, T.EV[:], T.VV[:].indirect(T.LU[:]), T.ME[:, 0:256], A.mult, r="VV LU ME", w="EV")
+        for hf in range(2):
+            mm(T.PG[:, 1536 + 8 * hf:1544 + 8 * hf], T.EV[:, 128 * hf:128 * hf + 128], T.KB[:], False, hf == 1, r="EV KB", w="p3", b="PG3")
+        v(V.tensor_scalar, T.SI[:], T.SUM[:], 4095, None, A.bitwise_and, r="SUM", w="SI")
+        if not last:
+            v(V.tensor_scalar, T.U[:], T.NP[:], 77, None, A.mult, r="NP", w="U")
+            v(V.tensor_tensor, T.T1[:], T.SI[:], T.SI[:], A.mult, r="SI", w="T1")
+        v(V.tensor_copy, T.MLS[:, 16 * t:16 * t + 16], T.PG[:, 1536:1552], r="p3", w="MLS", b="PG3")
+        send("M1%d" % t, nxt, T.M1R[:, m1:m1 + 288], T.M1S[:, m1:m1 + 288], r="Za Zb Zc Zd")
+        send("ML%d" % t, nxt, T.MLR[:, 16 * t:16 * t + 16], T.MLS[:, 16 * t:16 * t + 16], r="MLS")
+
+    def xupdate(t, cols, lo, e0, e1, ck, xk):
+        win = T.X[:, lo:8192]
+        v(V.tensor_tensor, T.XT[:, e0:e1], win.indirect(cols), T.M1R[:, 288 * t + e0:288 * t + e1], A.add, r="M1R%d %s %s" % (t, ck, xk), w="XT")
+        v(V.tensor_scalar, T.XU[:, e0:e1], T.XT[:, e0:e1], 0.5, 127.75, A.mult, A.add, r="XT", w="XU")
+        v(V.tensor_tensor, win.indirect(cols), T.XU[:, e0:e1], T.NEG[:, e0:e1], A.add, r="XU NEG " + ck, w=xk)
+
+    def first():
+        bound()
+        v(V.memset, T.ONE[:], 1.0, w="ONE")
+        v(V.memset, T.THR[:], -1.0, w="THR")
+        v(V.memset, T.THR[:, 0:320:20], 1000.0, r="THR", w="THR0")
+        n1(T.N0[:], "N0")
+        thr()
+        v(V.memset, T.ZR[:, 0:2048:8], 0.0, r="ZR", w="ZR")
+        v(V.tensor_copy, T.WTF[:], T.WTI[:], r="WTI", w="WTF")
+        v(V.tensor_scalar, T.BI[:], T.IK[:], T.P15[:], None, A.add, r="IK P15", w="BI")
+        act(T.WTB[:], T.KB[:], scale=T.WTF[:], r="KB WTF", w="WTB")
+        act(T.K256[:], T.KB[:], scale=256.0, r="KB", w="K256")
+        act(T.B8[:], T.BI[:], scale=8.0, r="BI", w="B8")
+        act(T.B16[:], T.BI[:], scale=16.0, r="BI", w="B16")
+        v(V.tensor_scalar, T.S5[:], T.SI[:], 5, None, A.mult, r="SI", w="S5")
+
+    def rot_list():
+        v(V.tensor_scalar, T.P15I[:, 2:3], T.P15I[:, 0:1], 8, None, A.bitwise_and, r="P15I", w="P15c")
+        v(V.tensor_scalar, T.P15I[:, 3:4], T.P15I[:, 0:1], -1, None, A.add, r="P15I", w="P15d")
+        v(V.tensor_scalar, T.P15I[:, 3:4], T.P15I[:, 3:4], 7, None, A.bitwise_and, r="P15d", w="P15d")
+        v(V.tensor_tensor, T.P15I[:, 2:3], T.P15I[:, 2:3], T.P15I[:, 3:4], A.add, r="P15c P15d", w="P15c")
+        v(V.tensor_copy, T.ROT[:, 0:1], T.P15I[:, 2:3], r="P15c", w="ROT")
+
+    for t in range(TV):
+        if t < TV - 1:
+            send("W2%d" % t, nxt, T.W2R[:, 256 * t:256 * t + 256], T.W2[:, 256 * t:256 * t + 256], r="W2%d" % t)
+            build_sh(t)
+        else:
+            for h in (8, 5, 3, 2, 1, 0):
+                c = 256 * SLOT[h]
+                dma("sh", T.SH[0:128 - h, c:c + 256], T.W2[h:128, 1024:1280], r="W24", w="SA%d SB%d" % (h, h))
+            dma("sh2", T.SH[0:128:16, 1280:1536], T.LFR[0:128:16, 1024:1280], r="LFR4 SA0 SB0", w="SHf SHg")
+        bulk(t, *((first0, first) if t == 0 else (mid, hole)))
+        if t == 0:
+            consts_scan()
+            rot_list()
+        decode(t)
+        if t == TV - 1:
+            break
+        u = t + 1
+        m1 = 288 * t
+        push1(T.NP[:], "NP", lambda: v(V.tensor_reduce, T.NS[:], T.NH[:], AxisListType.X, A.add, r="NH", w="NS"))
+        v(V.tensor_copy, T.MNS[:, 32 * t:32 * t + 16], T.SI[:].indirect(T.ROT[:, 0:1]), r="SI ROT", w="MNa")
+        v(V.tensor_tensor, T.KBI[:], T.M1R[:, m1 + 256:m1 + 272], T.BI[:], A.add, r="M1R%d BI" % t, w="KBI")
+        v(V.tensor_copy, T.L2[:], T.KBI[:], r="KBI", w="L2")
+        act(T.W2[:, 256 * u:256 * u + 256], T.SH[:].indirect(T.L2[:]), r="L2 " + shk, w="W2%d" % u)
+        mm(T.PG[:, 256:257], T.ONEF[:], T.NS[:], r="ONEF NS", w="pA", b="PG0")
+        push2(0)
+        rearr(u, 0)
+        push2a()
+        push2b("LSN")
+        push2w()
+        rearr(u, 1)
+        push2f()
+        v(V.tensor_scalar, T.AI[:], T.PG[:, 256:257], -1, 2048, A.mult, A.add, r="pA", w="AI", b="PG0")
+        xupdate(t, T.MLR[:, 16 * t:16 * t + 16], 0, 0, 256, "MLR%d" % t, "XA XB XD")
+        lists(0)
+
+        push3()
+
+        def mid(m1=m1):
+            lists(1)
+            push4()
+            v(V.tensor_scalar, T.AJ[:], T.AI[:], 15, None, A.bitwise_and, r="AI", w="AJ")
+            n1(T.M1R[:, m1 + 272:m1 + 288], "M1R%d" % (m1 // 288))
+
+        def hole(t=t, u=u):
+            v(V.tensor_copy, T.MNS[:, 32 * t + 16:32 * t + 32], T.B5[:, 0:16], r="pL", w="MNb", b="B5")
+            send("MN%d" % t, nxt, T.MNR[:, 32 * t:32 * t + 32], T.MNS[:, 32 * t:32 * t + 32], r="MNa MNb")
+            push3f(u)
+            send("LF%d" % u, nx2 if u < 4 else nxt, T.LFR[:, 256 * u:256 * u + 256], T.LF[:, 256 * u:256 * u + 256], r="LF%d" % u)
+            v(V.tensor_scalar, T.BC[:], T.AJ[:], T.THF[:], -1, A.add, A.mult, r="AJ THF", w="BC")
+            thr()
+            bound()
+
+    v(V.tensor_copy, T.SF[:], T.SI[:], r="SI", w="SF")
+    v(V.tensor_tensor, T.KBI[:], T.M1S[:, 4 * 288 + 256:4 * 288 + 272], T.BI[:], A.add, r="Zc BI", w="KBI")
+    v(V.tensor_copy, T.L2[:], T.KBI[:], r="KBI", w="L2")
+    v(V.tensor_copy, T.RS[:], T.NP[:].indirect(T.LS9[:]), r="NP LS9", w="RS")
+    for hf in range(2):
+        mm(T.PG[:, 512 + 128 * hf:640 + 128 * hf], T.RS[:, 144 * hf + 16:144 * hf + 144], T.IDB[:], r="RS IDB", w="pR", b="PG1")
+    for hf in range(2):
+        mm(T.PG[0:8, 128 * hf:128 * hf + 128], T.NP[:, 8 * hf:8 * hf + 8], T.IDF[:], r="NP IDF", w="pN", b="PG0")
+    for hf in range(2):
+        mm(T.PG[0:8, 1024 + 128 * hf:1152 + 128 * hf], T.SF[:, 8 * hf:8 * hf + 8], T.IDF[:], r="SF IDF", w="pS", b="PG2")
+    v(V.tensor_scalar, T.MK[:], T.PG[:, 512:768], T.P15[:], None, A.is_gt, r="pR P15", w="MK", b="PG1")
+    v(V.tensor_tensor, T.YW[:], T.SH[:].indirect(T.L2[:]), T.MK[:], A.mult, r="L2 MK " + shk, w="YW")
+    dma("oyw", T.yw[:], T.YW[:], r="YW")
+    xupdate(4, T.MLR[:, 64:72], 0, 0, 128, "MLR4", "XA XB XD")
+    dma("oyx", T.yx[:, 0:2048], T.X[:, 0:2048], r="XA")
+    v(V.tensor_scalar, T.CL[:, 0:8], T.MLR[:, 72:80], -2048, None, A.add, r="MLR4", w="CL")
+    xupdate(4, T.CL[:, 0:8], 2048, 128, 256, "CL", "XB XD")
+    dma("oyx", T.yx[:, 2048:4096], T.X[:, 2048:4096], r="XB")
+    act(T.YN[:], T.PG[0:8, 0:256], r="pN", w="YN", b="PG0")
+    act(T.YS[:], T.PG[0:8, 1024:1280], r="pS", w="YS", b="PG2")
+    dma("oyn", T.yn[:], T.YN[:], r="YN")
+    dma("oyn", T.ys[:], T.YS[:], r="YS")
+    for sem, n in tot.items():
+        if known["g"].get(sem, 0) < n:
+            g.wait_ge(T.sem[sem], n)

@@ -2,54 +2,42 @@ from concourse.mybir import AluOpType as A, AxisListType, ActivationFunctionType
 
 HS = (8, 5, 3, 2, 1)
 BASE = {8: 1, 5: 9, 3: 14, 2: 17, 1: 19}
-SLOT = {1: 0, 2: 1, 3: 2, 5: 4, 8: 7, 0: 5}
+NPL, HALF = 21, 168
 TV = 5
-MAXED = (1, 2, 3)
-PAIRS = [(h, j) for h in (5, 3, 2, 1) for j in range(h)]
+EMPTY = 4097
+ZW, WW = 272, 296
+MAXED = [(8, 0), (8, 1)] + [(h, j) for h in (5, 3, 2, 1) for j in range(h)]
+NQ = 2
 
-SCRATCH = {
-    "X": ("sbuf", [128, 8192], "bfloat16"), "LS": ("sbuf", [128, 1024], "int32"), "LSN": ("sbuf", [128, 1024], "int32"),
-    "SH": ("sbuf", [128, 2048], "float32"), "GL": ("sbuf", [128, 2048], "bfloat16"), "GH": ("sbuf", [128, 2048], "bfloat16"),
-    "D8": ("sbuf", [128, 2048], "bfloat16"), "DL": ("sbuf", [128, 11 * 256], "bfloat16"), "ZC": ("sbuf", [128, 2048], "bfloat16"),
-    "ZR": ("sbuf", [128, 2048], "bfloat16"), "NEG": ("sbuf", [128, 256], "bfloat16"),
-    "M1S": ("sbuf", [128, 5 * 288], "bfloat16"), "M1R": ("sbuf", [128, 5 * 288], "bfloat16"),
-    "MLS": ("sbuf", [128, 5 * 16], "uint16"), "MLR": ("sbuf", [128, 5 * 16], "uint16"),
-    "MNS": ("sbuf", [128, 5 * 32], "float32"), "MNR": ("sbuf", [128, 5 * 32], "float32"),
-    "W2": ("sbuf", [128, 5 * 256], "float32"), "W2R": ("sbuf", [128, 5 * 256], "float32"),
-    "LF": ("sbuf", [128, 5 * 256], "float32"), "LFR": ("sbuf", [128, 5 * 256], "float32"),
-    "IDB": ("sbuf", [128, 128], "bfloat16"), "NIB": ("sbuf", [128, 128], "bfloat16"), "IDF": ("sbuf", [128, 128], "float32"),
-    "ONE": ("sbuf", [128, 128], "bfloat16"), "ONEF": ("sbuf", [128, 128], "float32"), "ROW0": ("sbuf", [128, 128], "float32"),
-    "RA": ("sbuf", [128, 512], "float32"), "ME": ("sbuf", [128, 288], "float32"),
-    "KB": ("sbuf", [128, 8], "bfloat16"), "KF": ("sbuf", [128, 8], "float32"), "K256": ("sbuf", [128, 8], "bfloat16"),
-    "K2": ("sbuf", [128, 8], "bfloat16"), "KN": ("sbuf", [128, 8], "bfloat16"), "WTB": ("sbuf", [128, 8], "bfloat16"),
-    "CP": ("sbuf", [128, 1280], "bfloat16"), "DB": ("sbuf", [128, 160], "bfloat16"), "RB": ("sbuf", [128, 160], "bfloat16"),
-    "D0": ("sbuf", [128, 160], "bfloat16"), "C2": ("sbuf", [128, 160], "bfloat16"), "THR": ("sbuf", [128, 320], "float32"),
-    "E": ("sbuf", [128, 320], "bfloat16"), "SC2": ("sbuf", [128, 320], "bfloat16"),
-    "EK": ("sbuf", [128, 288], "bfloat16"), "EC": ("sbuf", [128, 288], "float32"), "RS": ("sbuf", [128, 288], "bfloat16"),
-    "EV": ("sbuf", [128, 256], "bfloat16"), "EL": ("sbuf", [128, 256], "float32"),
-    "LS9": ("sbuf", [128, 18], "uint16"), "LK9": ("sbuf", [128, 18], "uint16"), "LU": ("sbuf", [128, 16], "uint16"), "ROT": ("sbuf", [128, 2], "uint16"),
-    "BI": ("sbuf", [128, 16], "float32"), "B8": ("sbuf", [128, 16], "bfloat16"), "B16": ("sbuf", [128, 16], "bfloat16"),
-    "II": ("sbuf", [128, 128], "int32"), "IM": ("sbuf", [128, 288], "int32"), "IG": ("sbuf", [128, 8], "int32"), "I20": ("sbuf", [128, 160], "int32"),
-    "IP": ("sbuf", [128, 4], "int32"), "IK": ("sbuf", [128, 16], "int32"), "I9": ("sbuf", [128, 18], "int32"), "IU": ("sbuf", [128, 16], "int32"),
-    "P15": ("sbuf", [128, 1], "float32"), "PB": ("sbuf", [128, 2], "float32"), "P15I": ("sbuf", [128, 4], "int32"),
-    "SDI": ("sbuf", [8, 256], "int32"), "NLI": ("sbuf", [8, 256], "int32"), "SDF": ("sbuf", [8, 256], "float32"), "NLF": ("sbuf", [8, 256], "float32"),
-    "WTI": ("sbuf", [128, 1], "int32"), "WTF": ("sbuf", [128, 1], "float32"), "THI": ("sbuf", [128, 1], "int32"), "THF": ("sbuf", [128, 1], "float32"),
-    "WI": ("sbuf", [128, 256], "int32"), "LH": ("sbuf", [128, 256], "uint16"), "L1": ("sbuf", [128, 16], "uint16"), "L2": ("sbuf", [128, 16], "uint16"),
-    "LLU": ("sbuf", [128, 16], "uint16"), "CL": ("sbuf", [128, 16], "uint16"), "KBI": ("sbuf", [128, 16], "int32"),
-    "N0": ("sbuf", [128, 16], "float32"), "N1": ("sbuf", [128, 16], "float32"), "NP": ("sbuf", [128, 16], "float32"),
-    "NH": ("sbuf", [128, 16], "float32"), "H": ("sbuf", [128, 16], "float32"), "H1": ("sbuf", [128, 16], "float32"),
-    "S5": ("sbuf", [128, 16], "float32"), "AD": ("sbuf", [128, 16], "float32"), "DU": ("sbuf", [128, 16], "int32"),
-    "SUM": ("sbuf", [128, 16], "int32"), "V15": ("sbuf", [128, 16], "int32"), "VV": ("sbuf", [128, 16], "int32"), "SI": ("sbuf", [128, 16], "int32"),
-    "S15": ("sbuf", [128, 16], "int32"), "T1": ("sbuf", [128, 16], "int32"), "T2": ("sbuf", [128, 16], "int32"), "U": ("sbuf", [128, 16], "int32"), "CI": ("sbuf", [128, 16], "int32"),
-    "MK": ("sbuf", [128, 256], "float32"), "MM": ("sbuf", [128, 256], "float32"), "LW": ("sbuf", [128, 16], "float32"),
-    "XT": ("sbuf", [128, 256], "bfloat16"), "XU": ("sbuf", [128, 256], "bfloat16"),
-    "NS": ("sbuf", [128, 1], "float32"), "AI": ("sbuf", [128, 1], "int32"), "BC": ("sbuf", [128, 1], "float32"), "AJ": ("sbuf", [128, 1], "int32"),
-    "YW": ("sbuf", [128, 256], "float32"), "YN": ("sbuf", [8, 256], "float32"), "YS": ("sbuf", [8, 256], "float32"), "SF": ("sbuf", [128, 16], "float32"),
-    "PG": ("psum", [128, 2048], "float32"), "B4": ("psum", [128, 512], "float32"), "B5": ("psum", [128, 512], "float32"),
-    "PD0": ("psum", [128, 512], "float32"), "PD1": ("psum", [128, 512], "float32"),
-}
-_ARR = ["%s%d" % (n, t) for n in ("M1", "ML", "MN", "W2", "LF") for t in range(TV)] + ["LS"]
-_DMA = ["small", "sm2", "ls", "wd", "x", "sh", "sh2", "oyx", "oyw", "oyn"]
+bf, f32, i32, u16 = "bfloat16", "float32", "int32", "uint16"
+SCRATCH = {n: ("sbuf", [p, c], d) for n, p, c, d in [
+    ("X", 128, 8192, bf), ("LS", 128, 1024, i32), ("LSN", 128, 1024, i32), ("SH", 128, 2304, f32),
+    ("GL", 128, 2048, bf), ("GH", 128, 2048, bf), ("ZC", 128, 2064, bf), ("ZR", 128, 1024, bf),
+    ("DL", 128, 13 * 256, bf), ("DA", 128, 1536, bf), ("NEG", 128, 256, bf),
+    ("ZS", 128, 5 * ZW, bf), ("ZM", 128, 5 * ZW, bf), ("HS", 128, 5 * 128, u16), ("HM", 128, 5 * 128, u16),
+    ("LLS", 128, 5 * 128, u16), ("LLM", 128, 5 * 128, u16), ("WS", 128, 5 * WW, f32), ("WM", 128, 5 * WW, f32),
+    ("WI", 128, 256, i32), ("WN", 128, 256, f32), ("MM", 128, 256, f32), ("MK", 128, 256, bf), ("MS", 128, 256, bf),
+    ("IDB", 128, 128, bf), ("NIB", 128, 128, bf), ("IZ", 128, 128, f32), ("RA", 128, 512, f32), ("RB", 128, 512, bf),
+    ("EXT", 128, 136, f32), ("ONE", 128, 128, bf), ("THL", 128, 128, bf), ("LQ", 128, 128, bf), ("ZER", 32, 128, bf),
+    ("CQ", 128, 368, bf), ("DB", 128, 336, bf), ("D0", 128, 336, bf), ("M1", 128, 336, bf), ("CP", 128, 176, bf),
+    ("S1", 128, 336, bf), ("U", 128, 344, f32), ("E", 128, 144, f32), ("ES", 128, 256, f32), ("RR", 128, 48, f32),
+    ("ZROW", 128, 32, bf), ("MT", 128, 32, bf), ("M01", 128, 32, bf),
+    ("KF", 128, 16, f32), ("KB", 128, 8, bf), ("KN", 128, 8, bf), ("K2", 128, 8, bf), ("WP", 128, 8, bf), ("WQ", 128, 8, bf),
+    ("II", 128, 128, i32), ("IG", 128, 16, i32), ("IP", 128, 4, i32), ("IQ", 128, 4, i32), ("IU", 128, 32, i32), ("I9", 128, 10, i32),
+    ("IS", 128, 16, i32), ("IT", 128, 16, i32), ("IA", 128, 16, i32), ("IL", 128, 16, i32), ("COL", 128, 16, f32),
+    ("POS", 128, 16, i32), ("POSU", 128, 16, u16), ("BA", 128, 16, f32), ("BS", 128, 16, i32), ("BL", 128, 16, f32),
+    ("CV", 128, 10, u16), ("SV", 128, 32, u16),
+    ("SI", 128, 16, i32), ("NP", 128, 16, i32), ("THI", 128, 1, i32), ("WTI", 128, 1, i32), ("WTF", 128, 1, f32),
+    ("ZO", 128, 16, u16), ("UI", 128, 16, i32), ("FI", 128, 16, i32), ("UR", 128, 16, i32), ("H", 128, 16, i32), ("HB", 128, 16, i32),
+    ("PL", 128, 16, i32), ("PU", 128, 16, u16), ("NU", 128, 16, u16), ("NH", 128, 16, bf), ("A5", 128, 16, f32), ("SUM", 128, 16, i32),
+    ("S15", 128, 16, i32), ("SU", 128, 16, u16), ("T1", 128, 16, i32), ("T2", 128, 16, i32), ("U7", 128, 16, i32), ("CU", 128, 16, u16),
+    ("CI", 128, 16, i32), ("CX", 128, 16, u16), ("NS", 128, 1, f32), ("NJ", 128, 16, f32), ("AI", 128, 1, i32), ("AJ", 128, 1, i32), ("BC", 128, 1, f32),
+    ("XT", 128, 256, bf), ("XU", 128, 256, bf), ("YW", 128, 256, f32), ("FO", 128, 40, f32), ("YO", 128, 32, f32),
+]}
+for _b in range(8):
+    SCRATCH["B%d" % _b] = ("psum", [128, 512], f32)
+_ARR = ["%s%d" % (n, t) for n in ("Z", "H", "L", "W") for t in range(TV)] + ["LS"]
+_DMA = ["small", "sm2", "ls", "wd", "x", "sh", "oyx", "oyw", "oyn"]
 SEMAPHORES = ["qv", "qa", "qp", "qg", "loc"] + ["r" + n for n in _ARR] + ["d" + n for n in _DMA]
 
 
@@ -58,9 +46,11 @@ def rank_program(g, core, T, topo):
     if rank is None:
         return
     N = len(T.cores)
-    nxt, nx2, prv = T.cores[(rank + 1) % N], T.cores[(rank + 2) % N], T.cores[(rank - 1) % N]
+    nxt, prv = T.cores[(rank + 1) % N], T.cores[(rank - 1) % N]
     V, P, S = g.vector, g.tensor, g.scalar
     Q = {"v": V, "a": S, "p": P, "g": g, "s": g.sync}
+    B = [T["B%d" % b] for b in range(8)]
+    PD, PC = B[6], B[7]
 
     tot = {}
     known = {q: {} for q in Q}
@@ -68,10 +58,10 @@ def rank_program(g, core, T, topo):
 
     def need(q, deps):
         for o in sorted(deps, reverse=True):
-            sem, val, snap, dma = ops[o]
+            sem, val, snap, dma_ = ops[o]
             if known[q].get(sem, 0) >= val:
                 continue
-            if dma:
+            if dma_:
                 val = tot[sem]
             Q[q].wait_ge(T.sem[sem], val)
             for s_, v_ in snap.items():
@@ -89,10 +79,10 @@ def rank_program(g, core, T, topo):
             d.update(o for q_, o in banks.get(k, {}).items() if q_ != q)
         return d
 
-    def note(q, sem, inc, r, w, b, dma=False):
+    def note(q, sem, inc, r, w, b, dma_=False):
         tot[sem] = tot.get(sem, 0) + inc
         o = len(ops)
-        ops.append((sem, tot[sem], dict(known[q]) if q else {}, dma))
+        ops.append((sem, tot[sem], dict(known[q]) if q else {}, dma_))
         for k in w:
             lastw[k] = [o]
             readers[k] = []
@@ -112,24 +102,35 @@ def rank_program(g, core, T, topo):
     def v(fn, *a, **k):
         run("v", fn, *a, **k)
 
+    def ts(out, in_, s1, op0, s2=None, op1=None, **k):
+        if op1 is None:
+            run("v", V.tensor_scalar, out, in_, s1, None, op0, **k)
+        else:
+            run("v", V.tensor_scalar, out, in_, s1, s2, op0, op1, **k)
+
+    def tt(out, a, b_, op, **k):
+        run("v", V.tensor_tensor, out, a, b_, op, **k)
+
+    def cp(out, in_, **k):
+        run("v", V.tensor_copy, out, in_, **k)
+
     def act(out, in_, func=F.Copy, r="", w="", b="", **k):
         run("a", S.activation, out, in_, func, r=r, w=w, b=b, **k)
 
-    def mm(out, l, rh, start=True, stop=True, r="", w="", b=""):
-        r, w, b = r.split(), w.split(), b.split()
+    def mm(out, l, rh, start, stop, r, b):
+        r, b = r.split(), b.split()
         need("p", deps_of("p", r, [], b))
         P.matmul(out, l, rh, start, stop).then_inc(T.sem.qp, 1)
-        note("p", "qp", 1, r, w, b)
+        note("p", "qp", 1, r, [], b)
 
-    def dma(sem, out, in_, r="", w=""):
+    def dma(sem, out, in_, r="", w="", q="s"):
         r, w = r.split(), w.split()
-        need("s", deps_of("s", r, w, []))
-        g.sync.dma_start(out, in_).then_inc(T.sem["d" + sem], 16)
-        note("s", "d" + sem, 16, r, w, [], True)
+        need(q, deps_of(q, r, w, []))
+        Q[q].dma_start(out, in_).then_inc(T.sem["d" + sem], 16)
+        note(q, "d" + sem, 16, r, w, [], True)
 
     def send(name, dst, out, in_, r=""):
-        r = r.split()
-        need("g", deps_of("g", r, [], []))
+        need("g", deps_of("g", r.split(), [], []))
         rid, pid = topo.addr(dst)[:2]
         g.remote_dma(out, in_, T.sem["r" + name], T.sem.loc, pid, rid, topo.mask(core, dst))
         note("g", "loc", len(topo.engines(core, dst)), [], [], [])
@@ -140,489 +141,422 @@ def rank_program(g, core, T, topo):
         lastw[key] = [len(ops)]
         ops.append(("r" + name, n, {}, False))
 
-    p2 = T.cores[(rank - 2) % N]
     for t in range(TV):
-        arrive("M1%d" % t, prv, "M1R%d" % t)
-        arrive("ML%d" % t, prv, "MLR%d" % t)
-        if t < 4:
-            arrive("MN%d" % t, prv, "MNR%d" % t)
-            arrive("W2%d" % t, prv, "W2R%d" % t)
-        arrive("LF%d" % t, prv if t in (0, 4) else p2, "LFR%d" % t)
+        arrive("Z%d" % t, prv, "ZM%d" % t)
+        if t > 0:
+            for n_ in "HLW":
+                arrive("%s%d" % (n_, t), prv, "%sM%d" % (n_, t))
     arrive("LS", nxt, "LSN")
 
     v(V.memset, T.THI[:], 0, w="THI")
-    dma("small", T.SDI[:], T.sd[:], w="SDI")
-    dma("small", T.NLI[:], T.nl[:], w="NLI")
+    dma("small", T.SI[:], T.sd[:], w="SI")
+    dma("small", T.NP[:], T.nl[:], w="NP")
     dma("wd", T.WI[1:128, :], T.wd[0:127, :], w="WIa")
     dma("wd", T.WI[0:1, :], T.wd[0:1, :], w="WIb")
     dma("sm2", T.THI[0:128:16, :], T.th[:], w="THI")
     dma("sm2", T.WTI[:], T.wt[:], w="WTI")
-    dma("x", T.X[:, 0:4096], T.x[:], w="XA XB")
     dma("ls", T.LS[:], T.ls[:], w="LS")
+    dma("x", T.X[:, 0:4096], T.x[:], w="X0 X1 X2 X3")
+    XK = "X0 X1 X2 X3 XD XE"
 
-    def iota(out, pat, base, cm, key):
-        run("g", g.iota, out, pat, base, cm, w=key)
-    iota(T.II[:], [[-1, 128]], 0, 1, "II")
-    iota(T.IG[:], [[-16, 8]], 0, 1, "IG")
+    def iota(out, pat, base, cm, key, r=""):
+        run("g", g.iota, out, pat, base, cm, w=key, r=r, allow_small_or_imprecise_dtypes=True)
     iota(T.IP[:], [[0, 4]], 0, 1, "IP")
-    iota(T.I9[:, 1:9], [[1, 8]], 0, 0, "I9a")
-    iota(T.I9[:, 10:18], [[1, 8]], 8, 0, "I9b")
-    iota(T.I9[:, 0:1], [[1, 1]], 7, 0, "I9c")
-    iota(T.I9[:, 9:10], [[1, 1]], 15, 0, "I9d")
-    iota(T.IM[:], [[0, 18], [-1, 16]], 0, 1, "IM")
-    iota(T.IU[:], [[1, 16]], 0, 0, "IU")
-    iota(T.IK[:], [[16, 16]], 0, 0, "IK")
-    iota(T.I20[:], [[-16, 8], [0, 20]], 0, 1, "I20")
-    v(V.memset, T.ZR[:], 1.0, w="ZR")
-    act(T.CP[:], T.ZR[:, 0:1280], scale=0.0, r="ZR", w="CP")
-    for c in (4096, 6144):
-        act(T.X[:, c:c + 2048], T.ZR[:], scale=0.0, r="ZR", w="XD")
+    iota(T.IS[:], [[1, 16]], 0, 16, "IS")
+    iota(T.IU[:], [[1, 32]], 0, 0, "IU")
+    iota(T.II[:], [[-1, 128]], 0, 1, "II")
+    iota(T.IG[:, 1:9], [[-16, 8]], 0, 1, "IGa")
+    iota(T.IG[:, 0:1], [[1, 1]], -112, 1, "IGb")
+    v(V.memset, T.M1[:], -1.0, w="M1")
+    run("g", g.affine_select, T.DB[:], T.M1[:], [[0, 2], [-16, 8], [0, NPL]], A.is_equal, 0.0, 0, 1, r="M1", w="DB")
+    iota(T.I9[:, 1:9], [[NPL, 8]], 28, 0, "I9a")
+    iota(T.I9[:, 0:10:9], [[0, 2]], 28 + 7 * NPL, 0, "I9b")
+    iota(T.IT[:], [[16, 16]], 0, 256, "IT")
+    iota(T.IA[:], [[256, 16]], 0, 0, "IA")
+    iota(T.IL[:], [[0, NQ], [256, 16 // NQ]], 0, 0, "IL")
+    for buf, c in (("ZR", 1.0), ("CQ", 0.0), ("D0", 1.0), ("LQ", 0.0), ("ONE", 1.0), ("EXT", 0.0), ("CP", 0.0), ("ZER", 0.0)):
+        v(V.memset, T[buf][:], c, w=buf)
+    v(V.memset, T.X[:, 4096:4112], 32.0, w="XE")
+    v(V.memset, T.ZR[:, 0:1024:8], 0.0, w="ZR")
+    v(V.memset, T.LQ[0:1, :], 2.0 ** -5, r="LQ", w="LQa")
+    v(V.memset, T.LQ[32:33, :], 2.0 ** -22, r="LQ", w="LQb")
+    cq = {0: 64, 1: -16, 8: 24, 9: -24, 13: 27, 14: -27, 16: 29, 17: -29, 18: 30, 19: 1, 20: 1}
+    for q_, c in cq.items():
+        v(V.memset, T.CQ[:, q_:336:NPL], float(c), r="CQ", w="CQ%d" % q_)
+    cqk = "LQ LQa LQb CQ " + " ".join("CQ%d" % q_ for q_ in cq)
+    for q_ in (0, 1, 9, 14, 17, 19):
+        v(V.memset, T.D0[:, q_:336:NPL], 0.0, r="D0", w="D0%d" % q_)
     d0k = "D0 " + " ".join("D0%d" % q_ for q_ in (0, 1, 9, 14, 17, 19))
-    c2k = "C2 C20 C28 C213 C216 C218"
+    C = {n: T.COL[:, i:i + 1] for i, n in enumerate("p15 s8 n24 zb x16 lo hi sel h168 m0 thx".split())}
+    ts(T.IQ[:, 0:1], T.IP[:, 0:1], 15, A.bitwise_and, r="IP", w="IQ0")
+    ts(T.POS[:], T.IS[:], 255, A.bitwise_and, r="IS", w="POS")
+    cp(C["p15"], T.IQ[:, 0:1], r="IQ0", w="p15")
+    cp(T.POSU[:], T.POS[:], r="POS", w="POSU")
+    ts(C["hi"], T.IQ[:, 0:1], 8, A.is_ge, r="IQ0", w="hi")
+    ts(C["m0"], T.IQ[:, 0:1], 0, A.is_equal, r="IQ0", w="m0")
+    ts(T.MT[:], T.IU[:], C["p15"], A.is_le, 8192, A.mult, r="IU p15", w="MT")
+    ts(T.RR[:, 32:48], T.IU[:, 0:16], C["p15"], A.is_equal, r="IU p15", w="RR1")
+    ts(C["lo"], C["hi"], C["m0"], A.add, 0, A.is_equal, r="hi m0", w="lo")
 
-    def consts_scan():
-        v(V.memset, T.D0[:], 1.0, w="D0")
-        v(V.memset, T.C2[:], 0.0, w="C2")
-        for q_ in (0, 1, 9, 14, 17, 19):
-            v(V.memset, T.D0[:, q_:160:20], 0.0, r="D0", w="D0%d" % q_)
-        for q_, c in ((0, -2.0), (8, 3.0), (13, 2.0), (16, 1.0), (18, 1.0)):
-            v(V.memset, T.C2[:, q_:160:20], c, r="C2", w="C2%d" % q_)
+    def slot(u):
+        k = "M" if u == 0 else "S"
+        return T["H" + k][:, 128 * u:128 * u + 128], T["LL" + k][:, 128 * u:128 * u + 128], T["W" + k][:, WW * u:WW * u + WW], k
 
-    v(V.tensor_scalar, T.IDF[:], T.II[:], 0, None, A.is_equal, r="II", w="IDF")
-    v(V.tensor_scalar, T.P15I[:, 1:2], T.IP[:, 0:1], 3, 1, A.arith_shift_right, A.bitwise_and, r="IP", w="P15b")
-    v(V.tensor_copy, T.PB[:, 1:2], T.P15I[:, 1:2], r="P15b", w="PB1")
-    v(V.tensor_scalar, T.PB[:, 0:1], T.P15I[:, 1:2], -1, 1, A.mult, A.add, r="P15b", w="PB0")
-    for b_ in range(2):
+    def lengths():
+        ts(T.NU[:], T.NP[:], 1, A.add, 16, A.min, r="NP", w="NU")
+        act(T.MS[:], T.MT[:].indirect(T.NU[:]), r="MT NU", w="MS")
+
+    def rows(b_, bank, last):
         for w_ in range(2):
             c = 128 * (2 * b_ + w_)
-            v(V.tensor_scalar, T.RA[:, c:c + 128], T.II[:], 8 * (b_ - w_), T.PB[:, b_:b_ + 1], A.is_equal, A.mult, r="II PB%d" % b_, w="RA%d%d" % (b_, w_))
-    v(V.tensor_copy, T.SDF[:], T.SDI[:], r="SDI", w="SDF")
-    v(V.tensor_copy, T.NLF[:], T.NLI[:], r="NLI", w="NLF")
-    for hf in range(2):
-        mm(T.B4[:, 8 * hf:8 * hf + 8], T.SDF[:, 128 * hf:128 * hf + 128], T.IDF[0:8, 0:8], r="SDF IDF", w="B4sd", b="B4")
-    for hf in range(2):
-        mm(T.B4[:, 16 + 8 * hf:24 + 8 * hf], T.NLF[:, 128 * hf:128 * hf + 128], T.IDF[0:8, 0:8], r="NLF IDF", w="B4sd", b="B4")
-    v(V.memset, T.ROW0[:], 0.0, w="ROW0")
-    v(V.tensor_scalar, T.IG[:], T.IG[:], 4, None, A.arith_shift_right, r="IG", w="IG")
-    v(V.tensor_scalar, T.KB[:], T.IG[:], 0, None, A.is_equal, r="IG", w="KB")
-    v(V.tensor_scalar, T.KF[:], T.IG[:], 0, None, A.is_equal, r="IG", w="KF")
-    v(V.tensor_scalar, T.IM[:], T.IM[:], 15, None, A.bitwise_and, r="IM", w="IM")
-    v(V.tensor_scalar, T.ME[:], T.IM[:], 0, None, A.is_equal, r="IM", w="ME")
-    v(V.tensor_copy, T.LS9[:], T.I9[:], r="I9a I9b I9c I9d", w="LS9")
-    v(V.tensor_scalar, T.LK9[:], T.I9[:], 20, 19, A.mult, A.add, r="I9a I9b I9c I9d", w="LK9")
-    v(V.tensor_copy, T.LU[:], T.IU[:], r="IU", w="LU")
-    v(V.tensor_copy, T.SI[:], T.B4[:, 0:16], r="B4sd", w="SI", b="B4")
-    v(V.tensor_copy, T.N0[:], T.B4[:, 16:32], r="B4sd", w="N0", b="B4")
-    v(V.tensor_scalar, T.P15I[:, 0:1], T.IP[:, 0:1], 15, None, A.bitwise_and, r="IP", w="P15I")
-    v(V.tensor_copy, T.P15[:], T.P15I[:, 0:1], r="P15I", w="P15")
-    v(V.tensor_copy, T.IDB[:], T.IDF[:], r="IDF", w="IDB")
-
-    def push1(ncol, nkey, first=None):
-        if not first:
-            v(V.tensor_tensor, T.T1[:], T.SI[:], T.SI[:], A.mult, r="SI", w="T1")
-            v(V.tensor_scalar, T.U[:], ncol, 77, None, A.mult, r=nkey, w="U")
-        v(V.tensor_scalar, T.S15[:], T.SI[:], 15, None, A.bitwise_and, r="SI", w="S15")
-        if first:
-            first()
-        v(V.tensor_scalar, T.T2[:], T.T1[:], 5, None, A.arith_shift_right, r="T1", w="T2")
-        v(V.tensor_tensor, T.U[:], T.U[:], T.SI[:], A.add, r="U SI", w="U")
-        v(V.tensor_tensor, T.T1[:], T.T2[:], T.U[:], A.add, r="T2 U", w="T1")
-        v(V.tensor_scalar, T.CI[:], T.T1[:], 1023, None, A.bitwise_and, r="T1", w="CI")
-        v(V.tensor_tensor, T.EC[:], T.CI[:].indirect(T.LS9[:]), T.ME[:], A.mult, r="CI LS9 ME", w="EC")
-        v(V.tensor_copy, T.RS[:], T.S15[:].indirect(T.LS9[:]), r="S15 LS9", w="RS")
-
-    def push2(sl):
-        for hf in range(2):
-            mm(T.PG[:, 8 * hf:8 * hf + 8], T.EC[:, 144 * hf + sl:144 * hf + sl + 128], T.KF[:], r="EC KF", w="pC", b="PG0")
-        for hf in range(2):
-            mm(T.PG[:, 512 + 128 * hf:640 + 128 * hf], T.RS[:, 144 * hf + sl:144 * hf + sl + 128], T.IDB[:], r="RS IDB", w="pR", b="PG1")
-
-    def push2a():
-        v(V.tensor_copy, T.CL[:], T.PG[:, 0:16], r="pC", w="CL", b="PG0")
-        v(V.tensor_scalar, T.MK[:], T.PG[:, 512:768], T.P15[:], None, A.is_equal, r="pR P15", w="MK", b="PG1")
-
-    def push2b(ls):
-        v(V.tensor_tensor, T.MM[:], T[ls][:].indirect(T.CL[:]), T.MK[:], A.mult, r=ls + " CL MK", w="MM")
-
-    lwb = {0: (T.B5, 16, "B5"), 1: (T.PG, 1024, "PG2")}
-
-    def push2w(k_=1):
-        B, c, bk = lwb[k_]
-        for hf in range(2):
-            mm(B[:, c + 8 * hf:c + 8 + 8 * hf], T.MM[:, 128 * hf:128 * hf + 128], T.KF[:], r="MM KF", w="pW", b=bk)
-
-    def push2f():
-        mm(T.B5[:, 256:512], T.ROW0[:], T.MM[:], r="MM ROW0", w="pF", b="B5")
-
-    def push3(k_=1):
-        B, c, bk = lwb[k_]
-        v(V.tensor_copy, T.LW[:], B[:, c:c + 16], r="pW", w="LW", b=bk)
-
-    def push3f(t):
-        act(T.LF[:, 256 * t:256 * t + 256], T.B5[:, 256:512], r="pF", w="LF%d" % t, b="B5")
-
-    def push4():
-        v(V.tensor_tensor, T.EL[:], T.LW[:].indirect(T.LU[:]), T.ME[:, 0:256], A.mult, r="LW LU ME", w="EL")
-        for hf in range(2):
-            mm(T.B5[:, 8 * hf:8 * hf + 8], T.EL[:, 128 * hf:128 * hf + 128], T.KF[:], r="EL KF", w="pL", b="B5")
-
-    v(V.tensor_copy, T.W2[:, 0:256], T.WI[:], r="WIa WIb", w="W20")
-    push1(T.N0[:], "N0")
-
-    def rearr(t, b_):
-        w2 = 256 * t
-        out, bk = (T.B4[:, 128:256], "B4") if b_ == 0 else (T.PG[:, 1792:1920], "PG3")
+            mm(B[bank][:, 0:128], T.RA[:, c:c + 128], T.WN[:, w_:256:2], w_ == 0, False, "WN RA%d%d" % (b_, w_), "B%d" % bank)
         for w_ in range(2):
             c = 128 * (2 * b_ + w_)
-            mm(out, T.RA[:, c:c + 128], T.W2[:, w2 + w_:w2 + 256:2], w_ == 0, w_ == 1, r="W2%d RA%d%d" % (t, b_, w_), w="pH%d" % b_, b=bk)
+            mm(B[bank][:, 0:128], T.RB[:, c:c + 128], T.MS[:, w_:256:2], False, last and w_ == 1, "MS RB%d%d" % (b_, w_), "B%d" % bank)
 
-    def lists(b_):
-        src, bk = (T.B4[:, 128:256], "B4") if b_ == 0 else (T.PG[:, 1792:1920], "PG3")
-        v(V.tensor_copy, T.LH[:, 128 * b_:128 * b_ + 128], src, r="pH%d" % b_, w="LH%d" % b_, b=bk)
+    def high_out(u):
+        ts(slot(u)[0], B[1][:, 0:128], EMPTY, A.min, w="H%s%d" % (slot(u)[3], u), b="B1")
 
-    rearr(0, 0)
-    rearr(0, 1)
-    push2(16)
-    lists(0)
-    act(T.KN[:], T.KB[:], scale=-1.0, r="KB", w="KN")
-    act(T.K2[:], T.KB[:], scale=2.0, r="KB", w="K2")
-    act(T.NIB[:], T.IDB[:], scale=-1.0, r="IDB", w="NIB")
-    act(T.ROW0[:, 0:128:16], T.KF[:], r="KF", w="ROW0")
-    cpk = ["CP"] * 5
-    for k_ in (1, 2, 3, 0, 4):
-        rr = k_ % 4
-        for h in HS[k_ // 4:]:
-            for j in (rr, rr - h):
-                if 0 <= j < h:
-                    key, c = "CP%d%d" % (k_, h), 160 * k_ + BASE[h] + j
-                    act(T.CP[:, c:160 * k_ + 160:20], T.KN[:], r="KN CP", w=key)
-                    cpk[k_] += " " + key
-    act(T.SH[:, 768:1024], T.W2[:, 0:256], scale=0.0, r="W20", w="SH3")
-    act(T.SH[:, 1536:1792], T.W2[:, 0:256], scale=0.0, r="W20", w="SH6")
-    act(T.ONEF[:], T.IDF[:], F.Identity, scale=0.0, bias=1.0, r="IDF", w="ONEF")
-    act(T.NEG[:], T.W2[:, 0:256], F.Identity, scale=0.0, bias=-128.0, r="W20", w="NEG")
-    push2a()
-    send("LS", prv, T.LSN[:], T.LS[:], r="LS")
+    def row_of_ls():
+        ts(T.S15[:], T.SI[:], 15, A.bitwise_and, r="SI", w="S15")
+        tt(T.T1[:], T.SI[:], T.SI[:], A.mult, r="SI", w="T1")
+        ts(T.U7[:], T.NP[:], 77, A.mult, r="NP", w="U7")
+        cp(T.SU[:], T.S15[:], r="S15", w="SU")
+        act(T.MK[:], T.RR[:, 32:48].indirect(T.SU[:]), r="RR1 SU", w="MK")
 
-    def first0():
-        lists(1)
+    def col_of_ls(between=None):
+        ts(T.T2[:], T.T1[:], 5, A.arith_shift_right, r="T1", w="T2")
+        tt(T.U7[:], T.U7[:], T.SI[:], A.add, r="U7 SI", w="U7")
+        tt(T.T1[:], T.T2[:], T.U7[:], A.add, r="T2 U7", w="T1")
+        ts(T.T2[:], T.T1[:], 1023, A.bitwise_and, r="T1", w="T2")
+        cp(T.CU[:], T.T2[:], r="T2", w="CU")
 
-    v(V.tensor_copy, T.THF[:], T.THI[:], r="THI", w="THF")
-    v(V.tensor_scalar, T.DB[:], T.I20[:], 0, None, A.is_equal, r="I20", w="DB")
-    v(V.tensor_scalar, T.BC[:], T.THF[:], -1, None, A.mult, r="THF", w="BC")
+    def letters(u, ls):
+        _, lo, wf, k = slot(u)
+        tt(T.MM[:], T[ls][:].indirect(T.CU[:]), T.MK[:], A.mult, r=ls + " CU MK", w="MM")
+        for w_ in range(2):
+            mm(B[2][:, 0:128], T.EXT[:, 8 - 8 * w_:136 - 8 * w_], T.MM[:, w_:256:2], False, w_ == 1, "MM EXT", "B2")
+        mm(B[3][:, 0:256], T.EXT[:, 8:136], T.MM[:], False, True, "MM EXT", "B3")
+        ts(wf[:, 264:280], T.SI[:], 5, A.mult, -16, A.add, r="SI", w="Ws%d" % u)
+        ts(wf[:, 280:296], T.NP[:], 1, A.add, 16, A.min, r="NP", w="Wn%d" % u)
+        ts(lo, B[2][:, 0:128], EMPTY, A.min, w="L%s%d" % (k, u), b="B2")
+        act(wf[:, 0:256], B[3][:, 0:256], w="Ww%d" % u, b="B3")
 
-    shk = "SH3 SH6 SHf SHg " + " ".join("SA%d SB%d" % (h, h) for h in (8, 5, 3, 2, 1, 0))
+    def words_in():
+        mm(B[3][:, 0:256], T.IZ[:], T.WN[:], True, False, "IZ WN", "B3")
 
-    def n1(ncol, nkey):
-        v(V.tensor_scalar, T.N1[:], ncol, 1, 16, A.add, A.min, r=nkey, w="N1")
+    def wkey(u):
+        return "WM%d" % u if u else "Ww0 Ws0 Wn0 Wz"
 
-    def thr():
-        for h in HS:
-            e = BASE[h] + h - 1
-            v(V.tensor_scalar, T.THR[:, e:320:20], T.N1[:], 0.5 - 2 * h, 0.0, A.add, A.min, r="N1 THR", w="THR%d" % e)
-    thk = "THR THR0 " + " ".join("THR%d" % (BASE[h] + h - 1) for h in HS)
-
-    def bound():
-        v(V.tensor_scalar, T.RB[:], T.DB[:], T.BC[:], None, A.mult, r="DB BC", w="RB")
-
-    def build_sh(t):
+    def build_sh(u):
+        lo, wk = WW * u, "WM%d" % u if u else "Ww0 X0"
         for h in (8, 5, 3, 2, 1, 0):
-            c, d = 256 * SLOT[h], 17 - h
-            dma("sh", T.SH[d:128, c:c + 256], T.W2R[0:128 - d, 256 * t:256 * t + 256], r="W2R%d" % t, w="SA%d" % h)
-            dma("sh", T.SH[0:d, c:c + 256], T.W2R[128 - d:128, 256 * t:256 * t + 256], r="W2R%d" % t, w="SB%d" % h)
-        dma("sh2", T.SH[17:128:16, 1280:1536], T.LFR[0:112:16, 256 * t:256 * t + 256], r="LFR%d SA0 SB0" % t, w="SHf")
-        dma("sh2", T.SH[1:2, 1280:1536], T.LFR[112:113, 256 * t:256 * t + 256], r="LFR%d SA0 SB0" % t, w="SHg")
+            c = 256 * h
+            if u < TV - 1:
+                d = 17 - h
+                dma("sh", T.SH[d:128, c:c + 256], T.WM[0:128 - d, lo:lo + 256], r=wk, w="SA%d" % h)
+                dma("sh", T.SH[0:d, c:c + 256], T.WM[128 - d:128, lo:lo + 256], r=wk, w="SB%d" % h)
+            else:
+                dma("sh", T.SH[0:128 - h, c:c + 256], T.WM[h:128, lo:lo + 256], r=wk, w="SA%d SB%d" % (h, h))
+    shk = "SH4 SH6 " + " ".join("SA%d SB%d" % (h, h) for h in (8, 5, 3, 2, 1, 0))
 
-    def idx(h, j):
-        return PAIRS.index((h, j))
+    lengths()
+    row_of_ls()
+    for b_ in (1, 0):
+        for w_ in range(2):
+            c = 128 * (2 * b_ + w_)
+            ts(T.RA[:, c:c + 128], T.II[:], 8 * (b_ - w_), A.is_equal, C["hi" if b_ else "lo"], A.mult, r="II hi lo", w="RA%d%d" % (b_, w_))
+            act(T.RB[:, c:c + 128], T.RA[:, c:c + 128], r="RA%d%d" % (b_, w_), w="RB%d%d" % (b_, w_))
+        if b_:
+            cp(T.WN[:], T.WI[:].indirect(T.POSU[:]), r="WIa WIb POSU", w="WN")
+            col_of_ls()
+            rows(1, 1, True)
+    ts(T.IG[:, 0:9], T.IG[:, 0:9], 4, A.arith_shift_right, r="IGa IGb", w="IG")
+    ts(T.KF[:, 0:9], T.IG[:, 0:9], 0, A.is_equal, r="IG", w="KF")
+    ts(C["zb"], C["m0"], -1, A.mult, 1, A.add, r="m0", w="zb")
+    cp(T.EXT[:, 8:136:16], T.KF[:, 1:9], r="KF", w="EXT")
+    ts(T.IZ[:], T.II[:], 0, A.is_equal, C["zb"], A.mult, r="II zb", w="IZ")
+    rows(0, 2, False)
+    words_in()
+    high_out(0)
+    send("LS", prv, T.LSN[:], T.LS[:], r="LS")
+    ts(T.IDB[:], T.II[:], 0, A.is_equal, r="II", w="IDB")
+    cp(C["thx"], T.THI[:], r="THI", w="thx")
+    cp(T.WTF[:], T.WTI[:], r="WTI", w="WTF")
+    tt(C["thx"], C["thx"], C["zb"], A.add, r="thx zb", w="thx")
+    act(T.KN[:], T.KF[:, 1:9], scale=-1.0, r="KF", w="KN")
+    act(T.NIB[:], T.IDB[:], scale=-1.0, r="IDB", w="NIB")
+    act(T.K2[:], T.KF[:, 1:9], scale=2.0, r="KF", w="K2")
+    act(T.KB[:], T.KF[:, 1:9], r="KF", w="KB")
+    act(T.THL[:], T.ONE[:], scale=C["thx"], r="ONE thx", w="THL")
+    ts(T.WP[:], T.KF[:, 1:9], T.WTF[:], A.mult, 2.0 ** -22, A.mult, r="KF WTF", w="WP")
+    ts(T.WQ[:], T.KF[:, 1:9], T.WTF[:], A.mult, -2.0 ** -22, A.mult, r="KF WTF", w="WQ")
+    v(V.memset, T.DB[:, 0:336:NPL], 0.0, r="DB", w="DBa")
+    v(V.memset, T.DB[:, 20:336:NPL], 64.0, r="DB", w="DBb")
+    for h in HS:
+        cp(T.CP[:, 1 + BASE[h]:169:NPL], T.KN[:], r="KN CP", w="CP%d" % h)
+    cpk = "CP " + " ".join("CP%d" % h for h in HS)
+    letters(0, "LS")
+    build_sh(0)
+    iota(T.WM[:, 256:264], [[0, 8]], 0, 0, "Wz")
+    iota(T.ZROW[0:32, 0:16], [[0, 16]], 0, 0, "ZROW")
+    iota(T.ZROW[0:32, 16:32], [[8, 16]], 0, 0, "ZROWb")
+    iota(T.U[:, 0:8], [[0, 8]], 0, 0, "Uz")
+    iota(T.ZC[:, 2048:2064], [[0, 16]], 0, 0, "ZCz")
+    iota(T.SH[:, 1024:1280], [[0, 256]], 0, 0, "SH4")
+    iota(T.SH[:, 1536:2048], [[0, 512]], 0, 0, "SH6")
+    iota(T.NEG[:], [[0, 256]], -128, 0, "NEG")
+    for u in range(1, TV):
+        iota(T.WS[:, WW * u + 256:WW * u + 264], [[0, 8]], 0, 0, "Wz%d" % u)
+    iota(T.FO[:, 0:8], [[0, 8]], 0, 0, "FOz")
 
-    def pd(hf, lo, hi):
-        return (T.PD0 if hf == 0 else T.PD1)[:, lo:hi]
+    def late_consts():
+        ts(T.IQ[:, 1:2], T.IP[:, 0:1], 4, A.arith_shift_right, r="IP", w="IQ1")
+        ts(T.IQ[:, 2:3], T.IP[:, 0:1], 7, A.bitwise_and, r="IP", w="IQ2")
+        ts(C["h168"], C["hi"], HALF, A.mult, r="hi", w="h168")
+        tt(C["sel"], T.IQ[:, 1:2], T.IQ[:, 2:3], A.is_equal, r="IQ1 IQ2", w="sel")
+        ts(C["s8"], C["p15"], 8, A.add, r="p15", w="s8")
+        ts(C["n24"], C["p15"], 24, A.add, r="p15", w="n24")
+        ts(T.CV[:], T.I9[:], C["h168"], A.add, C["sel"], A.mult, r="I9a I9b h168 sel", w="CV")
+        for o, lo in ((0, 0), (16, 1)):
+            ts(T.SV[:, o:o + 8], T.KF[:, lo:lo + 8], C["s8"], A.mult, r="KF s8", w="SV%da" % o)
+            ts(T.SV[:, o + 8:o + 16], T.KF[:, lo:lo + 8], C["n24"], A.mult, r="KF n24", w="SV%db" % o)
+        ts(T.RR[:, 0:16], T.RR[:, 32:48], 2.0 ** 22, A.mult, r="RR1", w="RR2")
+        ts(T.RR[:, 16:32], T.RR[:, 32:48], 32.0, A.mult, r="RR1", w="RR3")
+        ts(C["x16"], C["p15"], 16, A.mult, r="p15", w="x16")
+        ts(C["zb"], C["p15"], 128, A.mult, -1, A.add, r="p15", w="zb")
+        ts(T.BS[:], T.IT[:], 4095, A.bitwise_and, r="IT", w="BS")
+        ts(T.BA[:], T.IA[:], C["x16"], A.add, r="IA x16", w="BA")
+        ts(T.BL[:], T.IL[:], C["x16"], A.add, r="IL x16", w="BL")
+        ts(T.M01[:], T.IU[:], C["p15"], A.is_gt, r="IU p15", w="M01")
 
-    def place(hf, h, j):
-        return (T.PD0 if hf == 0 else T.PD1)[:, BASE[h] + j:160:20]
+    def spare_columns():
+        act(T.X[:, 4112:5120], T.ZR[:, 0:1008], scale=0.0, r="ZR", w="XD")
+        for c in (5120, 6144, 7168):
+            act(T.X[:, c:c + 1024], T.ZR[:], scale=0.0, r="ZR", w="XD")
 
-    def bulk(t, mid, hole):
-        PGK = "PG0 PG1 PG2 PG3"
-        v(V.tensor_copy, T.GL[:, 1024:1536], T.X[:, 0:4096].indirect(T.LH[:, 64:96]), r="XA XB LH0", w="GLd R0d")
-        for c, k_ in ((0, "c"), (512, "a"), (1536, "b")):
-            act(T.GL[:, c:c + 512], T.X[:, 0:4096].indirect(T.LH[:, c // 16:c // 16 + 32]), r="XA XB LH0", w="GL%s R0%s" % (k_, k_))
-        for b_ in range(2):
-            if b_ == 1:
-                mid()
-            c, k_ = 512 * b_, "a" if b_ else "c"
-            mm(T.PG[:, c:c + 512], T.IDB[:], T.GL[:, c:c + 512], r="IDB GL%s R0%s" % (k_, k_), w="pg", b="PG%d" % b_)
-            c, k_ = 1024 + 512 * b_, "b" if b_ else "d"
-            for j in range(1, 6):
-                mm(T.PG[:, c + j:c + 512:8], T.IDB[:], T.GL[:, c + j:c + 512:8], r="IDB GL%s" % k_, w="pg", b="PG%d" % (2 + b_))
-        act(T.GH[:, 0:1024], T.X[:, 0:4096].indirect(T.LH[:, 128:192]), r="XA XB LH1", w="GHa")
-        act(T.GH[:, 1024:2048], T.X[:, 0:4096].indirect(T.LH[:, 192:256]), r="XA XB LH1", w="GHb")
-        hole()
+    def place(bank, hf, q_):
+        return bank[:, HALF * hf + q_:HALF * hf + HALF:NPL]
 
-        def low(hf, j):
-            gl = T.GL[:, 1024 * hf + j:1024 * hf + 1024:8]
-            key = ("R0" if j == 0 else "GL") + "ab"[hf]
-            if j < 4:
-                k_ = 4 if hf == 1 and j == 0 else j
-                mm(pd(hf, 0, 160), gl, T.CP[:, 160 * k_:160 * k_ + 160], False, False, r=key + " " + cpk[k_], w="pd%d" % hf, b="PD%d" % hf)
-                return
-            for h in HS:
-                if h > j and not (h == 8 and hf == 1):
-                    mm(place(hf, h, j), gl, T.KN[:], False, False, r=key + " KN", w="pd%d" % hf, b="PD%d" % hf)
+    def row(buf, hf, j):
+        return buf[:, 1024 * hf + j:1024 * hf + 1024:8]
 
-        def high(hf, rr):
-            for h in HS:
-                j = rr - h
-                if 0 <= j < h and not (h == 8 and hf == 1 and j not in MAXED):
-                    src, key = (T.GL, "GL") if rr < 8 else (T.GH, "GH")
-                    o = 1024 * hf + rr % 8
-                    mm(place(hf, h, j), src[:, o:1024 * hf + 1024:8], T.KN[:], False, False, r=key + "ab"[hf] + " KN", w="pd%d" % hf, b="PD%d" % hf)
+    def diff_at(hf, j):
+        if j < 6:
+            return (1 if hf == 0 else 3), 128 * (j - 2)
+        return 2, 256 * hf + 128 * (j - 6)
+
+    def bulk(t):
+        win = T.X[:, 0:4112]
+        xk = "X0 X1 X2 X3 XE "
+        Hl, Ll = T.HM[:, 128 * t:128 * t + 128], T.LLM[:, 128 * t:128 * t + 128]
+
+        def gather(q, buf, lst, c, n, key, lk):
+            if q == "v":
+                cp(buf[:, c:c + n], win.indirect(lst[:, c // 16:(c + n) // 16]), r=xk + lk, w=key)
+            else:
+                act(buf[:, c:c + n], win.indirect(lst[:, c // 16:(c + n) // 16]), r=xk + lk, w=key)
+        gather("v", T.GH, Hl, 0, 1024, "GH0", "HM%d" % t)
+        gather("a", T.GH, Hl, 1024, 1024, "GH1", "HM%d" % t)
+        gather("v", T.GL, Ll, 0, 512, "GL0a", "LM%d" % t)
+        gather("a", T.GL, Ll, 512, 512, "GL0b", "LM%d" % t)
+        gather("a", T.GL, Ll, 1024, 1024, "GL1", "LM%d" % t)
+        gl = ("GL0a GL0b", "GL1")
+        mm(PD[:, 0:336], T.THL[:], T.DB[:], True, False, "THL DB DBa DBb", "B6")
+        mm(PC[:, 0:368], T.LQ[0:64, :], T.CQ[0:64, :], True, False, cqk, "B7")
+        for bk in (1, 2, 3):
+            mm(B[bk][:, 0:512], T.ZER[0:1, :], T.ZR[0:1, 0:512], True, False, "ZER ZR", "B%d" % bk)
+
+        def highs(hf):
+            for j in range(2):
+                mm(B[0][:, 256 * hf + 128 * j:256 * hf + 128 * j + 128], T.IDB[:], row(T.GH, hf, j), True, True, "IDB GH%d" % hf, "B0")
+
+        def highd(hf):
+            for j in range(2, 8):
+                bk, c = diff_at(hf, j)
+                mm(B[bk][:, c:c + 128], T.IDB[:], row(T.GH, hf, j), False, False, "IDB GH%d" % hf, "B%d" % bk)
+
+        def sums(hf, buf, j, places, key):
+            for q_ in places:
+                mm(place(PD, hf, q_), row(buf, hf, j), T.KN[:], False, False, key + " KN", "B6")
+
+        def lows(hf):
+            for j in range(3):
+                mm(B[4 + hf][:, 128 * j:128 * j + 128], T.IDB[:], row(T.GL, hf, j), True, True, "IDB " + gl[hf], "B%d" % (4 + hf))
+
+        def lowd(hf):
+            for j in range(2, 8):
+                bk, c = diff_at(hf, j)
+                mm(B[bk][:, c:c + 128], T.NIB[:], row(T.GL, hf, j), False, j == 5 or (hf, j) == (1, 7), "NIB " + gl[hf], "B%d" % bk)
+
+        def lowsums(hf):
+            o = PD[:, HALF * hf:HALF * hf + HALF]
+            mm(o, row(T.GL, hf, 0), T.CP[:, 1:169], False, False, gl[hf] + " " + cpk, "B6")
+            mm(o, row(T.GL, hf, 1), T.CP[:, 0:168], False, False, gl[hf] + " " + cpk, "B6")
+            for j in range(1, 8):
+                pl = [BASE[h] + j - h for h in (5, 3, 2, 1) if 0 <= j - h < h] + [BASE[h] + j for h in (5, 3) if 1 < j < h]
+                sums(hf, T.GL, j, pl, gl[hf])
+
+        def zc(hf):
+            v(V.tensor_tensor_scan, T.ZC[:, 1024 * hf:1024 * hf + 1024], T.ZR[:], T.GL[:, 1024 * hf:1024 * hf + 1024], 0.0, A.mult, A.max,
+              r="ZR " + gl[hf], w="ZC%d" % hf)
+
+        def seeds(hf, last=False):
+            l = [(h, BASE[h] + h - 1, "WQ") for h in HS] + [(h, BASE[h] + h, "WP") for h in HS] + [(1, 1, "WP")]
+            for i, (h, q_, wk) in enumerate(l):
+                mm(place(PC, hf, q_), row(T.ZC, hf, h - 1), T[wk][:], False, last and i == len(l) - 1, "ZC%d %s" % (hf, wk), "B7")
+
+        def pair(hf, h, j):
+            c = 256 * MAXED.index((h, j)) + 128 * hf
+            if j + h >= 8:
+                k_ = j + h - 8
+                a, bk, o = B[0][:, 256 * hf + 128 * k_:256 * hf + 128 * k_ + 128], "B0", j
+            else:
+                a, bk, o = B[4 + hf][:, 128 * j:128 * j + 128], "B%d" % (4 + hf), j + h
+            tt(T.DL[:, c:c + 128], a, row(T.GL, hf, o), A.max, r=gl[hf], w="DL%d%d%d" % (hf, h, j), b=bk)
 
         def add(hf, h, j, last=False):
-            o = place(hf, h, j)
-            if h == 8:
-                if hf == 0:
-                    mm(o, T.D8[:, j:1024:8], T.K2[:], False, last, r="K2 D8a D8b" + (" D8j" if j == 0 else ""), w="pd0", b="PD0")
-                else:
-                    mm(o, T.D8[:, 1024 + 128 * j:1152 + 128 * j], T.K2[:] if j in MAXED else T.KB[:], False, last,
-                       r="K2 D8y%d" % j if j in MAXED else "KB D8x%d" % min(j, 4), w="pd1", b="PD1")
-            else:
-                c = 256 * idx(h, j) + 128 * hf
-                mm(o, T.DL[:, c:c + 128], T.K2[:], False, last, r="K2 DL%d%d" % (h, j), w="pd%d" % hf, b="PD%d" % hf)
+            c = 256 * MAXED.index((h, j)) + 128 * hf
+            mm(place(PD, hf, BASE[h] + j), T.DL[:, c:c + 128], T.K2[:], False, last, "K2 DL%d%d%d" % (hf, h, j), "B6")
 
-        def pair(h, j):
-            c = 256 * idx(h, j)
-            if j == 0:
-                i0, i1, key = T.PG[:, h:2048:8], T.GL[:, 0:2048:8], "R0a R0b"
-            elif j + h < 8:
-                i0, i1, key = T.PG[:, j:2048:8], T.GL[:, j + h:2048:8], "GLa GLb"
-            else:
-                i0, i1, key = T.PG[:, j:2048:8], T.GH[:, j + h - 8:2048:8], "GHa GHb"
-            v(V.tensor_tensor, T.DL[:, c:c + 256], i0, i1, A.max, r="pg " + key, w="DL%d%d" % (h, j), b=PGK)
+        def sizes(bk):
+            act(T.DA[:, 512 * (bk - 1):512 * bk], B[bk][:, 0:512], F.Abs, w="DA%d" % bk, b="B%d" % bk)
 
-        def sizes(js, B, bk):
-            n = 128 * len(js)
-            for q_, j in enumerate(js):
-                mm(B[:, 128 * q_:128 * q_ + 128], T.IDB[:], T.GL[:, 1024 + j:2048:8], True, False, r="IDB %sb" % ("R0" if j == 0 else "GL"), b=bk)
-                mm(B[:, 128 * q_:128 * q_ + 128], T.NIB[:], T.GH[:, 1024 + j:2048:8], False, True, r="NIB GHb", w="pB" + bk, b=bk)
-            act(T.D8[:, 1024 + 128 * js[0]:1024 + 128 * js[0] + n], B[:, 0:n], F.Abs, r="pB" + bk, w="D8x%d" % js[0], b=bk)
+        def add_sizes(bk):
+            for hf in range(2):
+                for j in range(2, 8):
+                    b_, c = diff_at(hf, j)
+                    if b_ == bk:
+                        c += 512 * (bk - 1)
+                        mm(place(PD, hf, BASE[8] + j), T.DA[:, c:c + 128], T.KB[:], False, False, "KB DA%d" % bk, "B6")
 
-        def row0():
-            act(T.GL[:, 0:2048:8], T.X[:, 0:4096].indirect(T.LLU[:]), r="XA XB LLU GLa GLb", w="R0a R0b R0c R0d")
-
-        early = ((2, 1), (3, 1), (3, 2), (5, 1), (5, 2))
-        for h, j in early:
-            pair(h, j)
-        v(V.tensor_tensor, T.D8[:, 0:512], T.PG[:, 0:512], T.GH[:, 0:512], A.max, r="pg GHa", w="D8a", b="PG0")
-        if t > 0:
-            v(V.tensor_copy, T.LLU[:], T.MNR[:, 32 * (t - 1) + 16:32 * t], r="MNR%d" % (t - 1), w="LLU")
-            v(V.tensor_scalar, T.S5[:], T.MNR[:, 32 * (t - 1):32 * (t - 1) + 16], 5, None, A.mult, r="MNR%d" % (t - 1), w="S5")
-            row0()
-        else:
-            push2b("LS")
+        up = [p_ for p_ in MAXED if sum(p_) >= 8]
+        dn = [p_ for p_ in MAXED if sum(p_) < 8]
+        highs(0)
+        highs(1)
+        highd(0)
+        lows(0)
+        highd(1)
+        lowd(0)
         for hf in range(2):
-            if hf == 1:
-                if t == 0:
-                    push2w(0)
-                    push3(0)
-                    push4()
-                v(V.tensor_tensor, T.D8[:, 512:1024], T.PG[:, 512:1024], T.GH[:, 512:1024], A.max, r="pg GHa", w="D8b", b="PG1")
-            mm(pd(hf, 0, 160), T.ONE[:], T.RB[:], True, False, r="ONE RB", w="pd%d" % hf, b="PD%d" % hf)
-            for rr in range(1, 8):
-                low(hf, rr)
-                if rr > 3:
-                    high(hf, rr)
-        if t == 0:
-            v(V.tensor_copy, T.LLU[:], T.B5[:, 0:16], r="pL", w="LLU", b="B5")
-            row0()
-        sizes((4, 5, 6, 7), T.B4, "B4")
-        sizes((0,), T.B5, "B5")
-        for j in MAXED:
-            v(V.tensor_tensor, T.D8[:, 1024 + 128 * j:1152 + 128 * j], T.PG[:, 1024 + j:2048:8], T.GH[:, 1024 + j:2048:8], A.max, r="pg GHb", w="D8y%d" % j, b="PG2 PG3")
-        for rr in range(8, 16):
-            high(0, rr)
-        for h, j in early:
-            for hf in range(2):
-                add(hf, h, j)
-        for j in range(1, 8):
-            add(0, 8, j)
-        for rr in (8, 9) + tuple(8 + j for j in MAXED if j > 1):
-            high(1, rr)
-        for h, j in ((5, 3), (5, 4)):
-            pair(h, j)
-            for hf in range(2):
-                add(hf, h, j)
-        for hf in range(2):
-            low(hf, 0)
-        v(V.tensor_tensor, T.D8[:, 0:1024:8], T.GL[:, 0:1024:8], T.GH[:, 0:1024:8], A.max, r="R0a GHa D8a D8b", w="D8j")
-        add(0, 8, 0)
-        for j in range(1, 8):
-            add(1, 8, j)
-        add(1, 8, 0)
-        for h in (5, 3, 2, 1):
-            pair(h, 0)
-            for hf in range(2):
-                add(hf, h, 0, h == 1)
-        if t == 0:
-            push2f()
-            push3f(0)
-            send("LF0", nxt, T.LFR[:, 0:256], T.LF[:, 0:256], r="LF0")
-        v(V.tensor_tensor_scan, T.ZC[:], T.ZR[:], T.GL[:], 0.0, A.mult, A.max, r="ZR GLa GLb R0a R0b", w="ZC")
-        act(T.ZC[:, 5:2048:8], T.GL[:, 0:2048:8], r="R0a R0b ZC", w="ZC5")
+            sums(hf, T.GH, 0, (BASE[8], BASE[5] + 3), "GH%d" % hf)
+            sums(hf, T.GH, 1, (BASE[8] + 1, BASE[5] + 4), "GH%d" % hf)
+        sizes(1)
+        zc(0)
+        for p_ in up + dn:
+            pair(0, *p_)
+        lows(1)
+        lowd(1)
+        sizes(3)
+        sizes(2)
+        lowsums(0)
+        seeds(0)
+        for p_ in up + dn:
+            add(0, *p_)
+        zc(1)
+        lowsums(1)
+        add_sizes(1)
+        o = 16 if t == TV - 1 else 0
+        act(T.ES[:], T.WM[:, WW * t + 256:WW * t + WW].indirect(T.SV[:, o:o + 16]), r=wkey(t) + " SV%da SV%db" % (o, o), w="ES")
+        seeds(1)
+        add_sizes(3)
+        add_sizes(2)
+        for i, p_ in enumerate(up + dn):
+            pair(1, *p_)
+        for i, p_ in enumerate(up + dn):
+            add(1, *p_, last=i == len(MAXED) - 1)
+            if i == 5:
+                for k_ in range(2):
+                    mm(PC[:, 336 + 16 * k_:352 + 16 * k_], T.ES[:, 128 * k_:128 * k_ + 128], T.RR[:, 32:48], False, k_ == 1, "ES RR1", "B7")
 
     def decode(t):
         last = t == TV - 1
-        rs = 16 if last else 0
-        m1 = 288 * t
-        halves = ((0, T.B4, "B4", 0), (1, T.B5, "B5", 160))
-        for hf, B, bk, c in halves:
-            v(V.tensor_tensor_scan, B[:, 0:160], T.D0[:], pd(hf, 0, 160), 0.0, A.mult, A.max, r="pd%d %s" % (hf, d0k), w="s1%d" % hf, b="PD%d %s" % (hf, bk))
-        for hf, B, bk, c in halves:
-            v(V.tensor_tensor, T.E[:, c:c + 160], B[:, 0:160], T.THR[:, c:c + 160], A.is_gt, r="s1%d %s" % (hf, thk), w="E%d" % hf, b=bk)
-        for hf, B, bk, c in halves:
-            v(V.tensor_tensor_scan, T.SC2[:, c:c + 160], T.E[:, c:c + 160], T.C2[:], 0.0, A.mult, A.add, r="E%d %s" % (hf, c2k), w="SC%d" % hf)
-        v(V.tensor_tensor, T.EK[:], T.SC2[:].indirect(T.LK9[:]), T.ME[:], A.mult, r="SC0 SC1 LK9 ME", w="EK")
-        mm(T.PG[:, 0:16], T.IDB[:], T.B8[:], True, False, r="IDB B8", w="p1", b="PG0")
-        for hf in range(2):
-            mm(T.PG[:, 8 * hf:8 * hf + 8], T.EK[:, 144 * hf + 16:144 * hf + 144], T.KB[:], False, hf == 1, r="EK KB", w="p1", b="PG0")
-        for hf in range(2):
-            mm(T.PG[:, 512 + 8 * hf:520 + 8 * hf], T.EK[:, 144 * hf + rs:144 * hf + rs + 128], T.K256[:], r="EK K256", w="p2", b="PG1")
-        kap = T.SC2[:, 19:320:20]
-        v(V.tensor_scalar, T.NH[:], kap, 5, None, A.is_equal, r="SC0 SC1", w="NH")
-        v(V.tensor_scalar, T.DU[:], T.NH[:], 4096, None, A.mult, r="NH", w="DU")
-        v(V.tensor_scalar, T.H1[:], T.NH[:], -6, 1, A.mult, A.add, r="NH", w="H1")
-        v(V.tensor_tensor, T.S5[:], T.S5[:], T.NH[:], A.mult, r="S5 NH", w="S5")
-        v(V.tensor_copy, T.L1[:], T.PG[:, 0:16], r="p1", w="L1", b="PG0")
-        v(V.tensor_tensor, T.H[:], T.H1[:], kap, A.add, r="H1 SC0 SC1", w="H")
-        v(V.tensor_copy, T.M1S[:, m1:m1 + 128], T.ZC[:].indirect(T.L1[:, 0:8]), r="ZC ZC5 L1", w="Za")
-        act(T.M1S[:, m1 + 128:m1 + 256], T.ZC[:].indirect(T.L1[:, 8:16]), r="ZC ZC5 L1", w="Zb")
-        act(T.M1S[:, m1 + 256:m1 + 272], T.PG[:, 512:528], r="p2", w="Zc", b="PG1")
-        for hf in range(2):
-            mm(T.PG[:, 1024 + 8 * hf:1032 + 8 * hf], T.M1S[:, m1 + 128 * hf:m1 + 128 * hf + 128], T.WTB[:], r="Z%s WTB" % "ab"[hf], w="pt", b="PG2")
-        mm(T.PG[:, 1536:1552], T.IDB[:], T.B16[:], True, False, r="IDB B16", w="p3", b="PG3")
-        v(V.tensor_tensor, T.AD[:], T.S5[:], T.H[:], A.add, r="S5 H", w="AD")
-        v(V.tensor_tensor, T.NP[:], T.N1[:], T.H[:], A.subtract, r="N1 H", w="NP")
-        v(V.tensor_tensor, T.SUM[:], T.PG[:, 1024:1040], T.AD[:], A.add, r="pt AD", w="SUM", b="PG2")
+        z = T.ZS[:, ZW * t:ZW * t + ZW]
+        v(V.tensor_tensor_scan, T.S1[:], T.D0[:], PD[:, 0:336], 0.0, A.mult, A.max, r=d0k, w="S1", b="B6")
+        mm(B[0][:, 0:32], T.ONE[0:1, :], T.ZROW[0:1, :], True, False, "ONE ZROW ZROWb", "B0")
+        v(V.tensor_tensor_scan, T.U[:, 8:344], PC[:, 0:336], T.S1[:], 0.0, A.add, A.min, r="S1", w="U", b="B7")
+        cp(T.E[:], T.U[:].indirect(T.CV[:, 0:9]), r="U Uz CV", w="E")
+        mm(B[0][:, 0:32], T.E[:, 16:144], T.RR[:, 0:32], False, True, "E RR2 RR3", "B0")
+        o = 16 if last else 0
+        mm(B[4][:, 0:16], T.E[:, o:o + 128], T.RR[:, 0:16], True, True, "E RR2", "B4")
+        ts(T.ZO[:], B[0][:, 16:32], C["zb"], A.add, r="zb", w="ZO", b="B0")
+        cp(T.UI[:], B[0][:, 0:16], w="UI", b="B0")
+        act(z[:, 0:256], T.ZC[:].indirect(T.ZO[:]), r="ZC0 ZC1 ZCz ZO", w="Za")
+        cp(T.UR[:], B[4][:, 0:16], w="UR", b="B4")
+        ts(T.FI[:], T.UI[:], (1 << 21) + 15, A.bitwise_and, r="UI", w="FI")
+        ts(T.H[:], T.UR[:], 17, A.arith_shift_right, 15, A.bitwise_and, r="UR", w="H")
+        ts(z[:, 256:272], T.FI[:], 4096, A.min, r="FI", w="Zb")
+        send("Z%d" % t, nxt, T.ZM[:, ZW * t:ZW * t + ZW], z, r="Za Zb")
+        ts(T.HB[:], T.UR[:], 9, A.arith_shift_right, 0xF00, A.bitwise_and, r="UR", w="HB")
+        tt(T.NP[:], PC[:, 352:368], T.H[:], A.subtract, r="H", w="NP", b="B7")
+        tt(T.PL[:], T.HB[:], T.POS[:], A.add, r="HB POS", w="PL")
         if last:
-            v(V.tensor_copy, T.M1S[:, m1 + 272:m1 + 288], T.NP[:], r="NP", w="Zd")
+            cp(T.NU[:], T.NP[:], r="NP", w="NU")
+            act(T.MS[:], T.M01[:].indirect(T.NU[:]), r="M01 NU", w="MS")
         else:
-            v(V.tensor_copy, T.M1S[:, m1 + 272:m1 + 288], T.NP[:].indirect(T.ROT[:, 0:1]), r="NP ROT", w="Zd")
-        v(V.tensor_scalar, T.V15[:], T.SUM[:], 15, None, A.bitwise_and, r="SUM", w="V15")
-        v(V.tensor_tensor, T.VV[:], T.V15[:], T.DU[:], A.max, r="V15 DU", w="VV")
-        v(V.tensor_tensor, T.EV[:], T.VV[:].indirect(T.LU[:]), T.ME[:, 0:256], A.mult, r="VV LU ME", w="EV")
-        for hf in range(2):
-            mm(T.PG[:, 1536 + 8 * hf:1544 + 8 * hf], T.EV[:, 128 * hf:128 * hf + 128], T.KB[:], False, hf == 1, r="EV KB", w="p3", b="PG3")
-        v(V.tensor_scalar, T.SI[:], T.SUM[:], 4095, None, A.bitwise_and, r="SUM", w="SI")
+            lengths()
+        cp(T.PU[:], T.PL[:], r="PL", w="PU")
         if not last:
-            v(V.tensor_scalar, T.U[:], T.NP[:], 77, None, A.mult, r="NP", w="U")
-            v(V.tensor_tensor, T.T1[:], T.SI[:], T.SI[:], A.mult, r="SI", w="T1")
-        v(V.tensor_copy, T.MLS[:, 16 * t:16 * t + 16], T.PG[:, 1536:1552], r="p3", w="MLS", b="PG3")
-        send("M1%d" % t, nxt, T.M1R[:, m1:m1 + 288], T.M1S[:, m1:m1 + 288], r="Za Zb Zc Zd")
-        send("ML%d" % t, nxt, T.MLR[:, 16 * t:16 * t + 16], T.MLS[:, 16 * t:16 * t + 16], r="MLS")
+            act(T.WN[:], T.SH[:].indirect(T.PU[:]), r="PU " + shk, w="WN")
+            rows(1, 1, True)
+        ts(T.NH[:], T.UR[:], 1 << 21, A.is_ge, r="UR", w="NH")
+        tt(T.A5[:], PC[:, 336:352], T.NH[:], A.mult, r="NH", w="A5", b="B7")
+        tt(T.SUM[:], T.A5[:], T.UR[:], A.add, r="A5 UR", w="SUM")
+        ts(T.SI[:], T.SUM[:], 4095, A.bitwise_and, r="SUM", w="SI")
 
-    def xupdate(t, cols, lo, e0, e1, ck, xk):
-        win = T.X[:, lo:8192]
-        v(V.tensor_tensor, T.XT[:, e0:e1], win.indirect(cols), T.M1R[:, 288 * t + e0:288 * t + e1], A.add, r="M1R%d %s %s" % (t, ck, xk), w="XT")
-        v(V.tensor_scalar, T.XU[:, e0:e1], T.XT[:, e0:e1], 0.5, 127.75, A.mult, A.add, r="XT", w="XU")
-        v(V.tensor_tensor, win.indirect(cols), T.XU[:, e0:e1], T.NEG[:, e0:e1], A.add, r="XU NEG " + ck, w=xk)
+    def columns(t, base):
+        tt(T.CI[:], T.ZM[:, ZW * t + 256:ZW * t + ZW], T[base][:], A.add, r="ZM%d %s" % (t, base), w="CI")
+        cp(T.CX[:], T.CI[:], r="CI", w="CX")
 
-    def first():
-        bound()
-        v(V.memset, T.ONE[:], 1.0, w="ONE")
-        v(V.memset, T.THR[:], -1.0, w="THR")
-        v(V.memset, T.THR[:, 0:320:20], 1000.0, r="THR", w="THR0")
-        n1(T.N0[:], "N0")
-        thr()
-        v(V.memset, T.ZR[:, 0:2048:8], 0.0, r="ZR", w="ZR")
-        v(V.tensor_copy, T.WTF[:], T.WTI[:], r="WTI", w="WTF")
-        v(V.tensor_scalar, T.BI[:], T.IK[:], T.P15[:], None, A.add, r="IK P15", w="BI")
-        act(T.WTB[:], T.KB[:], scale=T.WTF[:], r="KB WTF", w="WTB")
-        act(T.K256[:], T.KB[:], scale=256.0, r="KB", w="K256")
-        act(T.B8[:], T.BI[:], scale=8.0, r="BI", w="B8")
-        act(T.B16[:], T.BI[:], scale=16.0, r="BI", w="B16")
-        v(V.tensor_scalar, T.S5[:], T.SI[:], 5, None, A.mult, r="SI", w="S5")
+    def xupdate(t, lo, e0, e1, xk):
+        win, cols = T.X[:, lo:8192], T.CX[:, e0 // 16:e1 // 16]
+        tt(T.XT[:, e0:e1], win.indirect(cols), T.ZM[:, ZW * t + e0:ZW * t + e1], A.add, r="ZM%d CX %s" % (t, xk), w="XT")
+        ts(T.XU[:, e0:e1], T.XT[:, e0:e1], 0.5, A.mult, 127.75, A.add, r="XT", w="XU")
+        tt(win.indirect(cols), T.XU[:, e0:e1], T.NEG[:, e0:e1], A.add, r="XU NEG CX", w=xk)
 
-    def rot_list():
-        v(V.tensor_scalar, T.P15I[:, 2:3], T.P15I[:, 0:1], 8, None, A.bitwise_and, r="P15I", w="P15c")
-        v(V.tensor_scalar, T.P15I[:, 3:4], T.P15I[:, 0:1], -1, None, A.add, r="P15I", w="P15d")
-        v(V.tensor_scalar, T.P15I[:, 3:4], T.P15I[:, 3:4], 7, None, A.bitwise_and, r="P15d", w="P15d")
-        v(V.tensor_tensor, T.P15I[:, 2:3], T.P15I[:, 2:3], T.P15I[:, 3:4], A.add, r="P15c P15d", w="P15c")
-        v(V.tensor_copy, T.ROT[:, 0:1], T.P15I[:, 2:3], r="P15c", w="ROT")
-
+    late_consts()
     for t in range(TV):
-        if t < TV - 1:
-            send("W2%d" % t, nxt, T.W2R[:, 256 * t:256 * t + 256], T.W2[:, 256 * t:256 * t + 256], r="W2%d" % t)
-            build_sh(t)
-        else:
-            for h in (8, 5, 3, 2, 1, 0):
-                c = 256 * SLOT[h]
-                dma("sh", T.SH[0:128 - h, c:c + 256], T.W2[h:128, 1024:1280], r="W24", w="SA%d SB%d" % (h, h))
-            dma("sh2", T.SH[0:128:16, 1280:1536], T.LFR[0:128:16, 1024:1280], r="LFR4 SA0 SB0", w="SHf SHg")
-        bulk(t, *((first0, first) if t == 0 else (mid, hole)))
+        bulk(t)
         if t == 0:
-            consts_scan()
-            rot_list()
+            spare_columns()
         decode(t)
         if t == TV - 1:
             break
         u = t + 1
-        m1 = 288 * t
-        push1(T.NP[:], "NP", lambda: v(V.tensor_reduce, T.NS[:], T.NH[:], AxisListType.X, A.add, r="NH", w="NS"))
-        v(V.tensor_copy, T.MNS[:, 32 * t:32 * t + 16], T.SI[:].indirect(T.ROT[:, 0:1]), r="SI ROT", w="MNa")
-        v(V.tensor_tensor, T.KBI[:], T.M1R[:, m1 + 256:m1 + 272], T.BI[:], A.add, r="M1R%d BI" % t, w="KBI")
-        v(V.tensor_copy, T.L2[:], T.KBI[:], r="KBI", w="L2")
-        act(T.W2[:, 256 * u:256 * u + 256], T.SH[:].indirect(T.L2[:]), r="L2 " + shk, w="W2%d" % u)
-        mm(T.PG[:, 256:257], T.ONEF[:], T.NS[:], r="ONEF NS", w="pA", b="PG0")
-        push2(0)
-        rearr(u, 0)
-        push2a()
-        push2b("LSN")
-        push2w()
-        rearr(u, 1)
-        push2f()
-        v(V.tensor_scalar, T.AI[:], T.PG[:, 256:257], -1, 2048, A.mult, A.add, r="pA", w="AI", b="PG0")
-        xupdate(t, T.MLR[:, 16 * t:16 * t + 16], 0, 0, 256, "MLR%d" % t, "XA XB XD")
-        lists(0)
+        row_of_ls()
+        rows(0, 2, False)
+        mm(B[5][:, 0:16], T.ONE[:], T.NH[:], True, True, "ONE NH", "B5")
+        words_in()
+        col_of_ls()
+        high_out(u)
+        send("H%d" % u, nxt, T.HM[:, 128 * u:128 * u + 128], slot(u)[0], r="HS%d" % u)
+        act(T.NJ[:], B[5][:, 0:16], scale=-1.0, accum_out=T.NS[:], w="NS", b="B5")
+        letters(u, "LSN")
+        send("L%d" % u, nxt, T.LLM[:, 128 * u:128 * u + 128], slot(u)[1], r="LS%d" % u)
+        send("W%d" % u, nxt, T.WM[:, WW * u:WW * u + WW], slot(u)[2], r="Ww%d Ws%d Wn%d Wz%d" % (u, u, u, u))
+        build_sh(u)
+        cp(T.AI[:], T.NS[:], r="NS", w="AI")
+        columns(t, "BS" if t % 2 else "BA")
+        ts(T.AJ[:], T.AI[:], 15, A.bitwise_and, r="AI", w="AJ")
+        ts(T.BC[:], T.AJ[:], C["m0"], A.mult, C["thx"], A.add, r="AJ m0 thx", w="BC")
+        act(T.THL[:], T.ONE[:], scale=T.BC[:], r="ONE BC", w="THL")
+        xupdate(t, 0, 0, 256, XK)
 
-        push3()
-
-        def mid(m1=m1):
-            lists(1)
-            push4()
-            v(V.tensor_scalar, T.AJ[:], T.AI[:], 15, None, A.bitwise_and, r="AI", w="AJ")
-            n1(T.M1R[:, m1 + 272:m1 + 288], "M1R%d" % (m1 // 288))
-
-        def hole(t=t, u=u):
-            v(V.tensor_copy, T.MNS[:, 32 * t + 16:32 * t + 32], T.B5[:, 0:16], r="pL", w="MNb", b="B5")
-            send("MN%d" % t, nxt, T.MNR[:, 32 * t:32 * t + 32], T.MNS[:, 32 * t:32 * t + 32], r="MNa MNb")
-            push3f(u)
-            send("LF%d" % u, nx2 if u < 4 else nxt, T.LFR[:, 256 * u:256 * u + 256], T.LF[:, 256 * u:256 * u + 256], r="LF%d" % u)
-            v(V.tensor_scalar, T.BC[:], T.AJ[:], T.THF[:], -1, A.add, A.mult, r="AJ THF", w="BC")
-            thr()
-            bound()
-
-    v(V.tensor_copy, T.SF[:], T.SI[:], r="SI", w="SF")
-    v(V.tensor_tensor, T.KBI[:], T.M1S[:, 4 * 288 + 256:4 * 288 + 272], T.BI[:], A.add, r="Zc BI", w="KBI")
-    v(V.tensor_copy, T.L2[:], T.KBI[:], r="KBI", w="L2")
-    v(V.tensor_copy, T.RS[:], T.NP[:].indirect(T.LS9[:]), r="NP LS9", w="RS")
-    for hf in range(2):
-        mm(T.PG[:, 512 + 128 * hf:640 + 128 * hf], T.RS[:, 144 * hf + 16:144 * hf + 144], T.IDB[:], r="RS IDB", w="pR", b="PG1")
-    for hf in range(2):
-        mm(T.PG[0:8, 128 * hf:128 * hf + 128], T.NP[:, 8 * hf:8 * hf + 8], T.IDF[:], r="NP IDF", w="pN", b="PG0")
-    for hf in range(2):
-        mm(T.PG[0:8, 1024 + 128 * hf:1152 + 128 * hf], T.SF[:, 8 * hf:8 * hf + 8], T.IDF[:], r="SF IDF", w="pS", b="PG2")
-    v(V.tensor_scalar, T.MK[:], T.PG[:, 512:768], T.P15[:], None, A.is_gt, r="pR P15", w="MK", b="PG1")
-    v(V.tensor_tensor, T.YW[:], T.SH[:].indirect(T.L2[:]), T.MK[:], A.mult, r="L2 MK " + shk, w="YW")
+    tt(T.YW[:], T.SH[:].indirect(T.PU[:]), T.MS[:], A.mult, r="PU MS " + shk, w="YW")
     dma("oyw", T.yw[:], T.YW[:], r="YW")
-    xupdate(4, T.MLR[:, 64:72], 0, 0, 128, "MLR4", "XA XB XD")
-    dma("oyx", T.yx[:, 0:2048], T.X[:, 0:2048], r="XA")
-    v(V.tensor_scalar, T.CL[:, 0:8], T.MLR[:, 72:80], -2048, None, A.add, r="MLR4", w="CL")
-    xupdate(4, T.CL[:, 0:8], 2048, 128, 256, "CL", "XB XD")
-    dma("oyx", T.yx[:, 2048:4096], T.X[:, 2048:4096], r="XB")
-    act(T.YN[:], T.PG[0:8, 0:256], r="pN", w="YN", b="PG0")
-    act(T.YS[:], T.PG[0:8, 1024:1280], r="pS", w="YS", b="PG2")
-    dma("oyn", T.yn[:], T.YN[:], r="YN")
-    dma("oyn", T.ys[:], T.YS[:], r="YS")
+    cp(T.FO[:, 8:24], T.SI[:], r="SI", w="FOs")
+    cp(T.FO[:, 24:40], T.NP[:], r="NP", w="FOn")
+    act(T.ES[:], T.FO[:].indirect(T.SV[:, 16:32]), r="FOz FOs FOn SV16a SV16b", w="ES")
+    for k_ in range(2):
+        mm(B[1][:, 16 * k_:16 * k_ + 16], T.ES[:, 128 * k_:128 * k_ + 128], T.RR[:, 32:48], True, True, "ES RR1", "B1")
+    act(T.YO[:], B[1][:, 0:32], w="YO", b="B1")
+    dma("oyn", T.ys[:], T.YO[:, 0:16], r="YO", q="a")
+    dma("oyn", T.yn[:], T.YO[:, 16:32], r="YO", q="a")
+    columns(TV - 1, "BL")
+    for k_ in range(NQ):
+        c, e, xs = 4096 // NQ * k_, 256 // NQ * k_, range(4 // NQ * k_, 4)
+        xupdate(TV - 1, c, e, e + 256 // NQ, " ".join("X%d" % i for i in xs) + " XD XE")
+        dma("oyx", T.yx[:, c:c + 4096 // NQ], T.X[:, c:c + 4096 // NQ], r=" ".join("X%d" % i for i in xs[:4 // NQ]))
     for sem, n in tot.items():
         if known["g"].get(sem, 0) < n:
             g.wait_ge(T.sem[sem], n)

@@ -1,4 +1,4 @@
-from concourse.mybir import AluOpType as A, AxisListType, ActivationFunctionType as F
+from concourse.mybir import AluOpType as A, ActivationFunctionType as F
 
 HS = (8, 5, 3, 2, 1)
 BASE = {8: 1, 5: 9, 3: 14, 2: 17, 1: 19}
@@ -6,28 +6,28 @@ NPL, HALF = 21, 168
 TV = 5
 EMPTY = 4097
 ZW, WW = 272, 296
-MAXED = [(8, 0), (8, 1)] + [(h, j) for h in (5, 3, 2, 1) for j in range(h)]
+MAXED = [(8, 0), (8, 1)] + [(h, j) for h in (5, 3, 2) for j in range(h)]
 NQ = 2
 
-bf, f32, i32, u16 = "bfloat16", "float32", "int32", "uint16"
+bf, f16, f32, i32, u16 = "bfloat16", "float16", "float32", "int32", "uint16"
 SCRATCH = {n: ("sbuf", [p, c], d) for n, p, c, d in [
     ("X", 128, 8192, bf), ("LS", 128, 1024, i32), ("LSN", 128, 1024, i32), ("SH", 128, 2304, f32),
-    ("GL", 128, 2048, bf), ("GH", 128, 2048, bf), ("ZC", 128, 2064, bf), ("ZR", 128, 1024, bf),
-    ("DL", 128, 13 * 256, bf), ("DA", 128, 1536, bf), ("NEG", 128, 256, bf),
+    ("GL", 128, 2048, bf), ("GH", 128, 2048, bf), ("ZC", 128, 2064, bf), ("ZR", 128, 512, bf),
+    ("DL", 128, 12 * 256, bf), ("DA", 128, 1536, bf), ("NEG", 128, 256, bf),
     ("ZS", 128, 5 * ZW, bf), ("ZM", 128, 5 * ZW, bf), ("HS", 128, 5 * 128, u16), ("HM", 128, 5 * 128, u16),
     ("LLS", 128, 5 * 128, u16), ("LLM", 128, 5 * 128, u16), ("WS", 128, 5 * WW, f32), ("WM", 128, 5 * WW, f32),
-    ("WI", 128, 256, i32), ("WN", 128, 256, f32), ("MM", 128, 256, f32), ("MK", 128, 256, bf), ("MS", 128, 256, bf),
-    ("IDB", 128, 128, bf), ("NIB", 128, 128, bf), ("IZ", 128, 128, f32), ("RA", 128, 512, f32), ("RB", 128, 512, bf),
-    ("EXT", 128, 136, f32), ("ONE", 128, 128, bf), ("THL", 128, 128, bf), ("LQ", 128, 128, bf), ("ZER", 32, 128, bf),
-    ("CQ", 128, 368, bf), ("DB", 128, 336, bf), ("D0", 128, 336, bf), ("M1", 128, 336, bf), ("CP", 128, 176, bf),
+    ("WI", 128, 256, i32), ("WN", 128, 256, f16), ("MM", 128, 256, f32), ("MK", 128, 256, bf), ("MS", 128, 256, bf),
+    ("IDX", 128, 144, bf), ("NIB", 128, 128, bf), ("IZ", 128, 128, bf), ("RA", 128, 512, bf),
+    ("EXT", 128, 136, f32), ("ONE", 128, 128, bf), ("THL", 128, 128, bf), ("ZER", 32, 128, bf),
+    ("CQ", 128, HALF, bf), ("DB", 128, 336, bf), ("D0", 128, HALF, bf), ("M1", 128, HALF, bf), ("CP", 128, 176, bf),
     ("S1", 128, 336, bf), ("U", 128, 344, f32), ("E", 128, 144, f32), ("ES", 128, 256, f32), ("RR", 128, 48, f32),
     ("ZROW", 128, 32, bf), ("MT", 128, 32, bf), ("M01", 128, 32, bf),
     ("KF", 128, 16, f32), ("KB", 128, 8, bf), ("KN", 128, 8, bf), ("K2", 128, 8, bf), ("WP", 128, 8, bf), ("WQ", 128, 8, bf),
-    ("II", 128, 128, i32), ("IG", 128, 16, i32), ("IP", 128, 4, i32), ("IQ", 128, 4, i32), ("IU", 128, 32, i32), ("I9", 128, 10, i32),
+    ("II", 128, 144, i32), ("IG", 128, 16, i32), ("IP", 128, 4, i32), ("IQ", 128, 4, i32), ("IU", 128, 32, i32), ("I9", 128, 10, i32),
     ("IS", 128, 16, i32), ("IT", 128, 16, i32), ("IA", 128, 16, i32), ("IL", 128, 16, i32), ("COL", 128, 16, f32),
     ("POS", 128, 16, i32), ("POSU", 128, 16, u16), ("BA", 128, 16, f32), ("BS", 128, 16, i32), ("BL", 128, 16, f32),
     ("CV", 128, 10, u16), ("SV", 128, 32, u16),
-    ("SI", 128, 16, i32), ("NP", 128, 16, i32), ("THI", 128, 1, i32), ("WTI", 128, 1, i32), ("WTF", 128, 1, f32),
+    ("SI", 128, 16, i32), ("NP", 128, 16, i32), ("THI", 128, 1, i32), ("WTI", 128, 1, i32),
     ("ZO", 128, 16, u16), ("UI", 128, 16, i32), ("FI", 128, 16, i32), ("UR", 128, 16, i32), ("H", 128, 16, i32), ("HB", 128, 16, i32),
     ("PL", 128, 16, i32), ("PU", 128, 16, u16), ("NU", 128, 16, u16), ("NH", 128, 16, bf), ("A5", 128, 16, f32), ("SUM", 128, 16, i32),
     ("S15", 128, 16, i32), ("SU", 128, 16, u16), ("T1", 128, 16, i32), ("T2", 128, 16, i32), ("U7", 128, 16, i32), ("CU", 128, 16, u16),
@@ -50,7 +50,6 @@ def rank_program(g, core, T, topo):
     V, P, S = g.vector, g.tensor, g.scalar
     Q = {"v": V, "a": S, "p": P, "g": g, "s": g.sync}
     B = [T["B%d" % b] for b in range(8)]
-    PD, PC = B[6], B[7]
 
     tot = {}
     known = {q: {} for q in Q}
@@ -141,6 +140,9 @@ def rank_program(g, core, T, topo):
         lastw[key] = [len(ops)]
         ops.append(("r" + name, n, {}, False))
 
+    def iota(out, pat, base, cm, key, r=""):
+        run("g", g.iota, out, pat, base, cm, w=key, r=r, allow_small_or_imprecise_dtypes=True)
+
     for t in range(TV):
         arrive("Z%d" % t, prv, "ZM%d" % t)
         if t > 0:
@@ -158,45 +160,8 @@ def rank_program(g, core, T, topo):
     dma("ls", T.LS[:], T.ls[:], w="LS")
     dma("x", T.X[:, 0:4096], T.x[:], w="X0 X1 X2 X3")
     XK = "X0 X1 X2 X3 XD XE"
-
-    def iota(out, pat, base, cm, key, r=""):
-        run("g", g.iota, out, pat, base, cm, w=key, r=r, allow_small_or_imprecise_dtypes=True)
-    iota(T.IP[:], [[0, 4]], 0, 1, "IP")
-    iota(T.IS[:], [[1, 16]], 0, 16, "IS")
-    iota(T.IU[:], [[1, 32]], 0, 0, "IU")
-    iota(T.II[:], [[-1, 128]], 0, 1, "II")
-    iota(T.IG[:, 1:9], [[-16, 8]], 0, 1, "IGa")
-    iota(T.IG[:, 0:1], [[1, 1]], -112, 1, "IGb")
-    v(V.memset, T.M1[:], -1.0, w="M1")
-    run("g", g.affine_select, T.DB[:], T.M1[:], [[0, 2], [-16, 8], [0, NPL]], A.is_equal, 0.0, 0, 1, r="M1", w="DB")
-    iota(T.I9[:, 1:9], [[NPL, 8]], 28, 0, "I9a")
-    iota(T.I9[:, 0:10:9], [[0, 2]], 28 + 7 * NPL, 0, "I9b")
-    iota(T.IT[:], [[16, 16]], 0, 256, "IT")
-    iota(T.IA[:], [[256, 16]], 0, 0, "IA")
-    iota(T.IL[:], [[0, NQ], [256, 16 // NQ]], 0, 0, "IL")
-    for buf, c in (("ZR", 1.0), ("CQ", 0.0), ("D0", 1.0), ("LQ", 0.0), ("ONE", 1.0), ("EXT", 0.0), ("CP", 0.0), ("ZER", 0.0)):
-        v(V.memset, T[buf][:], c, w=buf)
-    v(V.memset, T.X[:, 4096:4112], 32.0, w="XE")
-    v(V.memset, T.ZR[:, 0:1024:8], 0.0, w="ZR")
-    v(V.memset, T.LQ[0:1, :], 2.0 ** -5, r="LQ", w="LQa")
-    v(V.memset, T.LQ[32:33, :], 2.0 ** -22, r="LQ", w="LQb")
-    cq = {0: 64, 1: -16, 8: 24, 9: -24, 13: 27, 14: -27, 16: 29, 17: -29, 18: 30, 19: 1, 20: 1}
-    for q_, c in cq.items():
-        v(V.memset, T.CQ[:, q_:336:NPL], float(c), r="CQ", w="CQ%d" % q_)
-    cqk = "LQ LQa LQb CQ " + " ".join("CQ%d" % q_ for q_ in cq)
-    for q_ in (0, 1, 9, 14, 17, 19):
-        v(V.memset, T.D0[:, q_:336:NPL], 0.0, r="D0", w="D0%d" % q_)
-    d0k = "D0 " + " ".join("D0%d" % q_ for q_ in (0, 1, 9, 14, 17, 19))
-    C = {n: T.COL[:, i:i + 1] for i, n in enumerate("p15 s8 n24 zb x16 lo hi sel h168 m0 thx".split())}
-    ts(T.IQ[:, 0:1], T.IP[:, 0:1], 15, A.bitwise_and, r="IP", w="IQ0")
-    ts(T.POS[:], T.IS[:], 255, A.bitwise_and, r="IS", w="POS")
-    cp(C["p15"], T.IQ[:, 0:1], r="IQ0", w="p15")
-    cp(T.POSU[:], T.POS[:], r="POS", w="POSU")
-    ts(C["hi"], T.IQ[:, 0:1], 8, A.is_ge, r="IQ0", w="hi")
-    ts(C["m0"], T.IQ[:, 0:1], 0, A.is_equal, r="IQ0", w="m0")
-    ts(T.MT[:], T.IU[:], C["p15"], A.is_le, 8192, A.mult, r="IU p15", w="MT")
-    ts(T.RR[:, 32:48], T.IU[:, 0:16], C["p15"], A.is_equal, r="IU p15", w="RR1")
-    ts(C["lo"], C["hi"], C["m0"], A.add, 0, A.is_equal, r="hi m0", w="lo")
+    IDB = T.IDX[:, 8:136]
+    C = {n: T.COL[:, i:i + 1] for i, n in enumerate("p15 s8 n24 zb x16 lo hi sel h168 m0 thx q1 q2 bw bl wts".split())}
 
     def slot(u):
         k = "M" if u == 0 else "S"
@@ -209,41 +174,40 @@ def rank_program(g, core, T, topo):
     def rows(b_, bank, last):
         for w_ in range(2):
             c = 128 * (2 * b_ + w_)
-            mm(B[bank][:, 0:128], T.RA[:, c:c + 128], T.WN[:, w_:256:2], w_ == 0, False, "WN RA%d%d" % (b_, w_), "B%d" % bank)
-        for w_ in range(2):
-            c = 128 * (2 * b_ + w_)
-            mm(B[bank][:, 0:128], T.RB[:, c:c + 128], T.MS[:, w_:256:2], False, last and w_ == 1, "MS RB%d%d" % (b_, w_), "B%d" % bank)
+            mm(B[bank][:, 0:128], T.RA[:, c:c + 128], T.WN[:, w_:256:2], w_ == 0, last and w_ == 1, "WN RA%d%d" % (b_, w_), "B%d" % bank)
+
+    def words_in():
+        rows(1, 1, True)
+        rows(0, 2, False)
+        mm(B[3][:, 0:256], T.IZ[:], T.WN[:], True, False, "IZ WN", "B3")
 
     def high_out(u):
-        ts(slot(u)[0], B[1][:, 0:128], EMPTY, A.min, w="H%s%d" % (slot(u)[3], u), b="B1")
+        ts(slot(u)[0], B[1][:, 0:128], 2048, A.add, EMPTY, A.min, w="H%s%d" % (slot(u)[3], u), b="B1")
 
-    def row_of_ls():
-        ts(T.S15[:], T.SI[:], 15, A.bitwise_and, r="SI", w="S15")
+    def row_of_ls(src):
+        ts(T.S15[:], T[src][:], 15, A.bitwise_and, r=src, w="S15")
         tt(T.T1[:], T.SI[:], T.SI[:], A.mult, r="SI", w="T1")
-        ts(T.U7[:], T.NP[:], 77, A.mult, r="NP", w="U7")
         cp(T.SU[:], T.S15[:], r="S15", w="SU")
         act(T.MK[:], T.RR[:, 32:48].indirect(T.SU[:]), r="RR1 SU", w="MK")
 
-    def col_of_ls(between=None):
+    def col_of_ls(u):
         ts(T.T2[:], T.T1[:], 5, A.arith_shift_right, r="T1", w="T2")
         tt(T.U7[:], T.U7[:], T.SI[:], A.add, r="U7 SI", w="U7")
         tt(T.T1[:], T.T2[:], T.U7[:], A.add, r="T2 U7", w="T1")
+        ts(slot(u)[2][:, 264:280], T.SI[:], 5, A.mult, -16, A.add, r="SI", w="Ws%d" % u)
         ts(T.T2[:], T.T1[:], 1023, A.bitwise_and, r="T1", w="T2")
         cp(T.CU[:], T.T2[:], r="T2", w="CU")
 
-    def letters(u, ls):
-        _, lo, wf, k = slot(u)
+    def letters(ls):
         tt(T.MM[:], T[ls][:].indirect(T.CU[:]), T.MK[:], A.mult, r=ls + " CU MK", w="MM")
         for w_ in range(2):
             mm(B[2][:, 0:128], T.EXT[:, 8 - 8 * w_:136 - 8 * w_], T.MM[:, w_:256:2], False, w_ == 1, "MM EXT", "B2")
         mm(B[3][:, 0:256], T.EXT[:, 8:136], T.MM[:], False, True, "MM EXT", "B3")
-        ts(wf[:, 264:280], T.SI[:], 5, A.mult, -16, A.add, r="SI", w="Ws%d" % u)
-        ts(wf[:, 280:296], T.NP[:], 1, A.add, 16, A.min, r="NP", w="Wn%d" % u)
-        ts(lo, B[2][:, 0:128], EMPTY, A.min, w="L%s%d" % (k, u), b="B2")
-        act(wf[:, 0:256], B[3][:, 0:256], w="Ww%d" % u, b="B3")
 
-    def words_in():
-        mm(B[3][:, 0:256], T.IZ[:], T.WN[:], True, False, "IZ WN", "B3")
+    def low_out(u):
+        _, lo, wf, k = slot(u)
+        ts(lo, B[2][:, 0:128], C["bl"], A.add, EMPTY, A.min, r="bl", w="L%s%d" % (k, u), b="B2")
+        act(wf[:, 0:256], B[3][:, 0:256], F.Identity, bias=C["bw"], r="bw", w="Ww%d" % u, b="B3")
 
     def wkey(u):
         return "WM%d" % u if u else "Ww0 Ws0 Wn0 Wz"
@@ -260,83 +224,119 @@ def rank_program(g, core, T, topo):
                 dma("sh", T.SH[0:128 - h, c:c + 256], T.WM[h:128, lo:lo + 256], r=wk, w="SA%d SB%d" % (h, h))
     shk = "SH4 SH6 " + " ".join("SA%d SB%d" % (h, h) for h in (8, 5, 3, 2, 1, 0))
 
-    lengths()
-    row_of_ls()
+    iota(T.IP[:], [[0, 4]], 0, 1, "IP")
+    iota(T.IS[:], [[1, 16]], 0, 16, "IS")
+    iota(T.IU[:], [[1, 32]], 0, 0, "IU")
+    iota(T.II[:], [[-1, 144]], 8, 1, "II")
+    iota(T.IG[:, 1:9], [[-16, 8]], 0, 1, "IGa")
+    iota(T.IG[:, 0:1], [[1, 1]], -112, 1, "IGb")
+    for buf, c in (("M1", -1.0), ("CQ", 0.0), ("ZR", 1.0), ("ONE", 1.0), ("EXT", 0.0), ("CP", 0.0), ("ZER", 0.0), ("D0", 1.0)):
+        v(V.memset, T[buf][:], c, w=buf)
+    run("g", g.affine_select, T.DB[:, 0:HALF], T.M1[:], [[-16, 8], [0, NPL]], A.is_equal, 0.0, 0, 1, r="M1", w="DB")
+    cq = {0: 64, 1: -16, 8: 24, 9: -24, 13: 27, 14: -27, 16: 29, 17: -29, 18: 30, 19: 1, 20: 1}
+    for q_, c in cq.items():
+        iota(T.CQ[:, q_:HALF:NPL], [[0, 8]], c, 0, "CQ%d" % q_, r="CQ")
+    cqk = "CQ " + " ".join("CQ%d" % q_ for q_ in cq)
+    v(V.memset, T.X[:, 4096:4112], 32.0, w="XE")
+    v(V.memset, T.ZR[:, 0:512:8], 0.0, w="ZR")
+    ts(T.IQ[:, 0:1], T.IP[:, 0:1], 15, A.bitwise_and, r="IP", w="IQ0")
+    ts(T.POS[:], T.IS[:], 255, A.bitwise_and, r="IS", w="POS")
+    cp(C["p15"], T.IQ[:, 0:1], r="IQ0", w="p15")
+    cp(T.POSU[:], T.POS[:], r="POS", w="POSU")
+    ts(C["hi"], T.IQ[:, 0:1], 8, A.is_ge, r="IQ0", w="hi")
+    ts(T.M01[:], T.IU[:], C["p15"], A.is_gt, r="IU p15", w="M01")
+    ts(C["m0"], T.IQ[:, 0:1], 0, A.is_equal, r="IQ0", w="m0")
+    ts(T.MT[:], T.M01[:], -8192, A.mult, 6144, A.add, r="M01", w="MT")
+    ts(T.RR[:, 32:48], T.IU[:, 0:16], C["p15"], A.is_equal, r="IU p15", w="RR1")
+    ts(C["lo"], C["hi"], C["m0"], A.add, 0, A.is_equal, r="hi m0", w="lo")
+    ts(T.IDX[:], T.II[:], 0, A.is_equal, r="II", w="IDX")
+    ts(C["zb"], C["m0"], -1, A.mult, 1, A.add, r="m0", w="zb")
+    ts(T.IG[:, 0:9], T.IG[:, 0:9], 4, A.arith_shift_right, r="IGa IGb", w="IG")
+    ts(T.IQ[:, 2:3], T.IP[:, 0:1], 7, A.bitwise_and, r="IP", w="IQ2")
+    ts(T.KF[:, 0:9], T.IG[:, 0:9], 0, A.is_equal, r="IG", w="KF")
     for b_ in (1, 0):
         for w_ in range(2):
-            c = 128 * (2 * b_ + w_)
-            ts(T.RA[:, c:c + 128], T.II[:], 8 * (b_ - w_), A.is_equal, C["hi" if b_ else "lo"], A.mult, r="II hi lo", w="RA%d%d" % (b_, w_))
-            act(T.RB[:, c:c + 128], T.RA[:, c:c + 128], r="RA%d%d" % (b_, w_), w="RB%d%d" % (b_, w_))
-        if b_:
-            cp(T.WN[:], T.WI[:].indirect(T.POSU[:]), r="WIa WIb POSU", w="WN")
-            col_of_ls()
-            rows(1, 1, True)
-    ts(T.IG[:, 0:9], T.IG[:, 0:9], 4, A.arith_shift_right, r="IGa IGb", w="IG")
-    ts(T.KF[:, 0:9], T.IG[:, 0:9], 0, A.is_equal, r="IG", w="KF")
-    ts(C["zb"], C["m0"], -1, A.mult, 1, A.add, r="m0", w="zb")
+            c, o = 128 * (2 * b_ + w_), 8 + 8 * (b_ - w_)
+            act(T.RA[:, c:c + 128], T.IDX[:, o:o + 128], scale=C["hi" if b_ else "lo"], r="IDX hi lo", w="RA%d%d" % (b_, w_))
+    lengths()
+    row_of_ls("SI")
+    ts(T.U7[:], T.NP[:], 77, A.mult, r="NP", w="U7")
+    act(T.IZ[:], IDB, scale=C["zb"], r="IDX zb", w="IZ")
+    ts(C["bw"], C["zb"], 2048, A.mult, r="zb", w="bw")
+    ts(C["bl"], T.IQ[:, 2:3], 0, A.is_gt, 2048, A.mult, r="IQ2", w="bl")
     cp(T.EXT[:, 8:136:16], T.KF[:, 1:9], r="KF", w="EXT")
-    ts(T.IZ[:], T.II[:], 0, A.is_equal, C["zb"], A.mult, r="II zb", w="IZ")
-    rows(0, 2, False)
+    col_of_ls(0)
+    tt(T.WN[:], T.WI[:].indirect(T.POSU[:]), T.MS[:], A.add, r="WIa WIb POSU MS", w="WN")
     words_in()
-    high_out(0)
     send("LS", prv, T.LSN[:], T.LS[:], r="LS")
-    ts(T.IDB[:], T.II[:], 0, A.is_equal, r="II", w="IDB")
-    cp(C["thx"], T.THI[:], r="THI", w="thx")
-    cp(T.WTF[:], T.WTI[:], r="WTI", w="WTF")
-    tt(C["thx"], C["thx"], C["zb"], A.add, r="thx zb", w="thx")
     act(T.KN[:], T.KF[:, 1:9], scale=-1.0, r="KF", w="KN")
-    act(T.NIB[:], T.IDB[:], scale=-1.0, r="IDB", w="NIB")
+    act(T.NIB[:], IDB, scale=-1.0, r="IDX", w="NIB")
+    ts(T.WM[:, 280:296], T.NP[:], 1, A.add, 16, A.min, r="NP", w="Wn0")
+    ts(C["q1"], T.IP[:, 0:1], 1, A.is_equal, 2.0 ** -5, A.mult, r="IP", w="q1")
+    ts(C["q2"], T.IP[:, 0:1], 2, A.is_equal, 2.0 ** -22, A.mult, r="IP", w="q2")
+    ts(C["wts"], T.WTI[:], 2.0 ** -22, A.mult, r="WTI", w="wts")
+    ts(C["thx"], T.THI[:], C["q1"], A.add, C["q2"], A.add, r="THI q1 q2", w="thx")
+    ts(C["q1"], C["q1"], C["q2"], A.add, 0, A.is_gt, r="q1 q2", w="q1")
+    high_out(0)
+    letters("LS")
+    act(T.THL[:], T.ONE[:], scale=C["thx"], r="ONE thx", w="THL")
+    act(T.DB[:, HALF:336], T.CQ[:], scale=C["q1"], r="q1 " + cqk, w="DBc")
     act(T.K2[:], T.KF[:, 1:9], scale=2.0, r="KF", w="K2")
     act(T.KB[:], T.KF[:, 1:9], r="KF", w="KB")
-    act(T.THL[:], T.ONE[:], scale=C["thx"], r="ONE thx", w="THL")
-    ts(T.WP[:], T.KF[:, 1:9], T.WTF[:], A.mult, 2.0 ** -22, A.mult, r="KF WTF", w="WP")
-    ts(T.WQ[:], T.KF[:, 1:9], T.WTF[:], A.mult, -2.0 ** -22, A.mult, r="KF WTF", w="WQ")
-    v(V.memset, T.DB[:, 0:336:NPL], 0.0, r="DB", w="DBa")
-    v(V.memset, T.DB[:, 20:336:NPL], 64.0, r="DB", w="DBb")
+    act(T.WP[:], T.KF[:, 1:9], scale=C["wts"], r="KF wts", w="WP")
+    act(T.WQ[:], T.WP[:], scale=-1.0, r="WP", w="WQ")
+    v(V.memset, T.DB[:, 0:HALF:NPL], 0.0, r="DB", w="DBa")
+    v(V.memset, T.DB[:, 20:HALF:NPL], 32768.0, r="DB", w="DBb")
     for h in HS:
         cp(T.CP[:, 1 + BASE[h]:169:NPL], T.KN[:], r="KN CP", w="CP%d" % h)
     cpk = "CP " + " ".join("CP%d" % h for h in HS)
-    letters(0, "LS")
+    low_out(0)
     build_sh(0)
+    iota(T.I9[:, 1:9], [[NPL, 8]], 28, 0, "I9a")
+    iota(T.I9[:, 0:10:9], [[0, 2]], 28 + 7 * NPL, 0, "I9b")
     iota(T.WM[:, 256:264], [[0, 8]], 0, 0, "Wz")
+    for q_ in (0, 1, 9, 14, 17, 19):
+        iota(T.D0[:, q_:HALF:NPL], [[0, 8]], 0, 0, "D0%d" % q_, r="D0")
+    d0k = "D0 " + " ".join("D0%d" % q_ for q_ in (0, 1, 9, 14, 17, 19))
     iota(T.ZROW[0:32, 0:16], [[0, 16]], 0, 0, "ZROW")
     iota(T.ZROW[0:32, 16:32], [[8, 16]], 0, 0, "ZROWb")
     iota(T.U[:, 0:8], [[0, 8]], 0, 0, "Uz")
     iota(T.ZC[:, 2048:2064], [[0, 16]], 0, 0, "ZCz")
+    iota(T.IT[:], [[16, 16]], 0, 256, "IT")
+    iota(T.IA[:], [[256, 16]], 0, 0, "IA")
+    iota(T.IL[:], [[0, NQ], [256, 16 // NQ]], 0, 0, "IL")
     iota(T.SH[:, 1024:1280], [[0, 256]], 0, 0, "SH4")
     iota(T.SH[:, 1536:2048], [[0, 512]], 0, 0, "SH6")
     iota(T.NEG[:], [[0, 256]], -128, 0, "NEG")
+    iota(T.X[:, 4112:8192:16], [[0, 255]], 0, 0, "XD")
     for u in range(1, TV):
         iota(T.WS[:, WW * u + 256:WW * u + 264], [[0, 8]], 0, 0, "Wz%d" % u)
     iota(T.FO[:, 0:8], [[0, 8]], 0, 0, "FOz")
+    ts(T.IQ[:, 1:2], T.IP[:, 0:1], 4, A.arith_shift_right, r="IP", w="IQ1")
+    ts(C["h168"], C["hi"], HALF, A.mult, r="hi", w="h168")
+    ts(C["s8"], C["p15"], 8, A.add, r="p15", w="s8")
+    ts(C["n24"], C["p15"], 24, A.add, r="p15", w="n24")
+    tt(C["sel"], T.IQ[:, 1:2], T.IQ[:, 2:3], A.is_equal, r="IQ1 IQ2", w="sel")
+    for o, lo in ((0, 0), (16, 1)):
+        ts(T.SV[:, o:o + 8], T.KF[:, lo:lo + 8], C["s8"], A.mult, r="KF s8", w="SV%da" % o)
+        ts(T.SV[:, o + 8:o + 16], T.KF[:, lo:lo + 8], C["n24"], A.mult, r="KF n24", w="SV%db" % o)
 
     def late_consts():
-        ts(T.IQ[:, 1:2], T.IP[:, 0:1], 4, A.arith_shift_right, r="IP", w="IQ1")
-        ts(T.IQ[:, 2:3], T.IP[:, 0:1], 7, A.bitwise_and, r="IP", w="IQ2")
-        ts(C["h168"], C["hi"], HALF, A.mult, r="hi", w="h168")
-        tt(C["sel"], T.IQ[:, 1:2], T.IQ[:, 2:3], A.is_equal, r="IQ1 IQ2", w="sel")
-        ts(C["s8"], C["p15"], 8, A.add, r="p15", w="s8")
-        ts(C["n24"], C["p15"], 24, A.add, r="p15", w="n24")
+        act(T.RR[:, 0:16], T.RR[:, 32:48], scale=2.0 ** 22, r="RR1", w="RR2")
+        act(T.RR[:, 16:32], T.RR[:, 32:48], scale=32.0, r="RR1", w="RR3")
+        act(C["zb"], C["p15"], F.Identity, scale=128.0, bias=-1.0, r="p15", w="zb")
+        act(C["x16"], C["p15"], scale=16.0, r="p15", w="x16")
         ts(T.CV[:], T.I9[:], C["h168"], A.add, C["sel"], A.mult, r="I9a I9b h168 sel", w="CV")
-        for o, lo in ((0, 0), (16, 1)):
-            ts(T.SV[:, o:o + 8], T.KF[:, lo:lo + 8], C["s8"], A.mult, r="KF s8", w="SV%da" % o)
-            ts(T.SV[:, o + 8:o + 16], T.KF[:, lo:lo + 8], C["n24"], A.mult, r="KF n24", w="SV%db" % o)
-        ts(T.RR[:, 0:16], T.RR[:, 32:48], 2.0 ** 22, A.mult, r="RR1", w="RR2")
-        ts(T.RR[:, 16:32], T.RR[:, 32:48], 32.0, A.mult, r="RR1", w="RR3")
-        ts(C["x16"], C["p15"], 16, A.mult, r="p15", w="x16")
-        ts(C["zb"], C["p15"], 128, A.mult, -1, A.add, r="p15", w="zb")
+
+    def last_consts():
         ts(T.BS[:], T.IT[:], 4095, A.bitwise_and, r="IT", w="BS")
         ts(T.BA[:], T.IA[:], C["x16"], A.add, r="IA x16", w="BA")
         ts(T.BL[:], T.IL[:], C["x16"], A.add, r="IL x16", w="BL")
-        ts(T.M01[:], T.IU[:], C["p15"], A.is_gt, r="IU p15", w="M01")
 
-    def spare_columns():
-        act(T.X[:, 4112:5120], T.ZR[:, 0:1008], scale=0.0, r="ZR", w="XD")
-        for c in (5120, 6144, 7168):
-            act(T.X[:, c:c + 1024], T.ZR[:], scale=0.0, r="ZR", w="XD")
+    PD, PC = 0, HALF
 
-    def place(bank, hf, q_):
-        return bank[:, HALF * hf + q_:HALF * hf + HALF:NPL]
+    def place(o, hf, q_):
+        return B[6 + hf][:, o + q_:o + HALF:NPL]
 
     def row(buf, hf, j):
         return buf[:, 1024 * hf + j:1024 * hf + 1024:8]
@@ -356,33 +356,39 @@ def rank_program(g, core, T, topo):
                 cp(buf[:, c:c + n], win.indirect(lst[:, c // 16:(c + n) // 16]), r=xk + lk, w=key)
             else:
                 act(buf[:, c:c + n], win.indirect(lst[:, c // 16:(c + n) // 16]), r=xk + lk, w=key)
-        gather("v", T.GH, Hl, 0, 1024, "GH0", "HM%d" % t)
-        gather("a", T.GH, Hl, 1024, 1024, "GH1", "HM%d" % t)
+        for hf in range(2):
+            gather("v", T.GH, Hl, 1024 * hf, 512, "GH%da" % hf, "HM%d" % t)
+            gather("a", T.GH, Hl, 1024 * hf + 512, 512, "GH%db" % hf, "HM%d" % t)
         gather("v", T.GL, Ll, 0, 512, "GL0a", "LM%d" % t)
         gather("a", T.GL, Ll, 512, 512, "GL0b", "LM%d" % t)
         gather("a", T.GL, Ll, 1024, 1024, "GL1", "LM%d" % t)
         gl = ("GL0a GL0b", "GL1")
-        mm(PD[:, 0:336], T.THL[:], T.DB[:], True, False, "THL DB DBa DBb", "B6")
-        mm(PC[:, 0:368], T.LQ[0:64, :], T.CQ[0:64, :], True, False, cqk, "B7")
+        gh = ("GH0a GH0b", "GH1a GH1b")
         for bk in (1, 2, 3):
-            mm(B[bk][:, 0:512], T.ZER[0:1, :], T.ZR[0:1, 0:512], True, False, "ZER ZR", "B%d" % bk)
+            mm(B[bk][:, 0:512], T.ZER[0:1, :], T.ZR[0:1, :], True, False, "ZER ZR", "B%d" % bk)
+        for hf in range(2):
+            mm(B[6 + hf][:, 0:336], T.THL[:], T.DB[:], True, False, "THL DB DBa DBb DBc", "B%d" % (6 + hf))
 
         def highs(hf):
             for j in range(2):
-                mm(B[0][:, 256 * hf + 128 * j:256 * hf + 128 * j + 128], T.IDB[:], row(T.GH, hf, j), True, True, "IDB GH%d" % hf, "B0")
+                mm(B[0][:, 256 * hf + 128 * j:256 * hf + 128 * j + 128], IDB, row(T.GH, hf, j), True, True, "IDX " + gh[hf], "B0")
 
         def highd(hf):
             for j in range(2, 8):
                 bk, c = diff_at(hf, j)
-                mm(B[bk][:, c:c + 128], T.IDB[:], row(T.GH, hf, j), False, False, "IDB GH%d" % hf, "B%d" % bk)
+                mm(B[bk][:, c:c + 128], IDB, row(T.GH, hf, j), False, False, "IDX " + gh[hf], "B%d" % bk)
 
         def sums(hf, buf, j, places, key):
             for q_ in places:
-                mm(place(PD, hf, q_), row(buf, hf, j), T.KN[:], False, False, key + " KN", "B6")
+                mm(place(PD, hf, q_), row(buf, hf, j), T.KN[:], False, False, key + " KN", "B%d" % (6 + hf))
+
+        def highsums(hf):
+            sums(hf, T.GH, 0, (BASE[8], BASE[5] + 3), gh[hf])
+            sums(hf, T.GH, 1, (BASE[8] + 1, BASE[5] + 4), gh[hf])
 
         def lows(hf):
             for j in range(3):
-                mm(B[4 + hf][:, 128 * j:128 * j + 128], T.IDB[:], row(T.GL, hf, j), True, True, "IDB " + gl[hf], "B%d" % (4 + hf))
+                mm(B[4 + hf][:, 128 * j:128 * j + 128], IDB, row(T.GL, hf, j), True, True, "IDX " + gl[hf], "B%d" % (4 + hf))
 
         def lowd(hf):
             for j in range(2, 8):
@@ -390,21 +396,24 @@ def rank_program(g, core, T, topo):
                 mm(B[bk][:, c:c + 128], T.NIB[:], row(T.GL, hf, j), False, j == 5 or (hf, j) == (1, 7), "NIB " + gl[hf], "B%d" % bk)
 
         def lowsums(hf):
-            o = PD[:, HALF * hf:HALF * hf + HALF]
-            mm(o, row(T.GL, hf, 0), T.CP[:, 1:169], False, False, gl[hf] + " " + cpk, "B6")
-            mm(o, row(T.GL, hf, 1), T.CP[:, 0:168], False, False, gl[hf] + " " + cpk, "B6")
+            o = B[6 + hf][:, 0:HALF]
+            mm(o, row(T.GL, hf, 0), T.CP[:, 1:169], False, False, gl[hf] + " " + cpk, "B%d" % (6 + hf))
+            mm(o, row(T.GL, hf, 1), T.CP[:, 0:168], False, False, gl[hf] + " " + cpk, "B%d" % (6 + hf))
             for j in range(1, 8):
                 pl = [BASE[h] + j - h for h in (5, 3, 2, 1) if 0 <= j - h < h] + [BASE[h] + j for h in (5, 3) if 1 < j < h]
                 sums(hf, T.GL, j, pl, gl[hf])
 
         def zc(hf):
-            v(V.tensor_tensor_scan, T.ZC[:, 1024 * hf:1024 * hf + 1024], T.ZR[:], T.GL[:, 1024 * hf:1024 * hf + 1024], 0.0, A.mult, A.max,
-              r="ZR " + gl[hf], w="ZC%d" % hf)
+            for k_ in range(2):
+                c = 1024 * hf + 512 * k_
+                v(V.tensor_tensor_scan, T.ZC[:, c:c + 512], T.ZR[:], T.GL[:, c:c + 512], 0.0, A.mult, A.max,
+                  r="ZR " + (gl[0].split()[k_] if hf == 0 else gl[1]), w="ZC%d%d" % (hf, k_))
 
-        def seeds(hf, last=False):
-            l = [(h, BASE[h] + h - 1, "WQ") for h in HS] + [(h, BASE[h] + h, "WP") for h in HS] + [(1, 1, "WP")]
-            for i, (h, q_, wk) in enumerate(l):
-                mm(place(PC, hf, q_), row(T.ZC, hf, h - 1), T[wk][:], False, last and i == len(l) - 1, "ZC%d %s" % (hf, wk), "B7")
+        def seeds(hf):
+            zk, bk = "ZC%d0 ZC%d1 " % (hf, hf), "B%d" % (6 + hf)
+            mm(place(PD, hf, BASE[1]), row(T.ZC, hf, 1), T.K2[:], False, False, zk + "K2", bk)
+            for h, q_, wk in [(h, BASE[h] + h - 1, "WQ") for h in HS] + [(h, BASE[h] + h, "WP") for h in HS] + [(1, 1, "WP")]:
+                mm(place(PC, hf, q_), row(T.ZC, hf, h - 1), T[wk][:], False, False, zk + wk, bk)
 
         def pair(hf, h, j):
             c = 256 * MAXED.index((h, j)) + 128 * hf
@@ -417,91 +426,94 @@ def rank_program(g, core, T, topo):
 
         def add(hf, h, j, last=False):
             c = 256 * MAXED.index((h, j)) + 128 * hf
-            mm(place(PD, hf, BASE[h] + j), T.DL[:, c:c + 128], T.K2[:], False, last, "K2 DL%d%d%d" % (hf, h, j), "B6")
+            mm(place(PD, hf, BASE[h] + j), T.DL[:, c:c + 128], T.K2[:], False, last, "K2 DL%d%d%d" % (hf, h, j), "B%d" % (6 + hf))
 
         def sizes(bk):
             act(T.DA[:, 512 * (bk - 1):512 * bk], B[bk][:, 0:512], F.Abs, w="DA%d" % bk, b="B%d" % bk)
 
-        def add_sizes(bk):
-            for hf in range(2):
+        def add_sizes(bk, last=False):
+            for hf in (1, 0):
                 for j in range(2, 8):
                     b_, c = diff_at(hf, j)
                     if b_ == bk:
                         c += 512 * (bk - 1)
-                        mm(place(PD, hf, BASE[8] + j), T.DA[:, c:c + 128], T.KB[:], False, False, "KB DA%d" % bk, "B6")
+                        mm(place(PD, hf, BASE[8] + j), T.DA[:, c:c + 128], T.KB[:], False, last and (hf, j) == (0, 7), "KB DA%d" % bk, "B%d" % (6 + hf))
 
         up = [p_ for p_ in MAXED if sum(p_) >= 8]
         dn = [p_ for p_ in MAXED if sum(p_) < 8]
         highs(0)
-        highs(1)
         highd(0)
-        lows(0)
+        highs(1)
         highd(1)
+        lows(0)
         lowd(0)
-        for hf in range(2):
-            sums(hf, T.GH, 0, (BASE[8], BASE[5] + 3), "GH%d" % hf)
-            sums(hf, T.GH, 1, (BASE[8] + 1, BASE[5] + 4), "GH%d" % hf)
         sizes(1)
         zc(0)
         for p_ in up + dn:
             pair(0, *p_)
+        highsums(0)
+        highsums(1)
+        lowsums(0)
         lows(1)
         lowd(1)
-        sizes(3)
         sizes(2)
-        lowsums(0)
+        sizes(3)
         seeds(0)
         for p_ in up + dn:
             add(0, *p_)
         zc(1)
         lowsums(1)
         add_sizes(1)
+        seeds(1)
+        add_sizes(2, True)
         o = 16 if t == TV - 1 else 0
         act(T.ES[:], T.WM[:, WW * t + 256:WW * t + WW].indirect(T.SV[:, o:o + 16]), r=wkey(t) + " SV%da SV%db" % (o, o), w="ES")
-        seeds(1)
-        add_sizes(3)
-        add_sizes(2)
-        for i, p_ in enumerate(up + dn):
+        for p_ in up + dn:
             pair(1, *p_)
         for i, p_ in enumerate(up + dn):
+            if i == 6:
+                add_sizes(3)
             add(1, *p_, last=i == len(MAXED) - 1)
-            if i == 5:
-                for k_ in range(2):
-                    mm(PC[:, 336 + 16 * k_:352 + 16 * k_], T.ES[:, 128 * k_:128 * k_ + 128], T.RR[:, 32:48], False, k_ == 1, "ES RR1", "B7")
+        for k_ in range(2):
+            mm(B[5][:, 16 * k_:16 * k_ + 16], T.ES[:, 128 * k_:128 * k_ + 128], T.RR[:, 32:48], True, True, "ES RR1", "B5")
 
     def decode(t):
         last = t == TV - 1
+        u = t + 1
         z = T.ZS[:, ZW * t:ZW * t + ZW]
-        v(V.tensor_tensor_scan, T.S1[:], T.D0[:], PD[:, 0:336], 0.0, A.mult, A.max, r=d0k, w="S1", b="B6")
         mm(B[0][:, 0:32], T.ONE[0:1, :], T.ZROW[0:1, :], True, False, "ONE ZROW ZROWb", "B0")
-        v(V.tensor_tensor_scan, T.U[:, 8:344], PC[:, 0:336], T.S1[:], 0.0, A.add, A.min, r="S1", w="U", b="B7")
-        cp(T.E[:], T.U[:].indirect(T.CV[:, 0:9]), r="U Uz CV", w="E")
+        for hf in range(2):
+            c, bk = HALF * hf, "B%d" % (6 + hf)
+            v(V.tensor_tensor_scan, T.S1[:, c:c + HALF], T.D0[:], B[6 + hf][:, 0:HALF], 0.0, A.mult, A.max, r=d0k, w="S1%d" % hf, b=bk)
+            v(V.tensor_tensor_scan, T.U[:, 8 + c:8 + c + HALF], B[6 + hf][:, HALF:336], T.S1[:, c:c + HALF], 0.0, A.add, A.min, r="S1%d" % hf, w="U%d" % hf, b=bk)
+        cp(T.E[:], T.U[:].indirect(T.CV[:, 0:9]), r="U0 U1 Uz CV", w="E")
         mm(B[0][:, 0:32], T.E[:, 16:144], T.RR[:, 0:32], False, True, "E RR2 RR3", "B0")
         o = 16 if last else 0
         mm(B[4][:, 0:16], T.E[:, o:o + 128], T.RR[:, 0:16], True, True, "E RR2", "B4")
         ts(T.ZO[:], B[0][:, 16:32], C["zb"], A.add, r="zb", w="ZO", b="B0")
         cp(T.UI[:], B[0][:, 0:16], w="UI", b="B0")
-        act(z[:, 0:256], T.ZC[:].indirect(T.ZO[:]), r="ZC0 ZC1 ZCz ZO", w="Za")
+        act(z[:, 0:256], T.ZC[:].indirect(T.ZO[:]), r="ZC00 ZC01 ZC10 ZC11 ZCz ZO", w="Za")
         cp(T.UR[:], B[4][:, 0:16], w="UR", b="B4")
         ts(T.FI[:], T.UI[:], (1 << 21) + 15, A.bitwise_and, r="UI", w="FI")
         ts(T.H[:], T.UR[:], 17, A.arith_shift_right, 15, A.bitwise_and, r="UR", w="H")
         ts(z[:, 256:272], T.FI[:], 4096, A.min, r="FI", w="Zb")
         send("Z%d" % t, nxt, T.ZM[:, ZW * t:ZW * t + ZW], z, r="Za Zb")
+        tt(T.NP[:], B[5][:, 16:32], T.H[:], A.subtract, r="H", w="NP", b="B5")
         ts(T.HB[:], T.UR[:], 9, A.arith_shift_right, 0xF00, A.bitwise_and, r="UR", w="HB")
-        tt(T.NP[:], PC[:, 352:368], T.H[:], A.subtract, r="H", w="NP", b="B7")
-        tt(T.PL[:], T.HB[:], T.POS[:], A.add, r="HB POS", w="PL")
         if last:
             cp(T.NU[:], T.NP[:], r="NP", w="NU")
             act(T.MS[:], T.M01[:].indirect(T.NU[:]), r="M01 NU", w="MS")
         else:
             lengths()
-        cp(T.PU[:], T.PL[:], r="PL", w="PU")
-        if not last:
-            act(T.WN[:], T.SH[:].indirect(T.PU[:]), r="PU " + shk, w="WN")
-            rows(1, 1, True)
+        tt(T.PL[:], T.HB[:], T.POS[:], A.add, r="HB POS", w="PL")
         ts(T.NH[:], T.UR[:], 1 << 21, A.is_ge, r="UR", w="NH")
-        tt(T.A5[:], PC[:, 336:352], T.NH[:], A.mult, r="NH", w="A5", b="B7")
+        cp(T.PU[:], T.PL[:], r="PL", w="PU")
+        tt(T.A5[:], B[5][:, 0:16], T.NH[:], A.mult, r="NH", w="A5", b="B5")
+        if not last:
+            ts(T.U7[:], T.NP[:], 77, A.mult, r="NP", w="U7")
         tt(T.SUM[:], T.A5[:], T.UR[:], A.add, r="A5 UR", w="SUM")
+        if not last:
+            ts(slot(u)[2][:, 280:296], T.NP[:], 1, A.add, 16, A.min, r="NP", w="Wn%d" % u)
         ts(T.SI[:], T.SUM[:], 4095, A.bitwise_and, r="SUM", w="SI")
 
     def columns(t, base):
@@ -514,32 +526,34 @@ def rank_program(g, core, T, topo):
         ts(T.XU[:, e0:e1], T.XT[:, e0:e1], 0.5, A.mult, 127.75, A.add, r="XT", w="XU")
         tt(win.indirect(cols), T.XU[:, e0:e1], T.NEG[:, e0:e1], A.add, r="XU NEG CX", w=xk)
 
-    late_consts()
     for t in range(TV):
         bulk(t)
         if t == 0:
-            spare_columns()
+            late_consts()
         decode(t)
         if t == TV - 1:
             break
         u = t + 1
-        row_of_ls()
-        rows(0, 2, False)
-        mm(B[5][:, 0:16], T.ONE[:], T.NH[:], True, True, "ONE NH", "B5")
+        row_of_ls("SUM")
+        mm(B[0][:, 32:48], T.ONE[:], T.NH[:], True, True, "ONE NH", "B0")
+        tt(T.WN[:], T.SH[:].indirect(T.PU[:]), T.MS[:], A.add, r="PU MS " + shk, w="WN")
         words_in()
-        col_of_ls()
+        act(T.NJ[:], B[0][:, 32:48], scale=-1.0, accum_out=T.NS[:], w="NS", b="B0")
+        col_of_ls(u)
         high_out(u)
         send("H%d" % u, nxt, T.HM[:, 128 * u:128 * u + 128], slot(u)[0], r="HS%d" % u)
-        act(T.NJ[:], B[5][:, 0:16], scale=-1.0, accum_out=T.NS[:], w="NS", b="B5")
-        letters(u, "LSN")
+        letters("LSN")
+        cp(T.AI[:], T.NS[:], r="NS", w="AI")
+        if t == 0:
+            last_consts()
+        ts(T.AJ[:], T.AI[:], 15, A.bitwise_and, r="AI", w="AJ")
+        ts(T.BC[:], T.AJ[:], C["m0"], A.mult, C["thx"], A.add, r="AJ m0 thx", w="BC")
+        low_out(u)
+        act(T.THL[:], T.ONE[:], scale=T.BC[:], r="ONE BC", w="THL")
         send("L%d" % u, nxt, T.LLM[:, 128 * u:128 * u + 128], slot(u)[1], r="LS%d" % u)
         send("W%d" % u, nxt, T.WM[:, WW * u:WW * u + WW], slot(u)[2], r="Ww%d Ws%d Wn%d Wz%d" % (u, u, u, u))
         build_sh(u)
-        cp(T.AI[:], T.NS[:], r="NS", w="AI")
         columns(t, "BS" if t % 2 else "BA")
-        ts(T.AJ[:], T.AI[:], 15, A.bitwise_and, r="AI", w="AJ")
-        ts(T.BC[:], T.AJ[:], C["m0"], A.mult, C["thx"], A.add, r="AJ m0 thx", w="BC")
-        act(T.THL[:], T.ONE[:], scale=T.BC[:], r="ONE BC", w="THL")
         xupdate(t, 0, 0, 256, XK)
 
     tt(T.YW[:], T.SH[:].indirect(T.PU[:]), T.MS[:], A.mult, r="PU MS " + shk, w="YW")

@@ -7,31 +7,29 @@ TV = 5
 EMPTY = 4097
 ZW, WW = 272, 296
 MAXED = [(8, 0), (8, 1)] + [(h, j) for h in (5, 3, 2) for j in range(h)]
-NQ = 2
 
 bf, f16, f32, i32, u16 = "bfloat16", "float16", "float32", "int32", "uint16"
 SCRATCH = {n: ("sbuf", [p, c], d) for n, p, c, d in [
-    ("X", 128, 8192, bf), ("LS", 128, 1024, i32), ("LSN", 128, 1024, i32), ("SH", 128, 2304, f32),
+    ("X", 128, 8192, bf), ("LS", 128, 1024, i32), ("LSN", 128, 1024, i32), ("SH", 128, 4352, f32),
     ("GL", 128, 2048, bf), ("GH", 128, 2048, bf), ("ZC", 128, 2064, bf), ("ZR", 128, 512, bf),
     ("DL", 128, 12 * 256, bf), ("DA", 128, 1536, bf), ("NEG", 128, 256, bf),
     ("ZS", 128, 5 * ZW, bf), ("ZM", 128, 5 * ZW, bf), ("HS", 128, 5 * 128, u16), ("HM", 128, 5 * 128, u16),
     ("LLS", 128, 5 * 128, u16), ("LLM", 128, 5 * 128, u16), ("WS", 128, 5 * WW, f32), ("WM", 128, 5 * WW, f32),
     ("WI", 128, 256, i32), ("WN", 128, 256, f16), ("MM", 128, 256, f32), ("MK", 128, 256, bf), ("MS", 128, 256, bf),
     ("IDX", 128, 144, bf), ("NIB", 128, 128, bf), ("IZ", 128, 128, bf), ("RA", 128, 512, bf),
-    ("EXT", 128, 136, f32), ("ONE", 128, 128, bf), ("THL", 128, 128, bf), ("ZER", 32, 128, bf),
+    ("I256", 128, 128, bf), ("J256", 128, 128, bf), ("EXT", 128, 136, f32), ("ONE", 128, 128, bf), ("THL", 128, 128, bf), ("ZER", 128, 128, bf),
     ("CQ", 128, HALF, bf), ("DB", 128, 336, bf), ("D0", 128, HALF, bf), ("M1", 128, HALF, bf), ("CP", 128, 176, bf),
-    ("S1", 128, 336, bf), ("U", 128, 344, f32), ("E", 128, 144, f32), ("ES", 128, 256, f32), ("RR", 128, 48, f32),
-    ("ZROW", 128, 32, bf), ("MT", 128, 32, bf), ("M01", 128, 32, bf),
+    ("S1", 128, 336, bf), ("U", 128, 344, f32), ("E", 128, 144, f32), ("ES", 128, 256, f32), ("RR", 128, 80, f32),
+    ("ZROW", 32, 32, bf), ("POSB", 128, 16, bf), ("NH", 128, 16, bf), ("HB", 128, 16, bf), ("MT", 128, 32, bf), ("M01", 128, 32, f32),
     ("KF", 128, 16, f32), ("KB", 128, 8, bf), ("KN", 128, 8, bf), ("K2", 128, 8, bf), ("WP", 128, 8, bf), ("WQ", 128, 8, bf),
     ("II", 128, 144, i32), ("IG", 128, 16, i32), ("IP", 128, 4, i32), ("IQ", 128, 4, i32), ("IU", 128, 32, i32), ("I9", 128, 10, i32),
-    ("IS", 128, 16, i32), ("IT", 128, 16, i32), ("IA", 128, 16, i32), ("IL", 128, 16, i32), ("COL", 128, 16, f32),
-    ("POS", 128, 16, i32), ("POSU", 128, 16, u16), ("BA", 128, 16, f32), ("BS", 128, 16, i32), ("BL", 128, 16, f32),
-    ("CV", 128, 10, u16), ("SV", 128, 32, u16),
+    ("IS", 128, 16, i32), ("IA", 128, 16, f32), ("IL", 128, 16, f32), ("COL", 128, 24, f32),
+    ("POS", 128, 16, i32), ("POSU", 128, 16, u16), ("BA", 128, 16, bf), ("BS", 128, 16, bf), ("BL", 128, 16, bf),
+    ("CV", 128, 10, u16), ("SV", 128, 32, u16), ("N77", 128, 16, f32), ("ROT", 128, 128, bf), ("M10", 128, 32, f32),
     ("SI", 128, 16, i32), ("NP", 128, 16, i32), ("THI", 128, 1, i32), ("WTI", 128, 1, i32),
-    ("ZO", 128, 16, u16), ("UI", 128, 16, i32), ("FI", 128, 16, i32), ("UR", 128, 16, i32), ("H", 128, 16, i32), ("HB", 128, 16, i32),
-    ("PL", 128, 16, i32), ("PU", 128, 16, u16), ("NU", 128, 16, u16), ("NH", 128, 16, bf), ("A5", 128, 16, f32), ("SUM", 128, 16, i32),
+    ("ZO", 128, 16, u16), ("PU", 128, 16, u16), ("NU", 128, 16, u16), ("A5", 128, 16, f32), ("SUM", 128, 16, i32),
     ("S15", 128, 16, i32), ("SU", 128, 16, u16), ("T1", 128, 16, i32), ("T2", 128, 16, i32), ("U7", 128, 16, i32), ("CU", 128, 16, u16),
-    ("CI", 128, 16, i32), ("CX", 128, 16, u16), ("NS", 128, 1, f32), ("NJ", 128, 16, f32), ("AI", 128, 1, i32), ("AJ", 128, 1, i32), ("BC", 128, 1, f32),
+    ("CX", 128, 16, u16), ("NS", 128, 1, f32), ("NJ", 128, 16, f32), ("AT", 128, 1, bf), ("AR", 128, 1, f32), ("BC", 128, 1, f32),
     ("XT", 128, 256, bf), ("XU", 128, 256, bf), ("YW", 128, 256, f32), ("FO", 128, 40, f32), ("YO", 128, 32, f32),
 ]}
 for _b in range(8):
@@ -153,48 +151,43 @@ def rank_program(g, core, T, topo):
     v(V.memset, T.THI[:], 0, w="THI")
     dma("small", T.SI[:], T.sd[:], w="SI")
     dma("small", T.NP[:], T.nl[:], w="NP")
-    dma("wd", T.WI[1:128, :], T.wd[0:127, :], w="WIa")
-    dma("wd", T.WI[0:1, :], T.wd[0:1, :], w="WIb")
     dma("sm2", T.THI[0:128:16, :], T.th[:], w="THI")
     dma("sm2", T.WTI[:], T.wt[:], w="WTI")
     dma("ls", T.LS[:], T.ls[:], w="LS")
-    dma("x", T.X[:, 0:4096], T.x[:], w="X0 X1 X2 X3")
-    XK = "X0 X1 X2 X3 XD XE"
+    dma("wd", T.WI[1:128, :], T.wd[0:127, :], w="WIa")
+    dma("wd", T.WI[0:1, :], T.wd[0:1, :], w="WIb")
+    dma("x", T.X[:, 0:4096], T.x[:], w="X0 X1")
+    XK = "X0 X1 XD XE"
     IDB = T.IDX[:, 8:136]
-    C = {n: T.COL[:, i:i + 1] for i, n in enumerate("p15 s8 n24 zb x16 lo hi sel h168 m0 thx q1 q2 bw bl wts".split())}
+    C = {n: T.COL[:, i:i + 1] for i, n in enumerate("p15 s8 n24 zb x16 lo sel h168 thx q1 q2 wts bw bl".split())}
+    C.update(m0=T.M01[:, 1:2], nz=T.M10[:, 1:2], hi=T.M10[:, 8:9])
 
     def slot(u):
         k = "M" if u == 0 else "S"
         return T["H" + k][:, 128 * u:128 * u + 128], T["LL" + k][:, 128 * u:128 * u + 128], T["W" + k][:, WW * u:WW * u + WW], k
 
-    def lengths():
-        ts(T.NU[:], T.NP[:], 1, A.add, 16, A.min, r="NP", w="NU")
+    def empty_rows():
         act(T.MS[:], T.MT[:].indirect(T.NU[:]), r="MT NU", w="MS")
 
-    def rows(b_, bank, last):
-        for w_ in range(2):
-            c = 128 * (2 * b_ + w_)
-            mm(B[bank][:, 0:128], T.RA[:, c:c + 128], T.WN[:, w_:256:2], w_ == 0, last and w_ == 1, "WN RA%d%d" % (b_, w_), "B%d" % bank)
-
     def words_in():
-        rows(1, 1, True)
-        rows(0, 2, False)
+        for b_ in (1, 0):
+            for w_ in range(2):
+                c = 128 * (2 * b_ + w_)
+                mm(B[2 - b_][:, 0:128], T.RA[:, c:c + 128], T.WN[:, w_:256:2], w_ == 0, b_ == 1 and w_ == 1, "WN RA%d%d" % (b_, w_), "B%d" % (2 - b_))
         mm(B[3][:, 0:256], T.IZ[:], T.WN[:], True, False, "IZ WN", "B3")
 
     def high_out(u):
         ts(slot(u)[0], B[1][:, 0:128], 2048, A.add, EMPTY, A.min, w="H%s%d" % (slot(u)[3], u), b="B1")
 
-    def row_of_ls(src):
-        ts(T.S15[:], T[src][:], 15, A.bitwise_and, r=src, w="S15")
+    def col_of_ls(u):
         tt(T.T1[:], T.SI[:], T.SI[:], A.mult, r="SI", w="T1")
+        tt(T.U7[:], T.N77[:], T.SI[:], A.add, r="N77 SI", w="U7")
+        ts(T.T2[:], T.T1[:], 5, A.arith_shift_right, r="T1", w="T2")
         cp(T.SU[:], T.S15[:], r="S15", w="SU")
         act(T.MK[:], T.RR[:, 32:48].indirect(T.SU[:]), r="RR1 SU", w="MK")
-
-    def col_of_ls(u):
-        ts(T.T2[:], T.T1[:], 5, A.arith_shift_right, r="T1", w="T2")
-        tt(T.U7[:], T.U7[:], T.SI[:], A.add, r="U7 SI", w="U7")
         tt(T.T1[:], T.T2[:], T.U7[:], A.add, r="T2 U7", w="T1")
-        ts(slot(u)[2][:, 264:280], T.SI[:], 5, A.mult, -16, A.add, r="SI", w="Ws%d" % u)
+        if u:
+            pop_at()
         ts(T.T2[:], T.T1[:], 1023, A.bitwise_and, r="T1", w="T2")
         cp(T.CU[:], T.T2[:], r="T2", w="CU")
 
@@ -202,12 +195,17 @@ def rank_program(g, core, T, topo):
         tt(T.MM[:], T[ls][:].indirect(T.CU[:]), T.MK[:], A.mult, r=ls + " CU MK", w="MM")
         for w_ in range(2):
             mm(B[2][:, 0:128], T.EXT[:, 8 - 8 * w_:136 - 8 * w_], T.MM[:, w_:256:2], False, w_ == 1, "MM EXT", "B2")
-        mm(B[3][:, 0:256], T.EXT[:, 8:136], T.MM[:], False, True, "MM EXT", "B3")
+
+    def pop_at():
+        ts(T.PU[:], B[1][:, 128:144], -32768, A.add, w="PU", b="B1")
 
     def low_out(u):
-        _, lo, wf, k = slot(u)
-        ts(lo, B[2][:, 0:128], C["bl"], A.add, EMPTY, A.min, r="bl", w="L%s%d" % (k, u), b="B2")
-        act(wf[:, 0:256], B[3][:, 0:256], F.Identity, bias=C["bw"], r="bw", w="Ww%d" % u, b="B3")
+        ts(T["W" + slot(u)[3]][:, WW * u + 264:WW * u + 280], T.SI[:], 5, A.mult, -16, A.add, r="SI", w="Ws%d" % u)
+        ts(slot(u)[1], B[2][:, 0:128], C["bl"], A.add, EMPTY, A.min, r="bl", w="L%s%d" % (slot(u)[3], u), b="B2")
+
+    def words_out(u):
+        mm(B[3][:, 0:256], T.EXT[:, 8:136], T.MM[:], False, True, "MM EXT", "B3")
+        act(T["W" + slot(u)[3]][:, WW * u:WW * u + 256], B[3][:, 0:256], F.Identity, bias=C["bw"], r="bw", w="Ww%d" % u, b="B3")
 
     def wkey(u):
         return "WM%d" % u if u else "Ww0 Ws0 Wn0 Wz"
@@ -215,123 +213,144 @@ def rank_program(g, core, T, topo):
     def build_sh(u):
         lo, wk = WW * u, "WM%d" % u if u else "Ww0 X0"
         for h in (8, 5, 3, 2, 1, 0):
-            c = 256 * h
+            c = 256 * (h or 16)
             if u < TV - 1:
                 d = 17 - h
                 dma("sh", T.SH[d:128, c:c + 256], T.WM[0:128 - d, lo:lo + 256], r=wk, w="SA%d" % h)
                 dma("sh", T.SH[0:d, c:c + 256], T.WM[128 - d:128, lo:lo + 256], r=wk, w="SB%d" % h)
             else:
                 dma("sh", T.SH[0:128 - h, c:c + 256], T.WM[h:128, lo:lo + 256], r=wk, w="SA%d SB%d" % (h, h))
-    shk = "SH4 SH6 " + " ".join("SA%d SB%d" % (h, h) for h in (8, 5, 3, 2, 1, 0))
+    shk = " ".join("SA%d SB%d" % (h, h) for h in (8, 5, 3, 2, 1, 0))
 
     iota(T.IP[:], [[0, 4]], 0, 1, "IP")
     iota(T.IS[:], [[1, 16]], 0, 16, "IS")
     iota(T.IU[:], [[1, 32]], 0, 0, "IU")
-    iota(T.II[:], [[-1, 144]], 8, 1, "II")
     iota(T.IG[:, 1:9], [[-16, 8]], 0, 1, "IGa")
     iota(T.IG[:, 0:1], [[1, 1]], -112, 1, "IGb")
-    for buf, c in (("M1", -1.0), ("CQ", 0.0), ("ZR", 1.0), ("ONE", 1.0), ("EXT", 0.0), ("CP", 0.0), ("ZER", 0.0), ("D0", 1.0)):
-        v(V.memset, T[buf][:], c, w=buf)
+    iota(T.II[:], [[-1, 144]], 8, 1, "II")
+    v(V.memset, T.D0[:], 1.0, w="D0")
+    act(T.M1[:], T.D0[:], scale=-1.0, r="D0", w="M1")
+    act(T.CQ[:], T.D0[:], scale=0.0, r="D0", w="CQ")
+    act(T.EXT[:], T.D0[:, 0:136], scale=0.0, r="D0", w="EXT")
+    v(V.memset, T.CP[:], 0.0, w="CP")
+    v(V.memset, T.X[:, 4096:4112], 32.0, w="XE")
+    v(V.memset, T.ONE[:], 1.0, w="ONE")
+    v(V.memset, T.ZER[:], 0.0, w="ZER")
     run("g", g.affine_select, T.DB[:, 0:HALF], T.M1[:], [[-16, 8], [0, NPL]], A.is_equal, 0.0, 0, 1, r="M1", w="DB")
+    iota(T.I9[:, 1:9], [[NPL, 8]], 28, 0, "I9a")
+    iota(T.I9[:, 0:10:9], [[0, 2]], 28 + 7 * NPL, 0, "I9b")
+    iota(T.DB[:, 0:HALF:NPL], [[0, 8]], 0, 0, "DBa", r="DB")
+    iota(T.DB[:, 20:HALF:NPL], [[0, 8]], 32768, 0, "DBb", r="DB")
     cq = {0: 64, 1: -16, 8: 24, 9: -24, 13: 27, 14: -27, 16: 29, 17: -29, 18: 30, 19: 1, 20: 1}
     for q_, c in cq.items():
         iota(T.CQ[:, q_:HALF:NPL], [[0, 8]], c, 0, "CQ%d" % q_, r="CQ")
+    send("LS", prv, T.LSN[:], T.LS[:], r="LS")
     cqk = "CQ " + " ".join("CQ%d" % q_ for q_ in cq)
-    v(V.memset, T.X[:, 4096:4112], 32.0, w="XE")
-    v(V.memset, T.ZR[:, 0:512:8], 0.0, w="ZR")
     ts(T.IQ[:, 0:1], T.IP[:, 0:1], 15, A.bitwise_and, r="IP", w="IQ0")
     ts(T.POS[:], T.IS[:], 255, A.bitwise_and, r="IS", w="POS")
     cp(C["p15"], T.IQ[:, 0:1], r="IQ0", w="p15")
     cp(T.POSU[:], T.POS[:], r="POS", w="POSU")
-    ts(C["hi"], T.IQ[:, 0:1], 8, A.is_ge, r="IQ0", w="hi")
-    ts(T.M01[:], T.IU[:], C["p15"], A.is_gt, r="IU p15", w="M01")
-    ts(C["m0"], T.IQ[:, 0:1], 0, A.is_equal, r="IQ0", w="m0")
+    ts(T.M01[:], T.IU[:], C["p15"], A.is_gt, r="IU p15", w="M01 m0")
+    ts(T.M10[:], T.IU[:], C["p15"], A.is_le, r="IU p15", w="hi nz")
     ts(T.MT[:], T.M01[:], -8192, A.mult, 6144, A.add, r="M01", w="MT")
+    ts(T.NU[:], T.NP[:], 1, A.add, 16, A.min, r="NP", w="NU")
     ts(T.RR[:, 32:48], T.IU[:, 0:16], C["p15"], A.is_equal, r="IU p15", w="RR1")
-    ts(C["lo"], C["hi"], C["m0"], A.add, 0, A.is_equal, r="hi m0", w="lo")
+    empty_rows()
+    ts(T.S15[:], T.SI[:], 15, A.bitwise_and, r="SI", w="S15")
+    ts(T.N77[:], T.NP[:], 77, A.mult, r="NP", w="N77")
+    ts(C["lo"], C["nz"], C["hi"], A.subtract, r="hi nz", w="lo")
     ts(T.IDX[:], T.II[:], 0, A.is_equal, r="II", w="IDX")
-    ts(C["zb"], C["m0"], -1, A.mult, 1, A.add, r="m0", w="zb")
-    ts(T.IG[:, 0:9], T.IG[:, 0:9], 4, A.arith_shift_right, r="IGa IGb", w="IG")
-    ts(T.IQ[:, 2:3], T.IP[:, 0:1], 7, A.bitwise_and, r="IP", w="IQ2")
-    ts(T.KF[:, 0:9], T.IG[:, 0:9], 0, A.is_equal, r="IG", w="KF")
     for b_ in (1, 0):
+        if not b_:
+            col_of_ls(0)
         for w_ in range(2):
             c, o = 128 * (2 * b_ + w_), 8 + 8 * (b_ - w_)
             act(T.RA[:, c:c + 128], T.IDX[:, o:o + 128], scale=C["hi" if b_ else "lo"], r="IDX hi lo", w="RA%d%d" % (b_, w_))
-    lengths()
-    row_of_ls("SI")
-    ts(T.U7[:], T.NP[:], 77, A.mult, r="NP", w="U7")
-    act(T.IZ[:], IDB, scale=C["zb"], r="IDX zb", w="IZ")
-    ts(C["bw"], C["zb"], 2048, A.mult, r="zb", w="bw")
-    ts(C["bl"], T.IQ[:, 2:3], 0, A.is_gt, 2048, A.mult, r="IQ2", w="bl")
+    ts(T.IG[:, 0:9], T.IG[:, 0:9], 4, A.arith_shift_right, r="IGa IGb", w="IG")
+    ts(T.IQ[:, 2:3], T.IP[:, 0:1], 7, A.bitwise_and, r="IP", w="IQ2")
+    ts(T.KF[:, 0:9], T.IG[:, 0:9], 0, A.is_equal, r="IG", w="KF")
+    ts(C["wts"], T.WTI[:], 2.0 ** -22, A.mult, r="WTI", w="wts")
     cp(T.EXT[:, 8:136:16], T.KF[:, 1:9], r="KF", w="EXT")
-    col_of_ls(0)
-    tt(T.WN[:], T.WI[:].indirect(T.POSU[:]), T.MS[:], A.add, r="WIa WIb POSU MS", w="WN")
-    words_in()
-    send("LS", prv, T.LSN[:], T.LS[:], r="LS")
-    act(T.KN[:], T.KF[:, 1:9], scale=-1.0, r="KF", w="KN")
-    act(T.NIB[:], IDB, scale=-1.0, r="IDX", w="NIB")
-    ts(T.WM[:, 280:296], T.NP[:], 1, A.add, 16, A.min, r="NP", w="Wn0")
+    ts(C["bl"], T.IQ[:, 2:3], 0, A.is_gt, 2048, A.mult, r="IQ2", w="bl")
+    ts(T.WM[:, 280:296], T.NU[:], -1, A.mult, 16, A.add, r="NU", w="Wn0")
+    act(T.IZ[:], IDB, scale=C["nz"], r="IDX nz", w="IZ")
+    for h in HS:
+        act(T.CP[:, 1 + BASE[h]:169:NPL], T.KF[:, 1:9], scale=-1.0, r="KF CP", w="CP%d" % h)
+    cpk = "CP " + " ".join("CP%d" % h for h in HS)
     ts(C["q1"], T.IP[:, 0:1], 1, A.is_equal, 2.0 ** -5, A.mult, r="IP", w="q1")
     ts(C["q2"], T.IP[:, 0:1], 2, A.is_equal, 2.0 ** -22, A.mult, r="IP", w="q2")
-    ts(C["wts"], T.WTI[:], 2.0 ** -22, A.mult, r="WTI", w="wts")
+    ts(C["s8"], C["p15"], 8, A.add, r="p15", w="s8")
     ts(C["thx"], T.THI[:], C["q1"], A.add, C["q2"], A.add, r="THI q1 q2", w="thx")
     ts(C["q1"], C["q1"], C["q2"], A.add, 0, A.is_gt, r="q1 q2", w="q1")
-    high_out(0)
+    ts(C["n24"], C["p15"], 24, A.add, r="p15", w="n24")
+    tt(T.WN[:], T.WI[:].indirect(T.POSU[:]), T.MS[:], A.add, r="WIa WIb POSU MS", w="WN")
+    words_in()
     letters("LS")
+    high_out(0)
     act(T.THL[:], T.ONE[:], scale=C["thx"], r="ONE thx", w="THL")
     act(T.DB[:, HALF:336], T.CQ[:], scale=C["q1"], r="q1 " + cqk, w="DBc")
-    act(T.K2[:], T.KF[:, 1:9], scale=2.0, r="KF", w="K2")
-    act(T.KB[:], T.KF[:, 1:9], r="KF", w="KB")
-    act(T.WP[:], T.KF[:, 1:9], scale=C["wts"], r="KF wts", w="WP")
-    act(T.WQ[:], T.WP[:], scale=-1.0, r="WP", w="WQ")
-    v(V.memset, T.DB[:, 0:HALF:NPL], 0.0, r="DB", w="DBa")
-    v(V.memset, T.DB[:, 20:HALF:NPL], 32768.0, r="DB", w="DBb")
-    for h in HS:
-        cp(T.CP[:, 1 + BASE[h]:169:NPL], T.KN[:], r="KN CP", w="CP%d" % h)
-    cpk = "CP " + " ".join("CP%d" % h for h in HS)
+    for k_, sc in (("KN", -1.0), ("K2", 2.0), ("KB", 1.0)):
+        act(T[k_][:], T.KF[:, 1:9], scale=sc, r="KF", w=k_)
+    ts(C["bw"], C["nz"], 2048, A.mult, r="nz", w="bw")
+    ts(T.WP[:], T.KF[:, 1:9], C["wts"], A.mult, r="KF wts", w="WP")
+    ts(T.WQ[:], T.KF[:, 1:9], C["wts"], A.mult, -1, A.mult, r="KF wts", w="WQ")
+    ts(T.SV[:, 0:8], T.KF[:, 0:8], C["s8"], A.mult, r="KF s8", w="SV0a")
+    ts(T.SV[:, 8:16], T.KF[:, 0:8], C["n24"], A.mult, r="KF n24", w="SV0b")
     low_out(0)
+    words_out(0)
     build_sh(0)
-    iota(T.I9[:, 1:9], [[NPL, 8]], 28, 0, "I9a")
-    iota(T.I9[:, 0:10:9], [[0, 2]], 28 + 7 * NPL, 0, "I9b")
-    iota(T.WM[:, 256:264], [[0, 8]], 0, 0, "Wz")
-    for q_ in (0, 1, 9, 14, 17, 19):
-        iota(T.D0[:, q_:HALF:NPL], [[0, 8]], 0, 0, "D0%d" % q_, r="D0")
-    d0k = "D0 " + " ".join("D0%d" % q_ for q_ in (0, 1, 9, 14, 17, 19))
-    iota(T.ZROW[0:32, 0:16], [[0, 16]], 0, 0, "ZROW")
-    iota(T.ZROW[0:32, 16:32], [[8, 16]], 0, 0, "ZROWb")
-    iota(T.U[:, 0:8], [[0, 8]], 0, 0, "Uz")
-    iota(T.ZC[:, 2048:2064], [[0, 16]], 0, 0, "ZCz")
-    iota(T.IT[:], [[16, 16]], 0, 256, "IT")
-    iota(T.IA[:], [[256, 16]], 0, 0, "IA")
-    iota(T.IL[:], [[0, NQ], [256, 16 // NQ]], 0, 0, "IL")
-    iota(T.SH[:, 1024:1280], [[0, 256]], 0, 0, "SH4")
-    iota(T.SH[:, 1536:2048], [[0, 512]], 0, 0, "SH6")
-    iota(T.NEG[:], [[0, 256]], -128, 0, "NEG")
-    iota(T.X[:, 4112:8192:16], [[0, 255]], 0, 0, "XD")
-    for u in range(1, TV):
-        iota(T.WS[:, WW * u + 256:WW * u + 264], [[0, 8]], 0, 0, "Wz%d" % u)
-    iota(T.FO[:, 0:8], [[0, 8]], 0, 0, "FOz")
     ts(T.IQ[:, 1:2], T.IP[:, 0:1], 4, A.arith_shift_right, r="IP", w="IQ1")
     ts(C["h168"], C["hi"], HALF, A.mult, r="hi", w="h168")
-    ts(C["s8"], C["p15"], 8, A.add, r="p15", w="s8")
-    ts(C["n24"], C["p15"], 24, A.add, r="p15", w="n24")
     tt(C["sel"], T.IQ[:, 1:2], T.IQ[:, 2:3], A.is_equal, r="IQ1 IQ2", w="sel")
-    for o, lo in ((0, 0), (16, 1)):
-        ts(T.SV[:, o:o + 8], T.KF[:, lo:lo + 8], C["s8"], A.mult, r="KF s8", w="SV%da" % o)
-        ts(T.SV[:, o + 8:o + 16], T.KF[:, lo:lo + 8], C["n24"], A.mult, r="KF n24", w="SV%db" % o)
+    cp(T.POSB[:], T.POS[:], r="POS", w="POSB")
+    ts(T.CV[:], T.I9[:], C["h168"], A.add, C["sel"], A.mult, r="I9a I9b h168 sel", w="CV")
+
+    def diagonal(out, n, base, val, key):
+        run("g", g.affine_select, out, T.ZER[:, 0:n], [[-1, n]], A.not_equal, val, base, 1, r="ZER", w=key)
+    diagonal(T.NIB[:], 128, 0, -1.0, "NIB")
+    iota(T.ZR[:], [[0, 512]], 1, 0, "ZR")
+    iota(T.ZR[:, 0:512:8], [[0, 64]], 0, 0, "ZR")
+    iota(T.WM[:, 256:264], [[0, 8]], 0, 0, "Wz")
+    for q_ in (0, 1, 9, 14, 17, 19):
+        iota(T.D0[:, q_:HALF:NPL], [[0, 8]], 0, 0, "D0%d" % q_, r="M1 CQ EXT")
+    d0k = "D0 " + " ".join("D0%d" % q_ for q_ in (0, 1, 9, 14, 17, 19))
+    iota(T.ZROW[0:32, 0:16], [[0, 16]], 144, 0, "ZROW")
+    iota(T.ZROW[0:32, 16:32], [[8, 16]], 0, 0, "ZROWd")
+    iota(T.U[:, 0:8], [[0, 8]], 0, 0, "Uz")
+    iota(T.ZC[:, 2048:2064], [[0, 16]], 0, 0, "ZCz")
+    diagonal(T.I256[:], 128, 0, 256.0, "I256")
+    diagonal(T.J256[:], 128, 0, 1 / 256, "J256")
+    diagonal(T.ROT[:, 0:112], 112, -16, 1.0, "ROTa")
+    diagonal(T.ROT[:, 112:128], 16, 0, 1.0, "ROTb")
+
+    def iotas_between():
+        iota(T.IA[:], [[256, 16]], 0, 0, "IA")
+        iota(T.X[:, 4112:8192:16], [[0, 255]], 0, 0, "XD")
+        iota(T.NEG[:], [[0, 256]], -128, 0, "NEG")
+        iota(T.WS[:, WW + 256:WW + 264], [[0, 8]], 0, 0, "Wz1")
 
     def late_consts():
-        act(T.RR[:, 0:16], T.RR[:, 32:48], scale=2.0 ** 22, r="RR1", w="RR2")
-        act(T.RR[:, 16:32], T.RR[:, 32:48], scale=32.0, r="RR1", w="RR3")
+        for c, sc, k_ in ((48, 2.0 ** -12, "RR4"), (64, -1.0, "RR5"), (16, 32.0, "RR3"), (0, 2.0 ** 22, "RR2")):
+            act(T.RR[:, c:c + 16], T.RR[:, 32:48], scale=sc, r="RR1", w=k_)
         act(C["zb"], C["p15"], F.Identity, scale=128.0, bias=-1.0, r="p15", w="zb")
-        act(C["x16"], C["p15"], scale=16.0, r="p15", w="x16")
-        ts(T.CV[:], T.I9[:], C["h168"], A.add, C["sel"], A.mult, r="I9a I9b h168 sel", w="CV")
 
-    def last_consts():
-        ts(T.BS[:], T.IT[:], 4095, A.bitwise_and, r="IT", w="BS")
-        ts(T.BA[:], T.IA[:], C["x16"], A.add, r="IA x16", w="BA")
-        ts(T.BL[:], T.IL[:], C["x16"], A.add, r="IL x16", w="BL")
+    def iotas_after():
+        for u in range(2, TV):
+            iota(T.WS[:, WW * u + 256:WW * u + 264], [[0, 8]], 0, 0, "Wz%d" % u)
+        iota(T.IL[:], [[0, 2], [256, 8]], 0, 0, "IL")
+        iota(T.FO[:, 0:8], [[0, 8]], 0, 0, "FOz")
+
+    def later_consts(t):
+        if t == 0:
+            act(C["x16"], C["p15"], scale=16.0, r="p15", w="x16")
+            act(T.BA[:], T.IA[:], F.Identity, bias=C["x16"], r="IA x16", w="BA")
+        if t == 1:
+            act(T.BS[:], T.POSB[:], scale=16.0, r="POSB", w="BS")
+        if t == 2:
+            ts(T.SV[:, 16:24], T.KF[:, 1:9], C["s8"], A.mult, r="KF s8", w="SV16a")
+            ts(T.SV[:, 24:32], T.KF[:, 1:9], C["n24"], A.mult, r="KF n24", w="SV16b")
+        if t == 3:
+            act(T.BL[:], T.IL[:], F.Identity, bias=C["x16"], r="IL x16", w="BL")
 
     PD, PC = 0, HALF
 
@@ -348,24 +367,22 @@ def rank_program(g, core, T, topo):
 
     def bulk(t):
         win = T.X[:, 0:4112]
-        xk = "X0 X1 X2 X3 XE "
+        xk = "X0 X1 XE "
         Hl, Ll = T.HM[:, 128 * t:128 * t + 128], T.LLM[:, 128 * t:128 * t + 128]
 
-        def gather(q, buf, lst, c, n, key, lk):
-            if q == "v":
-                cp(buf[:, c:c + n], win.indirect(lst[:, c // 16:(c + n) // 16]), r=xk + lk, w=key)
-            else:
-                act(buf[:, c:c + n], win.indirect(lst[:, c // 16:(c + n) // 16]), r=xk + lk, w=key)
+        def gather(q, buf, lk, c, n, key):
+            off = T[lk][:, 128 * t + c // 16:128 * t + (c + n) // 16]
+            (cp if q == "v" else act)(buf[:, c:c + n], win.indirect(off), r=xk + lk[-2:] + str(t), w=key)
         for hf in range(2):
-            gather("v", T.GH, Hl, 1024 * hf, 512, "GH%da" % hf, "HM%d" % t)
-            gather("a", T.GH, Hl, 1024 * hf + 512, 512, "GH%db" % hf, "HM%d" % t)
-        gather("v", T.GL, Ll, 0, 512, "GL0a", "LM%d" % t)
-        gather("a", T.GL, Ll, 512, 512, "GL0b", "LM%d" % t)
-        gather("a", T.GL, Ll, 1024, 1024, "GL1", "LM%d" % t)
-        gl = ("GL0a GL0b", "GL1")
+            gather("v", T.GH, "HM", 1024 * hf, 512, "GH%da" % hf)
+            gather("a", T.GH, "HM", 1024 * hf + 512, 512, "GH%db" % hf)
+        gather("v", T.GL, "LLM", 0, 512, "GL0a")
+        gather("a", T.GL, "LLM", 512, 512, "GL0b")
+        gather("a", T.GL, "LLM", 1024, 1024, "GL1a GL1b")
+        gl = ("GL0a GL0b", "GL1a GL1b")
         gh = ("GH0a GH0b", "GH1a GH1b")
         for bk in (1, 2, 3):
-            mm(B[bk][:, 0:512], T.ZER[0:1, :], T.ZR[0:1, :], True, False, "ZER ZR", "B%d" % bk)
+            mm(B[bk][:, 0:512], T.ZER[0:1, :], (T.ZR if t else T.X)[0:1, 0:512], True, False, "ZER ZR" if t else "ZER X0", "B%d" % bk)
         for hf in range(2):
             mm(B[6 + hf][:, 0:336], T.THL[:], T.DB[:], True, False, "THL DB DBa DBb DBc", "B%d" % (6 + hf))
 
@@ -407,7 +424,7 @@ def rank_program(g, core, T, topo):
             for k_ in range(2):
                 c = 1024 * hf + 512 * k_
                 v(V.tensor_tensor_scan, T.ZC[:, c:c + 512], T.ZR[:], T.GL[:, c:c + 512], 0.0, A.mult, A.max,
-                  r="ZR " + (gl[0].split()[k_] if hf == 0 else gl[1]), w="ZC%d%d" % (hf, k_))
+                  r="ZR " + gl[hf].split()[k_], w="ZC%d%d" % (hf, k_))
 
         def seeds(hf):
             zk, bk = "ZC%d0 ZC%d1 " % (hf, hf), "B%d" % (6 + hf)
@@ -424,105 +441,107 @@ def rank_program(g, core, T, topo):
                 a, bk, o = B[4 + hf][:, 128 * j:128 * j + 128], "B%d" % (4 + hf), j + h
             tt(T.DL[:, c:c + 128], a, row(T.GL, hf, o), A.max, r=gl[hf], w="DL%d%d%d" % (hf, h, j), b=bk)
 
-        def add(hf, h, j, last=False):
+        def add(hf, h, j, stop=False):
             c = 256 * MAXED.index((h, j)) + 128 * hf
-            mm(place(PD, hf, BASE[h] + j), T.DL[:, c:c + 128], T.K2[:], False, last, "K2 DL%d%d%d" % (hf, h, j), "B%d" % (6 + hf))
+            mm(place(PD, hf, BASE[h] + j), T.DL[:, c:c + 128], T.K2[:], False, stop, "K2 DL%d%d%d" % (hf, h, j), "B%d" % (6 + hf))
 
         def sizes(bk):
             act(T.DA[:, 512 * (bk - 1):512 * bk], B[bk][:, 0:512], F.Abs, w="DA%d" % bk, b="B%d" % bk)
 
-        def add_sizes(bk, last=False):
-            for hf in (1, 0):
-                for j in range(2, 8):
-                    b_, c = diff_at(hf, j)
-                    if b_ == bk:
-                        c += 512 * (bk - 1)
-                        mm(place(PD, hf, BASE[8] + j), T.DA[:, c:c + 128], T.KB[:], False, last and (hf, j) == (0, 7), "KB DA%d" % bk, "B%d" % (6 + hf))
+        def add_sizes(hf, js):
+            for j in js:
+                bk, c = diff_at(hf, j)
+                c += 512 * (bk - 1)
+                mm(place(PD, hf, BASE[8] + j), T.DA[:, c:c + 128], T.KB[:], False, False, "KB DA%d" % bk, "B%d" % (6 + hf))
 
         up = [p_ for p_ in MAXED if sum(p_) >= 8]
         dn = [p_ for p_ in MAXED if sum(p_) < 8]
-        highs(0)
-        highd(0)
-        highs(1)
-        highd(1)
+        for hf in range(2):
+            highs(hf)
+            highd(hf)
+            highsums(hf)
         lows(0)
         lowd(0)
         sizes(1)
         zc(0)
         for p_ in up + dn:
             pair(0, *p_)
-        highsums(0)
-        highsums(1)
         lowsums(0)
+        seeds(0)
+        for p_ in up:
+            add(0, *p_)
         lows(1)
         lowd(1)
         sizes(2)
         sizes(3)
-        seeds(0)
-        for p_ in up + dn:
+        lowsums(1)
+        for p_ in dn[:-1]:
             add(0, *p_)
         zc(1)
-        lowsums(1)
-        add_sizes(1)
+        add_sizes(0, range(2, 6))
         seeds(1)
-        add_sizes(2, True)
-        o = 16 if t == TV - 1 else 0
-        act(T.ES[:], T.WM[:, WW * t + 256:WW * t + WW].indirect(T.SV[:, o:o + 16]), r=wkey(t) + " SV%da SV%db" % (o, o), w="ES")
+        add_sizes(0, (6, 7))
+        add(0, *dn[-1], stop=True)
+        add_sizes(1, (6, 7))
         for p_ in up + dn:
             pair(1, *p_)
         for i, p_ in enumerate(up + dn):
             if i == 6:
-                add_sizes(3)
-            add(1, *p_, last=i == len(MAXED) - 1)
-        for k_ in range(2):
-            mm(B[5][:, 16 * k_:16 * k_ + 16], T.ES[:, 128 * k_:128 * k_ + 128], T.RR[:, 32:48], True, True, "ES RR1", "B5")
+                add_sizes(1, range(2, 6))
+            add(1, *p_, stop=i == len(MAXED) - 1)
+        o = 16 if t == TV - 1 else 0
+        act(T.ES[:], T.WM[:, WW * t + 256:WW * t + WW].indirect(T.SV[:, o:o + 16]), r=wkey(t) + " SV%da SV%db" % (o, o), w="ES")
 
     def decode(t):
         last = t == TV - 1
-        u = t + 1
-        z = T.ZS[:, ZW * t:ZW * t + ZW]
-        mm(B[0][:, 0:32], T.ONE[0:1, :], T.ZROW[0:1, :], True, False, "ONE ZROW ZROWb", "B0")
+        nh, c0 = T.NH[:], ZW * t
+        mm(B[4][:, 16:32], T.ES[:, 0:128], T.RR[:, 48:64], True, True, "ES RR4", "B4")
+        mm(B[5][:, 0:16], T.ONE[0:1, :], T.ZROW[0:1, 0:16], True, False, "ONE ZROW", "B5")
+        mm(B[5][:, 0:16], T.ES[:, 128:256], T.RR[:, 64:80], False, False, "ES RR5", "B5")
+        mm(B[0][:, 0:16], T.ONE[0:1, :], T.ZROW[0:1, 16:32], True, False, "ONE ZROWd", "B0")
+        mm(B[1][:, 128:144], IDB, T.POSB[:], True, False, "IDX POSB", "B1")
         for hf in range(2):
             c, bk = HALF * hf, "B%d" % (6 + hf)
             v(V.tensor_tensor_scan, T.S1[:, c:c + HALF], T.D0[:], B[6 + hf][:, 0:HALF], 0.0, A.mult, A.max, r=d0k, w="S1%d" % hf, b=bk)
+        for hf in range(2):
+            c, bk = HALF * hf, "B%d" % (6 + hf)
             v(V.tensor_tensor_scan, T.U[:, 8 + c:8 + c + HALF], B[6 + hf][:, HALF:336], T.S1[:, c:c + HALF], 0.0, A.add, A.min, r="S1%d" % hf, w="U%d" % hf, b=bk)
         cp(T.E[:], T.U[:].indirect(T.CV[:, 0:9]), r="U0 U1 Uz CV", w="E")
-        mm(B[0][:, 0:32], T.E[:, 16:144], T.RR[:, 0:32], False, True, "E RR2 RR3", "B0")
         o = 16 if last else 0
+        mm(B[0][:, 0:16], T.E[:, 16:144], T.RR[:, 16:32], False, True, "E RR3", "B0")
         mm(B[4][:, 0:16], T.E[:, o:o + 128], T.RR[:, 0:16], True, True, "E RR2", "B4")
-        ts(T.ZO[:], B[0][:, 16:32], C["zb"], A.add, r="zb", w="ZO", b="B0")
-        cp(T.UI[:], B[0][:, 0:16], w="UI", b="B0")
-        act(z[:, 0:256], T.ZC[:].indirect(T.ZO[:]), r="ZC00 ZC01 ZC10 ZC11 ZCz ZO", w="Za")
-        cp(T.UR[:], B[4][:, 0:16], w="UR", b="B4")
-        ts(T.FI[:], T.UI[:], (1 << 21) + 15, A.bitwise_and, r="UI", w="FI")
-        ts(T.H[:], T.UR[:], 17, A.arith_shift_right, 15, A.bitwise_and, r="UR", w="H")
-        ts(z[:, 256:272], T.FI[:], 4096, A.min, r="FI", w="Zb")
-        send("Z%d" % t, nxt, T.ZM[:, ZW * t:ZW * t + ZW], z, r="Za Zb")
-        tt(T.NP[:], B[5][:, 16:32], T.H[:], A.subtract, r="H", w="NP", b="B5")
-        ts(T.HB[:], T.UR[:], 9, A.arith_shift_right, 0xF00, A.bitwise_and, r="UR", w="HB")
+        ts(T.ZO[:], B[0][:, 0:16], C["zb"], A.add, r="zb", w="ZO", b="B0")
+        act(T.ZS[:, c0:c0 + 256], T.ZC[:].indirect(T.ZO[:]), r="ZC00 ZC01 ZC10 ZC11 ZCz ZO", w="Za")
+        ts(nh, B[4][:, 0:16], 1 << 21, A.is_ge, 4096, A.mult, w="NH", b="B4")
+        ts(T.HB[:], B[4][:, 0:16], 2.0 ** -17, A.mult, 127.77, A.add, w="HB", b="B4")
+        mm(B[1][:, 128:144], T.I256[:], T.HB[:], False, True, "I256 HB", "B1")
+        mm(B[5][:, 0:16], T.NIB[:], T.HB[:], False, False, "NIB HB", "B5")
+        mm(B[5][:, 0:16], T.J256[:], nh, False, True, "J256 NH", "B5")
+        tt(T.A5[:], B[4][:, 16:32], nh, A.mult, r="NH", w="A5", b="B4")
+        tt(T.SUM[:], B[4][:, 0:16], T.A5[:], A.add, r="A5", w="SUM", b="B4")
         if last:
-            cp(T.NU[:], T.NP[:], r="NP", w="NU")
+            cp(T.NU[:], B[5][:, 0:16], w="NU", b="B5")
             act(T.MS[:], T.M01[:].indirect(T.NU[:]), r="M01 NU", w="MS")
         else:
-            lengths()
-        tt(T.PL[:], T.HB[:], T.POS[:], A.add, r="HB POS", w="PL")
-        ts(T.NH[:], T.UR[:], 1 << 21, A.is_ge, r="UR", w="NH")
-        cp(T.PU[:], T.PL[:], r="PL", w="PU")
-        tt(T.A5[:], B[5][:, 0:16], T.NH[:], A.mult, r="NH", w="A5", b="B5")
-        if not last:
-            ts(T.U7[:], T.NP[:], 77, A.mult, r="NP", w="U7")
-        tt(T.SUM[:], T.A5[:], T.UR[:], A.add, r="A5 UR", w="SUM")
-        if not last:
-            ts(slot(u)[2][:, 280:296], T.NP[:], 1, A.add, 16, A.min, r="NP", w="Wn%d" % u)
+            ts(T.NU[:], B[5][:, 0:16], 1, A.add, 16, A.min, w="NU", b="B5")
+            act(T.N77[:], B[5][:, 0:16], scale=77.0, w="N77", b="B5")
+            empty_rows()
+        ts(T.S15[:], T.SUM[:], 15, A.bitwise_and, r="SUM", w="S15")
         ts(T.SI[:], T.SUM[:], 4095, A.bitwise_and, r="SUM", w="SI")
+        tt(T.ZS[:, c0 + 256:c0 + ZW], T.S15[:], nh, A.max, r="S15 NH", w="Zb")
+        send("Z%d" % t, nxt, T.ZM[:, c0:c0 + ZW], T.ZS[:, c0:c0 + ZW], r="Za Zb")
+        if last:
+            pop_at()
 
     def columns(t, base):
-        tt(T.CI[:], T.ZM[:, ZW * t + 256:ZW * t + ZW], T[base][:], A.add, r="ZM%d %s" % (t, base), w="CI")
-        cp(T.CX[:], T.CI[:], r="CI", w="CX")
+        rot, rk = (IDB, "IDX") if t == TV - 1 else (T.ROT[:], "ROTa ROTb")
+        mm(B[4][:, 32:48], IDB, T[base][:], True, False, "IDX " + base, "B4")
+        mm(B[4][:, 32:48], rot, T.ZM[:, ZW * t + 256:ZW * t + ZW], False, True, "ZM%d %s" % (t, rk), "B4")
+        cp(T.CX[:], B[4][:, 32:48], w="CX", b="B4")
 
-    def xupdate(t, lo, e0, e1, xk):
+    def xupdate(m, e0, e1, lo, xk):
         win, cols = T.X[:, lo:8192], T.CX[:, e0 // 16:e1 // 16]
-        tt(T.XT[:, e0:e1], win.indirect(cols), T.ZM[:, ZW * t + e0:ZW * t + e1], A.add, r="ZM%d CX %s" % (t, xk), w="XT")
+        tt(T.XT[:, e0:e1], win.indirect(cols), T.ZM[:, ZW * m + e0:ZW * m + e1], A.add, r="ZM%d CX %s" % (m, xk), w="XT")
         ts(T.XU[:, e0:e1], T.XT[:, e0:e1], 0.5, A.mult, 127.75, A.add, r="XT", w="XU")
         tt(win.indirect(cols), T.XU[:, e0:e1], T.NEG[:, e0:e1], A.add, r="XU NEG CX", w=xk)
 
@@ -534,32 +553,36 @@ def rank_program(g, core, T, topo):
         if t == TV - 1:
             break
         u = t + 1
-        row_of_ls("SUM")
+        if t == 0:
+            iotas_between()
         mm(B[0][:, 32:48], T.ONE[:], T.NH[:], True, True, "ONE NH", "B0")
+        col_of_ls(u)
         tt(T.WN[:], T.SH[:].indirect(T.PU[:]), T.MS[:], A.add, r="PU MS " + shk, w="WN")
         words_in()
-        act(T.NJ[:], B[0][:, 32:48], scale=-1.0, accum_out=T.NS[:], w="NS", b="B0")
-        col_of_ls(u)
+        letters("LSN")
         high_out(u)
         send("H%d" % u, nxt, T.HM[:, 128 * u:128 * u + 128], slot(u)[0], r="HS%d" % u)
-        letters("LSN")
-        cp(T.AI[:], T.NS[:], r="NS", w="AI")
-        if t == 0:
-            last_consts()
-        ts(T.AJ[:], T.AI[:], 15, A.bitwise_and, r="AI", w="AJ")
-        ts(T.BC[:], T.AJ[:], C["m0"], A.mult, C["thx"], A.add, r="AJ m0 thx", w="BC")
-        low_out(u)
+        act(T.WS[:, WW * u + 280:WW * u + WW], B[5][:, 0:16], F.Relu, scale=-1.0, bias=15.0, w="Wn%d" % u, b="B5")
+        act(T.NJ[:], B[0][:, 32:48], F.Identity, scale=-2.0 ** -12, bias=-128.0, accum_out=T.NS[:], w="NS", b="B0")
+        act(T.AT[:], T.NS[:], F.Identity, scale=-1 / 16, bias=0.47, r="NS", w="AT")
+        act(T.AR[:], T.AT[:], F.Identity, scale=16.0, bias=T.NS[:], r="AT NS", w="AR")
+        act(T.BC[:], T.AR[:], F.Identity, scale=C["m0"], bias=C["thx"], r="AR m0 thx", w="BC")
         act(T.THL[:], T.ONE[:], scale=T.BC[:], r="ONE BC", w="THL")
+        later_consts(t)
+        low_out(u)
         send("L%d" % u, nxt, T.LLM[:, 128 * u:128 * u + 128], slot(u)[1], r="LS%d" % u)
+        columns(t, "BS" if t % 2 else "BA")
+        words_out(u)
         send("W%d" % u, nxt, T.WM[:, WW * u:WW * u + WW], slot(u)[2], r="Ww%d Ws%d Wn%d Wz%d" % (u, u, u, u))
         build_sh(u)
-        columns(t, "BS" if t % 2 else "BA")
-        xupdate(t, 0, 0, 256, XK)
+        if t == 0:
+            iotas_after()
+        xupdate(t, 0, 256, 0, XK)
 
     tt(T.YW[:], T.SH[:].indirect(T.PU[:]), T.MS[:], A.mult, r="PU MS " + shk, w="YW")
     dma("oyw", T.yw[:], T.YW[:], r="YW")
     cp(T.FO[:, 8:24], T.SI[:], r="SI", w="FOs")
-    cp(T.FO[:, 24:40], T.NP[:], r="NP", w="FOn")
+    cp(T.FO[:, 24:40], B[5][:, 0:16], w="FOn", b="B5")
     act(T.ES[:], T.FO[:].indirect(T.SV[:, 16:32]), r="FOz FOs FOn SV16a SV16b", w="ES")
     for k_ in range(2):
         mm(B[1][:, 16 * k_:16 * k_ + 16], T.ES[:, 128 * k_:128 * k_ + 128], T.RR[:, 32:48], True, True, "ES RR1", "B1")
@@ -567,10 +590,10 @@ def rank_program(g, core, T, topo):
     dma("oyn", T.ys[:], T.YO[:, 0:16], r="YO", q="a")
     dma("oyn", T.yn[:], T.YO[:, 16:32], r="YO", q="a")
     columns(TV - 1, "BL")
-    for k_ in range(NQ):
-        c, e, xs = 4096 // NQ * k_, 256 // NQ * k_, range(4 // NQ * k_, 4)
-        xupdate(TV - 1, c, e, e + 256 // NQ, " ".join("X%d" % i for i in xs) + " XD XE")
-        dma("oyx", T.yx[:, c:c + 4096 // NQ], T.X[:, c:c + 4096 // NQ], r=" ".join("X%d" % i for i in xs[:4 // NQ]))
+    for k_ in range(2):
+        lo = 2048 * k_
+        xupdate(TV - 1, 128 * k_, 128 * k_ + 128, lo, "X1 XD XE" if k_ else XK)
+        dma("oyx", T.yx[:, lo:lo + 2048], T.X[:, lo:lo + 2048], r="X%d" % k_)
     for sem, n in tot.items():
         if known["g"].get(sem, 0) < n:
             g.wait_ge(T.sem[sem], n)

@@ -1,49 +1,64 @@
+from concourse.bass import DstId, RemoteDMATransfer
 from concourse.mybir import AluOpType as A, ActivationFunctionType as F
 
 HS = (8, 5, 3, 2, 1)
 BASE = {8: 1, 5: 9, 3: 14, 2: 17, 1: 19}
 NPL, HALF = 21, 168
 TV = 5
-EMPTY = 4097
+EMPTY = 4098
 ZW, WW = 272, 296
+SW = 4352
 MAXED = [(8, 0), (8, 1)] + [(h, j) for h in (5, 3, 2) for j in range(h)]
 
 bf, f16, f32, i32, u16 = "bfloat16", "float16", "float32", "int32", "uint16"
 SCRATCH = {n: ("sbuf", [p, c], d) for n, p, c, d in [
-    ("X", 128, 8192, bf), ("LS", 128, 1024, i32), ("LSN", 128, 1024, i32), ("SH", 128, 4352, f32),
+    ("X", 128, 8192, bf), ("LS", 128, 1024, i32), ("LSN", 128, 1024, i32), ("SH", 128, TV * SW, f32),
     ("GL", 128, 2048, bf), ("GH", 128, 2048, bf), ("ZC", 128, 2064, bf), ("ZR", 128, 512, bf),
     ("DL", 128, 12 * 256, bf), ("DA", 128, 1536, bf), ("NEG", 128, 256, bf),
     ("ZS", 128, 5 * ZW, bf), ("ZM", 128, 5 * ZW, bf), ("HS", 128, 5 * 128, u16), ("HM", 128, 5 * 128, u16),
-    ("LLS", 128, 5 * 128, u16), ("LLM", 128, 5 * 128, u16), ("WS", 128, 5 * WW, f32), ("WM", 128, 5 * WW, f32),
-    ("WI", 128, 256, i32), ("WN", 128, 256, f16), ("MM", 128, 256, f32), ("MK", 128, 256, bf), ("MS", 128, 256, bf),
-    ("IDX", 128, 144, bf), ("NIB", 128, 128, bf), ("IZ", 128, 128, bf), ("RA", 128, 512, bf),
-    ("I256", 128, 128, bf), ("J256", 128, 128, bf), ("EXT", 128, 136, f32), ("ONE", 128, 128, bf), ("THL", 128, 128, bf), ("ZER", 128, 128, bf),
+    ("LLS", 128, 5 * 128, u16), ("LLM", 128, 5 * 128, u16), ("WS", 128, 5 * WW, f32),
+    ("WI", 128, 256, i32), ("WN", 128, 256, f16), ("WX", 128, 256, bf), ("MM", 128, 256, f16), ("MK", 128, 256, bf), ("MS", 128, 256, f32),
+    ("MF", 128, 256, f32), ("EXF", 128, 144, f32), ("LOW", 128, 256, i32), ("MX2", 128, 32, bf), ("M0B", 128, 128, bf),
+    ("IDX", 128, 160, bf), ("IZ", 128, 128, bf), ("IZR", 128, 128, bf), ("NIB", 128, 128, bf), ("RA", 128, 512, bf), ("ROT", 128, 128, bf),
+    ("EXT", 128, 144, bf), ("EXR", 128, 128, bf), ("BA", 128, 48, bf), ("OB", 128, 48, bf), ("OF", 128, 48, u16),
+    ("J256", 128, 128, bf), ("J77", 128, 128, bf), ("ONE", 128, 128, bf), ("THL", 128, 128, bf), ("ZER", 128, 128, bf),
     ("CQ", 128, HALF, bf), ("DB", 128, 336, bf), ("D0", 128, HALF, bf), ("M1", 128, HALF, bf), ("CP", 128, 176, bf),
-    ("S1", 128, 336, bf), ("U", 128, 344, f32), ("E", 128, 144, f32), ("ES", 128, 256, f32), ("RR", 128, 80, f32),
-    ("ZROW", 32, 32, bf), ("POSB", 128, 16, bf), ("NH", 128, 16, bf), ("HB", 128, 16, bf), ("MT", 128, 32, bf), ("M01", 128, 32, f32),
-    ("KF", 128, 16, f32), ("KB", 128, 8, bf), ("KN", 128, 8, bf), ("K2", 128, 8, bf), ("WP", 128, 8, bf), ("WQ", 128, 8, bf),
-    ("II", 128, 144, i32), ("IG", 128, 16, i32), ("IP", 128, 4, i32), ("IQ", 128, 4, i32), ("IU", 128, 32, i32), ("I9", 128, 10, i32),
-    ("IS", 128, 16, i32), ("IA", 128, 16, f32), ("IL", 128, 16, f32), ("COL", 128, 24, f32),
-    ("POS", 128, 16, i32), ("POSU", 128, 16, u16), ("BA", 128, 16, bf), ("BS", 128, 16, bf), ("BL", 128, 16, bf),
-    ("CV", 128, 10, u16), ("SV", 128, 32, u16), ("N77", 128, 16, f32), ("ROT", 128, 128, bf), ("M10", 128, 32, f32),
+    ("S1", 128, 336, bf), ("U", 128, 344, f32), ("E", 128, 144, f32), ("E2", 128, 144, bf), ("ES", 128, 256, f32),
+    ("RR", 128, 96, f32), ("RB", 128, 80, bf), ("ZROW", 32, 80, bf), ("NH", 128, 16, bf), ("MT", 128, 32, f32), ("M01", 128, 32, f32),
+    ("KF", 128, 16, f32), ("KN", 128, 8, bf), ("K2", 128, 8, bf), ("KB", 128, 8, bf), ("WP", 128, 8, bf), ("WQ", 128, 8, bf),
+    ("II", 128, 160, i32), ("IG", 128, 16, i32), ("IP", 128, 4, i32), ("IQ", 128, 8, i32), ("IU", 128, 32, i32), ("I9", 128, 10, i32),
+    ("IS", 128, 16, i32), ("IA", 128, 32, f32), ("COL", 128, 24, f32), ("POS", 128, 16, i32), ("POSU", 128, 16, u16),
+    ("CV", 128, 10, u16), ("SV", 128, 32, u16), ("N77", 128, 16, f32), ("M10", 128, 32, f32),
     ("SI", 128, 16, i32), ("NP", 128, 16, i32), ("THI", 128, 1, i32), ("WTI", 128, 1, i32),
-    ("ZO", 128, 16, u16), ("PU", 128, 16, u16), ("NU", 128, 16, u16), ("A5", 128, 16, f32), ("SUM", 128, 16, i32),
+    ("NU", 128, 16, u16), ("A5", 128, 16, f32), ("SUM", 128, 16, i32),
     ("S15", 128, 16, i32), ("SU", 128, 16, u16), ("T1", 128, 16, i32), ("T2", 128, 16, i32), ("U7", 128, 16, i32), ("CU", 128, 16, u16),
-    ("CX", 128, 16, u16), ("NS", 128, 1, f32), ("NJ", 128, 16, f32), ("AT", 128, 1, bf), ("AR", 128, 1, f32), ("BC", 128, 1, f32),
+    ("CX", 128, 32, u16), ("AT", 128, 1, bf), ("AR", 128, 1, f32),
     ("XT", 128, 256, bf), ("XU", 128, 256, bf), ("YW", 128, 256, f32), ("FO", 128, 40, f32), ("YO", 128, 32, f32),
 ]}
 for _b in range(8):
     SCRATCH["B%d" % _b] = ("psum", [128, 512], f32)
-_ARR = ["%s%d" % (n, t) for n in ("Z", "H", "L", "W") for t in range(TV)] + ["LS"]
+_ARR = ["%s%d" % (n, t) for n in ("Z", "C", "H", "L", "W") for t in range(TV)] + ["LS"]
 _DMA = ["small", "sm2", "ls", "wd", "x", "sh", "oyx", "oyw", "oyn"]
 SEMAPHORES = ["qv", "qa", "qp", "qg", "loc"] + ["r" + n for n in _ARR] + ["d" + n for n in _DMA]
 
 
 def rank_program(g, core, T, topo):
-    rank = T.rank_of(core)
+    rank, N = T.rank_of(core), len(T.cores)
+
+    def helpers(r):
+        c, to = T.cores[r], T.cores[(r - 1) % N]
+        free = [h for h in topo.cores_of(c) if T.rank_of(h) is None and topo.may_write(h, to)]
+        return [[h for h in free if topo.die(h) == d][0] for d in (topo.die(c), 1 - topo.die(c))]
     if rank is None:
+        for r in range(N):
+            if core in helpers(r):
+                k, to = helpers(r).index(core), T.cores[(r - 1) % N]
+                rid, pid = topo.addr(to)[:2]
+                half = T.LSN[:, 512 * k:512 * k + 512]
+                g.wait_ge(T.sem.rLS, len(topo.engines(T.cores[r], core)) // 2)
+                g.remote_dma(half, half, T.sem.rLS, T.sem.loc, pid, rid, topo.mask(core, to))
+                g.wait_ge(T.sem.loc, len(topo.engines(core, to)))
         return
-    N = len(T.cores)
     nxt, prv = T.cores[(rank + 1) % N], T.cores[(rank - 1) % N]
     V, P, S = g.vector, g.tensor, g.scalar
     Q = {"v": V, "a": S, "p": P, "g": g, "s": g.sync}
@@ -60,6 +75,8 @@ def rank_program(g, core, T, topo):
                 continue
             if dma_:
                 val = tot[sem]
+            if sem == "q" + q:
+                val = max(val, tot[sem] - 1)
             Q[q].wait_ge(T.sem[sem], val)
             for s_, v_ in snap.items():
                 known[q][s_] = max(known[q].get(s_, 0), v_)
@@ -132,21 +149,21 @@ def rank_program(g, core, T, topo):
         g.remote_dma(out, in_, T.sem["r" + name], T.sem.loc, pid, rid, topo.mask(core, dst))
         note("g", "loc", len(topo.engines(core, dst)), [], [], [])
 
-    def arrive(name, src, key):
-        n = len(topo.engines(src, core))
-        tot["r" + name] = n
+    def arrive(name, senders, key):
+        tot["r" + name] = sum(len(topo.engines(c, core)) for c in senders)
         lastw[key] = [len(ops)]
-        ops.append(("r" + name, n, {}, False))
+        ops.append(("r" + name, tot["r" + name], {}, False))
 
     def iota(out, pat, base, cm, key, r=""):
         run("g", g.iota, out, pat, base, cm, w=key, r=r, allow_small_or_imprecise_dtypes=True)
 
     for t in range(TV):
-        arrive("Z%d" % t, prv, "ZM%d" % t)
+        arrive("Z%d" % t, [prv], "ZM%d" % t)
+        arrive("C%d" % t, [prv], "CM%d" % t)
         if t > 0:
             for n_ in "HLW":
-                arrive("%s%d" % (n_, t), prv, "%sM%d" % (n_, t))
-    arrive("LS", nxt, "LSN")
+                arrive("%s%d" % (n_, t), [prv], "%sM%d" % (n_, t))
+    arrive("LS", helpers((rank + 1) % N), "LSN")
 
     v(V.memset, T.THI[:], 0, w="THI")
     dma("small", T.SI[:], T.sd[:], w="SI")
@@ -156,201 +173,224 @@ def rank_program(g, core, T, topo):
     dma("ls", T.LS[:], T.ls[:], w="LS")
     dma("wd", T.WI[1:128, :], T.wd[0:127, :], w="WIa")
     dma("wd", T.WI[0:1, :], T.wd[0:1, :], w="WIb")
-    dma("x", T.X[:, 0:4096], T.x[:], w="X0 X1")
-    XK = "X0 X1 XD XE"
-    IDB = T.IDX[:, 8:136]
-    C = {n: T.COL[:, i:i + 1] for i, n in enumerate("p15 s8 n24 zb x16 lo sel h168 thx q1 q2 wts bw bl".split())}
-    C.update(m0=T.M01[:, 1:2], nz=T.M10[:, 1:2], hi=T.M10[:, 8:9])
+    dma("x", T.X[:, 0:4096], T.x[:], w="X0 X1 X2 X3")
+    XK = "X0 X1 X2 X3 XD XE"
+    IDB = T.IDX[:, 16:144]
+    C = {n: T.COL[:, i:i + 1] for i, n in enumerate("p15 s8 n24 lo sel h168 thx q1 q2 wts bw c0 q3 thy".split())}
+    C.update(m0=T.M01[:, 1:2], nz=T.M10[:, 1:2], hi=T.M10[:, 8:9], lo8=T.M01[:, 8:9])
+
+    def landing(u):
+        c = SW * u + (4096 if u == TV - 1 else 256) - 40
+        return T.SH[:, c:c + WW]
 
     def slot(u):
         k = "M" if u == 0 else "S"
-        return T["H" + k][:, 128 * u:128 * u + 128], T["LL" + k][:, 128 * u:128 * u + 128], T["W" + k][:, WW * u:WW * u + WW], k
+        return T["H" + k][:, 128 * u:128 * u + 128], T["LL" + k][:, 128 * u:128 * u + 128], T.WS[:, WW * u:WW * u + WW] if u else landing(0), k
 
-    def empty_rows():
-        act(T.MS[:], T.MT[:].indirect(T.NU[:]), r="MT NU", w="MS")
-
-    def words_in():
-        for b_ in (1, 0):
+    def lists(b_, src, stop):
+        for n_ in src:
             for w_ in range(2):
                 c = 128 * (2 * b_ + w_)
-                mm(B[2 - b_][:, 0:128], T.RA[:, c:c + 128], T.WN[:, w_:256:2], w_ == 0, b_ == 1 and w_ == 1, "WN RA%d%d" % (b_, w_), "B%d" % (2 - b_))
-        mm(B[3][:, 0:256], T.IZ[:], T.WN[:], True, False, "IZ WN", "B3")
+                mm(B[2 - b_][:, 0:128], T.RA[:, c:c + 128], T[n_][:, w_:256:2], (n_, w_) == (src[0], 0), stop and (n_, w_) == (src[-1], 1),
+                   "%s RA%d%d" % (n_, b_, w_), "B%d" % (2 - b_))
 
-    def high_out(u):
-        ts(slot(u)[0], B[1][:, 0:128], 2048, A.add, EMPTY, A.min, w="H%s%d" % (slot(u)[3], u), b="B1")
+    def list_out(b_, u):
+        ts(slot(u)[1 - b_], B[2 - b_][:, 0:128], 2048, A.add, EMPTY, A.min, w="%s%s%d" % ("LH"[b_], slot(u)[3], u), b="B%d" % (2 - b_))
 
-    def col_of_ls(u):
-        tt(T.T1[:], T.SI[:], T.SI[:], A.mult, r="SI", w="T1")
-        tt(T.U7[:], T.N77[:], T.SI[:], A.add, r="N77 SI", w="U7")
-        ts(T.T2[:], T.T1[:], 5, A.arith_shift_right, r="T1", w="T2")
+    def col_of_ls(u, *between):
         cp(T.SU[:], T.S15[:], r="S15", w="SU")
         act(T.MK[:], T.RR[:, 32:48].indirect(T.SU[:]), r="RR1 SU", w="MK")
-        tt(T.T1[:], T.T2[:], T.U7[:], A.add, r="T2 U7", w="T1")
+        tt(T.T1[:], T.SI[:], T.SI[:], A.mult, r="SI", w="T1")
         if u:
-            pop_at()
+            tt(T.U7[:], B[5][:, 16:32], T.SI[:], A.add, r="SI", w="U7", b="B5")
+        else:
+            tt(T.U7[:], T.N77[:], T.SI[:], A.add, r="N77 SI", w="U7")
+        ts(T.T2[:], T.T1[:], 5, A.arith_shift_right, r="T1", w="T2")
+        between[0]()
+        tt(T.T1[:], T.T2[:], T.U7[:], A.add, r="T2 U7", w="T1")
+        between[1]()
         ts(T.T2[:], T.T1[:], 1023, A.bitwise_and, r="T1", w="T2")
+        between[2]()
         cp(T.CU[:], T.T2[:], r="T2", w="CU")
 
-    def letters(ls):
-        tt(T.MM[:], T[ls][:].indirect(T.CU[:]), T.MK[:], A.mult, r=ls + " CU MK", w="MM")
+    def letters():
+        tt(T.MM[:], T.LSN[:].indirect(T.CU[:]), T.MK[:], A.mult, r="LSN CU MK", w="MM")
         for w_ in range(2):
-            mm(B[2][:, 0:128], T.EXT[:, 8 - 8 * w_:136 - 8 * w_], T.MM[:, w_:256:2], False, w_ == 1, "MM EXT", "B2")
+            mm(B[2][:, 0:128], T.EXT[:, 16 - 8 * w_:144 - 8 * w_], T.MM[:, w_:256:2], False, w_ == 1, "MM EXT", "B2")
 
-    def pop_at():
-        ts(T.PU[:], B[1][:, 128:144], -32768, A.add, w="PU", b="B1")
-
-    def low_out(u):
-        ts(T["W" + slot(u)[3]][:, WW * u + 264:WW * u + 280], T.SI[:], 5, A.mult, -16, A.add, r="SI", w="Ws%d" % u)
-        ts(slot(u)[1], B[2][:, 0:128], C["bl"], A.add, EMPTY, A.min, r="bl", w="L%s%d" % (slot(u)[3], u), b="B2")
+    def seeds_out(u):
+        ts(slot(u)[2][:, 8:24], T.SI[:], 5, A.mult, -16, A.add, r="SI", w="Ws%d" % u)
 
     def words_out(u):
-        mm(B[3][:, 0:256], T.EXT[:, 8:136], T.MM[:], False, True, "MM EXT", "B3")
-        act(T["W" + slot(u)[3]][:, WW * u:WW * u + 256], B[3][:, 0:256], F.Identity, bias=C["bw"], r="bw", w="Ww%d" % u, b="B3")
+        iz, ex = ("IZ", T.EXT[:, 16:144]) if u == TV - 1 else ("IZR", T.EXR[:])
+        mm(B[3][:, 0:256], T[iz][:], T.WN[:], True, u == 0, iz + " IZRa WN", "B3")
+        if u:
+            mm(B[3][:, 0:256], T[iz][:], T.WX[:], False, False, iz + " WX", "B3")
+            mm(B[3][:, 0:256], ex, T.MM[:], False, True, "MM EXT EXR", "B3")
+        act(slot(u)[2][:, 40:WW], B[3][:, 0:256], w="Ww%d" % u, b="B3")
 
     def wkey(u):
         return "WM%d" % u if u else "Ww0 Ws0 Wn0 Wz"
 
-    def build_sh(u):
-        lo, wk = WW * u, "WM%d" % u if u else "Ww0 X0"
-        for h in (8, 5, 3, 2, 1, 0):
-            c = 256 * (h or 16)
-            if u < TV - 1:
-                d = 17 - h
-                dma("sh", T.SH[d:128, c:c + 256], T.WM[0:128 - d, lo:lo + 256], r=wk, w="SA%d" % h)
-                dma("sh", T.SH[0:d, c:c + 256], T.WM[128 - d:128, lo:lo + 256], r=wk, w="SB%d" % h)
-            else:
-                dma("sh", T.SH[0:128 - h, c:c + 256], T.WM[h:128, lo:lo + 256], r=wk, w="SA%d SB%d" % (h, h))
-    shk = " ".join("SA%d SB%d" % (h, h) for h in (8, 5, 3, 2, 1, 0))
+    def copy(u, h):
+        c = SW * u + 256 * (h or 16)
+        return T.SH[:, c:c + 256]
+
+    def moved_by_dma(u):
+        wk, push = "WM%d" % u if u else "Ww0 X0", int(u < TV - 1)
+        for h in HS[:5 - push] + (0,) * push:
+            d = (h - push) % 128
+            dma("sh", copy(u, h)[0:128 - d, :], copy(u, push)[d:128, :], r=wk, w="SH%d" % h)
+            dma("sh", copy(u, h)[128 - d:128, :], copy(u, push)[0:d, :], r=wk, w="SH%da" % h)
+
+    def popped(u):
+        return T.SH[:, SW * u:SW * u + SW].indirect(T.OF[:, 16:32]), "OF SH0 SH0a SH1 SH1a SH2 SH2a SH3 SH3a SH5 SH5a SH8 SH8a " + wkey(u)
 
     iota(T.IP[:], [[0, 4]], 0, 1, "IP")
     iota(T.IS[:], [[1, 16]], 0, 16, "IS")
     iota(T.IU[:], [[1, 32]], 0, 0, "IU")
     iota(T.IG[:, 1:9], [[-16, 8]], 0, 1, "IGa")
     iota(T.IG[:, 0:1], [[1, 1]], -112, 1, "IGb")
-    iota(T.II[:], [[-1, 144]], 8, 1, "II")
+    iota(T.II[:], [[-1, 160]], 16, 1, "II")
     v(V.memset, T.D0[:], 1.0, w="D0")
     act(T.M1[:], T.D0[:], scale=-1.0, r="D0", w="M1")
     act(T.CQ[:], T.D0[:], scale=0.0, r="D0", w="CQ")
-    act(T.EXT[:], T.D0[:, 0:136], scale=0.0, r="D0", w="EXT")
+    act(T.EXF[:], T.D0[:, 0:144], scale=0.0, r="D0", w="EXF")
+    v(V.memset, T.LOW[:], -2048, w="LOW")
     v(V.memset, T.CP[:], 0.0, w="CP")
     v(V.memset, T.X[:, 4096:4112], 32.0, w="XE")
     v(V.memset, T.ONE[:], 1.0, w="ONE")
     v(V.memset, T.ZER[:], 0.0, w="ZER")
+    v(V.memset, T.ZR[:], 1.0, w="ZR")
     run("g", g.affine_select, T.DB[:, 0:HALF], T.M1[:], [[-16, 8], [0, NPL]], A.is_equal, 0.0, 0, 1, r="M1", w="DB")
-    iota(T.I9[:, 1:9], [[NPL, 8]], 28, 0, "I9a")
-    iota(T.I9[:, 0:10:9], [[0, 2]], 28 + 7 * NPL, 0, "I9b")
     iota(T.DB[:, 0:HALF:NPL], [[0, 8]], 0, 0, "DBa", r="DB")
     iota(T.DB[:, 20:HALF:NPL], [[0, 8]], 32768, 0, "DBb", r="DB")
     cq = {0: 64, 1: -16, 8: 24, 9: -24, 13: 27, 14: -27, 16: 29, 17: -29, 18: 30, 19: 1, 20: 1}
     for q_, c in cq.items():
         iota(T.CQ[:, q_:HALF:NPL], [[0, 8]], c, 0, "CQ%d" % q_, r="CQ")
-    send("LS", prv, T.LSN[:], T.LS[:], r="LS")
     cqk = "CQ " + " ".join("CQ%d" % q_ for q_ in cq)
-    ts(T.IQ[:, 0:1], T.IP[:, 0:1], 15, A.bitwise_and, r="IP", w="IQ0")
+    v(V.memset, T.ZR[:, 0:512:8], 0.0, w="ZR")
+    ts(T.IQ[:, 0:1], T.IP[:, 0:1], 15, A.bitwise_and, r="IP IU", w="IQ0")
     ts(T.POS[:], T.IS[:], 255, A.bitwise_and, r="IS", w="POS")
+    ts(T.IQ[:, 2:3], T.IP[:, 0:1], 7, A.bitwise_and, r="IP", w="IQ2")
+    ts(T.IQ[:, 1:2], T.IP[:, 0:1], 4, A.arith_shift_right, r="IP", w="IQ1")
     cp(C["p15"], T.IQ[:, 0:1], r="IQ0", w="p15")
     cp(T.POSU[:], T.POS[:], r="POS", w="POSU")
+    ts(T.IG[:, 0:9], T.IG[:, 0:9], 4, A.arith_shift_right, r="IGa IGb II", w="IG")
+    ts(T.IDX[:], T.II[:], 0, A.is_equal, r="II", w="IDX")
     ts(T.M01[:], T.IU[:], C["p15"], A.is_gt, r="IU p15", w="M01 m0")
     ts(T.M10[:], T.IU[:], C["p15"], A.is_le, r="IU p15", w="hi nz")
-    ts(T.MT[:], T.M01[:], -8192, A.mult, 6144, A.add, r="M01", w="MT")
-    ts(T.NU[:], T.NP[:], 1, A.add, 16, A.min, r="NP", w="NU")
     ts(T.RR[:, 32:48], T.IU[:, 0:16], C["p15"], A.is_equal, r="IU p15", w="RR1")
-    empty_rows()
-    ts(T.S15[:], T.SI[:], 15, A.bitwise_and, r="SI", w="S15")
-    ts(T.N77[:], T.NP[:], 77, A.mult, r="NP", w="N77")
-    ts(C["lo"], C["nz"], C["hi"], A.subtract, r="hi nz", w="lo")
-    ts(T.IDX[:], T.II[:], 0, A.is_equal, r="II", w="IDX")
-    for b_ in (1, 0):
-        if not b_:
-            col_of_ls(0)
-        for w_ in range(2):
-            c, o = 128 * (2 * b_ + w_), 8 + 8 * (b_ - w_)
-            act(T.RA[:, c:c + 128], T.IDX[:, o:o + 128], scale=C["hi" if b_ else "lo"], r="IDX hi lo", w="RA%d%d" % (b_, w_))
-    ts(T.IG[:, 0:9], T.IG[:, 0:9], 4, A.arith_shift_right, r="IGa IGb", w="IG")
-    ts(T.IQ[:, 2:3], T.IP[:, 0:1], 7, A.bitwise_and, r="IP", w="IQ2")
     ts(T.KF[:, 0:9], T.IG[:, 0:9], 0, A.is_equal, r="IG", w="KF")
-    ts(C["wts"], T.WTI[:], 2.0 ** -22, A.mult, r="WTI", w="wts")
-    cp(T.EXT[:, 8:136:16], T.KF[:, 1:9], r="KF", w="EXT")
-    ts(C["bl"], T.IQ[:, 2:3], 0, A.is_gt, 2048, A.mult, r="IQ2", w="bl")
-    ts(T.WM[:, 280:296], T.NU[:], -1, A.mult, 16, A.add, r="NU", w="Wn0")
+    for b_ in (1, 0):
+        for w_ in range(2):
+            c, o = 128 * (2 * b_ + w_), 16 + 8 * (b_ - w_)
+            act(T.RA[:, c:c + 128], T.IDX[:, o:o + 128], scale=C["hi" if b_ else "lo8"], r="IDX hi M01", w="RA%d%d" % (b_, w_))
+    ts(T.S15[:], T.SI[:], 15, A.bitwise_and, r="SI", w="S15")
+    ts(T.NU[:], T.NP[:], 1, A.add, 16, A.min, r="NP", w="NU")
+    ts(T.N77[:], T.NP[:], 77, A.mult, r="NP", w="N77")
+    ts(T.MT[:], T.M01[:], -EMPTY, A.mult, EMPTY - 2048, A.add, r="M01", w="MT")
+    cp(T.EXF[:, 16:144:16], T.KF[:, 1:9], r="KF", w="EXF")
+    col_of_ls(0, lambda: ts(C["q1"], T.IP[:, 0:1], 1, A.is_equal, 2.0 ** -5, A.mult, r="IP", w="q1"),
+              lambda: ts(C["q2"], T.IP[:, 0:1], 2, A.is_equal, 2.0 ** -22, A.mult, r="IP", w="q2"),
+              lambda: ts(C["bw"], C["m0"], -2048, A.mult, r="m0", w="bw"))
+    act(T.MS[:], T.MT[:].indirect(T.NU[:]), r="MT NU", w="MS")
     act(T.IZ[:], IDB, scale=C["nz"], r="IDX nz", w="IZ")
-    for h in HS:
-        act(T.CP[:, 1 + BASE[h]:169:NPL], T.KF[:, 1:9], scale=-1.0, r="KF CP", w="CP%d" % h)
-    cpk = "CP " + " ".join("CP%d" % h for h in HS)
-    ts(C["q1"], T.IP[:, 0:1], 1, A.is_equal, 2.0 ** -5, A.mult, r="IP", w="q1")
-    ts(C["q2"], T.IP[:, 0:1], 2, A.is_equal, 2.0 ** -22, A.mult, r="IP", w="q2")
-    ts(C["s8"], C["p15"], 8, A.add, r="p15", w="s8")
+    ts(C["wts"], T.WTI[:], 2.0 ** -22, A.mult, r="WTI", w="wts")
     ts(C["thx"], T.THI[:], C["q1"], A.add, C["q2"], A.add, r="THI q1 q2", w="thx")
-    ts(C["q1"], C["q1"], C["q2"], A.add, 0, A.is_gt, r="q1 q2", w="q1")
-    ts(C["n24"], C["p15"], 24, A.add, r="p15", w="n24")
-    tt(T.WN[:], T.WI[:].indirect(T.POSU[:]), T.MS[:], A.add, r="WIa WIb POSU MS", w="WN")
-    words_in()
-    letters("LS")
-    high_out(0)
-    act(T.THL[:], T.ONE[:], scale=C["thx"], r="ONE thx", w="THL")
-    act(T.DB[:, HALF:336], T.CQ[:], scale=C["q1"], r="q1 " + cqk, w="DBc")
+    ts(C["q3"], C["q1"], C["q2"], A.add, 0, A.is_gt, r="q1 q2", w="q3")
     for k_, sc in (("KN", -1.0), ("K2", 2.0), ("KB", 1.0)):
-        act(T[k_][:], T.KF[:, 1:9], scale=sc, r="KF", w=k_)
-    ts(C["bw"], C["nz"], 2048, A.mult, r="nz", w="bw")
+        ts(T[k_][:], T.KF[:, 1:9], sc, A.mult, r="KF", w=k_)
+    need("g", deps_of("g", ["LS", "LOW"], [], []))
+    en, to = topo.engines(core, helpers(rank)[0]), [topo.addr(h) for h in helpers(rank)]
+    g.remote_dma_fused([RemoteDMATransfer(dst_ids=[DstId(rid=to[k_ // 2][0], pnc=to[k_ // 2][1])], dma_engine_mask=sum(1 << e for e in en[k_::4]),
+                                          remote_sem=T.sem.rLS, srcs=[T.LS[:, 256 * k_:256 * k_ + 256], T.LOW[:]],
+                                          dsts=[T.LSN[:, 256 * k_:256 * k_ + 256]], alu_op=1) for k_ in range(4)], local_sem=T.sem.loc)
+    note("g", "loc", len(en), [], [], [])
+    tt(T.MF[:], T.LS[:].indirect(T.CU[:]), T.MK[:], A.mult, r="LS CU MK", w="MF")
+    tt(T.WN[:], T.WI[:].indirect(T.POSU[:]), T.MS[:], A.add, r="WIa WIb POSU MS", w="WN")
+    mm(B[3][:, 0:256], T.EXF[:, 16:144], T.MF[:], True, False, "MF EXF", "B3")
+    mm(B[3][:, 0:256], T.IZ[:], T.WN[:], False, True, "IZ WN", "B3")
+    act(T.THL[:], T.ONE[:], scale=C["thx"], r="ONE thx", w="THL")
+    act(T.DB[:, HALF:336], T.CQ[:], scale=C["q3"], r="q3 " + cqk, w="DBc")
+    act(T.IZR[:, 16:128], T.IDX[:, 16:128], r="IDX", w="IZRa")
+    act(T.IZR[:, 0:16], T.IDX[:, 128:144], r="IDX", w="IZR")
     ts(T.WP[:], T.KF[:, 1:9], C["wts"], A.mult, r="KF wts", w="WP")
     ts(T.WQ[:], T.KF[:, 1:9], C["wts"], A.mult, -1, A.mult, r="KF wts", w="WQ")
-    ts(T.SV[:, 0:8], T.KF[:, 0:8], C["s8"], A.mult, r="KF s8", w="SV0a")
-    ts(T.SV[:, 8:16], T.KF[:, 0:8], C["n24"], A.mult, r="KF n24", w="SV0b")
-    low_out(0)
+    ts(T.WN[:], B[3][:, 0:256], C["bw"], A.add, r="bw", w="WN", b="B3")
+    lists(1, ["WN"], True)
+    lists(0, ["WN"], True)
     words_out(0)
-    build_sh(0)
-    ts(T.IQ[:, 1:2], T.IP[:, 0:1], 4, A.arith_shift_right, r="IP", w="IQ1")
+    moved_by_dma(0)
+    ts(T.NIB[:], IDB, -1, A.mult, r="IDX", w="NIB")
+    for h in HS:
+        ts(T.CP[:, 1 + BASE[h]:169:NPL], T.KF[:, 1:9], -1, A.mult, r="KF CP", w="CP%d" % h)
+    cpk = "CP " + " ".join("CP%d" % h for h in HS)
+    list_out(1, 0)
+    list_out(0, 0)
+    act(T.EXT[:], T.EXF[:], r="EXF", w="EXT")
+    for c, sc, k_ in ((48, 2.0 ** -12, "RR4"), (64, -1.0, "RR5")):
+        act(T.RR[:, c:c + 16], T.RR[:, 32:48], scale=sc, r="RR1", w=k_)
+    iota(T.I9[:, 1:9], [[NPL, 8]], 28, 0, "I9a")
+    iota(T.I9[:, 0:10:9], [[0, 2]], 28 + 7 * NPL, 0, "I9b")
+    ts(C["s8"], C["p15"], 8, A.add, r="p15", w="s8")
+    ts(C["n24"], C["p15"], 24, A.add, r="p15", w="n24")
     ts(C["h168"], C["hi"], HALF, A.mult, r="hi", w="h168")
     tt(C["sel"], T.IQ[:, 1:2], T.IQ[:, 2:3], A.is_equal, r="IQ1 IQ2", w="sel")
-    cp(T.POSB[:], T.POS[:], r="POS", w="POSB")
-    ts(T.CV[:], T.I9[:], C["h168"], A.add, C["sel"], A.mult, r="I9a I9b h168 sel", w="CV")
+    ts(landing(0)[:, 24:40], T.NU[:], -1, A.mult, 16, A.add, r="NU", w="Wn0")
+    seeds_out(0)
+    ts(T.SV[:, 0:8], T.KF[:, 0:8], C["s8"], A.mult, r="KF s8", w="SV0a")
+    ts(T.SV[:, 8:16], T.KF[:, 0:8], C["n24"], A.mult, r="KF n24", w="SV0b")
+    ts(T.OB[:, 0:16], T.POS[:], 8, A.mult, r="POS", w="OBa")
+    cp(T.OB[:, 16:32], T.POS[:], r="POS", w="POSB")
+    ts(T.MX2[:, 0:16], T.IU[:, 0:16], C["p15"], A.add, 17, A.is_ge, r="IU p15", w="MX2")
+    for c, sc, k_ in ((80, -77.0, "RR6"), (0, 2.0 ** 22, "RR2")):
+        ts(T.RR[:, c:c + 16], T.RR[:, 32:48], sc, A.mult, r="RR1", w=k_)
+    for c, sc in ((16, 256), (32, 1), (48, -1), (64, -77)):
+        ts(T.RB[:, c:c + 16], T.RR[:, 32:48], sc, A.mult, r="RR1", w="RB%d" % c)
 
     def diagonal(out, n, base, val, key):
         run("g", g.affine_select, out, T.ZER[:, 0:n], [[-1, n]], A.not_equal, val, base, 1, r="ZER", w=key)
-    diagonal(T.NIB[:], 128, 0, -1.0, "NIB")
-    iota(T.ZR[:], [[0, 512]], 1, 0, "ZR")
-    iota(T.ZR[:, 0:512:8], [[0, 64]], 0, 0, "ZR")
-    iota(T.WM[:, 256:264], [[0, 8]], 0, 0, "Wz")
+    iota(landing(0)[:, 0:8], [[0, 8]], 0, 0, "Wz")
     for q_ in (0, 1, 9, 14, 17, 19):
-        iota(T.D0[:, q_:HALF:NPL], [[0, 8]], 0, 0, "D0%d" % q_, r="M1 CQ EXT")
+        iota(T.D0[:, q_:HALF:NPL], [[0, 8]], 0, 0, "D0%d" % q_, r="M1 CQ EXF")
     d0k = "D0 " + " ".join("D0%d" % q_ for q_ in (0, 1, 9, 14, 17, 19))
-    iota(T.ZROW[0:32, 0:16], [[0, 16]], 144, 0, "ZROW")
-    iota(T.ZROW[0:32, 16:32], [[8, 16]], 0, 0, "ZROWd")
+    for k_, (a, b_) in enumerate(((1024, 16), (77 * 1024, 77 * 16), (-1024, -1), (-1024 * 256, 0), (-1024, 0))):
+        iota(T.ZROW[0:2, 16 * k_:16 * k_ + 16], [[0, 16]], a, b_ - a, "ZROW%d" % k_)
+    iota(T.OB[:, 32:48], [[0, 16]], 0, 0, "OBz")
+    iota(T.MX2[:, 16:32], [[0, 16]], 0, 0, "MXz")
     iota(T.U[:, 0:8], [[0, 8]], 0, 0, "Uz")
     iota(T.ZC[:, 2048:2064], [[0, 16]], 0, 0, "ZCz")
-    diagonal(T.I256[:], 128, 0, 256.0, "I256")
+    diagonal(T.J77[:], 128, 0, 77 / 256, "J77")
     diagonal(T.J256[:], 128, 0, 1 / 256, "J256")
+    iota(T.IA[:, 0:16], [[256, 16]], 0, 0, "IA0")
+    iota(T.IA[:, 16:32], [[0, 4], [256, 4]], 0, 0, "IA1")
     diagonal(T.ROT[:, 0:112], 112, -16, 1.0, "ROTa")
     diagonal(T.ROT[:, 112:128], 16, 0, 1.0, "ROTb")
-
-    def iotas_between():
-        iota(T.IA[:], [[256, 16]], 0, 0, "IA")
-        iota(T.X[:, 4112:8192:16], [[0, 255]], 0, 0, "XD")
-        iota(T.NEG[:], [[0, 256]], -128, 0, "NEG")
-        iota(T.WS[:, WW + 256:WW + 264], [[0, 8]], 0, 0, "Wz1")
+    iota(T.EXR[:], [[0, 128]], 0, 0, "EXR")
+    iota(T.X[:, 4112:8192:16], [[0, 255]], 0, 0, "XD")
+    iota(T.NEG[:], [[0, 256]], -128, 0, "NEG")
+    for u in range(1, TV):
+        iota(T.WS[:, WW * u:WW * u + 8], [[0, 8]], 0, 0, "Wz%d" % u)
+    iota(T.FO[:, 0:8], [[0, 8]], 0, 0, "FOz")
 
     def late_consts():
-        for c, sc, k_ in ((48, 2.0 ** -12, "RR4"), (64, -1.0, "RR5"), (16, 32.0, "RR3"), (0, 2.0 ** 22, "RR2")):
-            act(T.RR[:, c:c + 16], T.RR[:, 32:48], scale=sc, r="RR1", w=k_)
-        act(C["zb"], C["p15"], F.Identity, scale=128.0, bias=-1.0, r="p15", w="zb")
-
-    def iotas_after():
-        for u in range(2, TV):
-            iota(T.WS[:, WW * u + 256:WW * u + 264], [[0, 8]], 0, 0, "Wz%d" % u)
-        iota(T.IL[:], [[0, 2], [256, 8]], 0, 0, "IL")
-        iota(T.FO[:, 0:8], [[0, 8]], 0, 0, "FOz")
+        act(C["lo"], C["lo8"], F.Identity, scale=C["nz"], r="M01 nz", w="lo")
+        act(C["c0"], C["p15"], scale=16.0, r="p15", w="c0")
+        act(T.IZR[:], T.IZR[:], scale=C["nz"], r="nz IZRa", w="IZR")
 
     def later_consts(t):
         if t == 0:
-            act(C["x16"], C["p15"], scale=16.0, r="p15", w="x16")
-            act(T.BA[:], T.IA[:], F.Identity, bias=C["x16"], r="IA x16", w="BA")
+            ts(T.RA[:, 0:256], T.RA[:, 0:256], C["lo"], A.mult, r="lo", w="RA00 RA01")
+            ts(C["thy"], C["m0"], -2048, A.mult, C["thx"], A.add, r="m0 thx", w="thy")
+            ts(T.M0B[:], T.ONE[:], C["m0"], A.mult, r="ONE m0", w="M0B")
+            cp(T.EXR[:, 0:128:16], T.KF[:, 0:8], r="KF", w="EXR")
+            act(T.BA[:, 0:32], T.IA[:, 0:32], F.Identity, bias=C["c0"], r="IA0 IA1 c0", w="BA0")
         if t == 1:
-            act(T.BS[:], T.POSB[:], scale=16.0, r="POSB", w="BS")
+            act(T.BA[:, 32:48], T.OB[:, 16:32], scale=16.0, r="POSB", w="BA1")
         if t == 2:
             ts(T.SV[:, 16:24], T.KF[:, 1:9], C["s8"], A.mult, r="KF s8", w="SV16a")
             ts(T.SV[:, 24:32], T.KF[:, 1:9], C["n24"], A.mult, r="KF n24", w="SV16b")
-        if t == 3:
-            act(T.BL[:], T.IL[:], F.Identity, bias=C["x16"], r="IL x16", w="BL")
 
     PD, PC = 0, HALF
 
@@ -366,9 +406,7 @@ def rank_program(g, core, T, topo):
         return 2, 256 * hf + 128 * (j - 6)
 
     def bulk(t):
-        win = T.X[:, 0:4112]
-        xk = "X0 X1 XE "
-        Hl, Ll = T.HM[:, 128 * t:128 * t + 128], T.LLM[:, 128 * t:128 * t + 128]
+        win, xk = T.X[:, 0:4112], "X0 X1 X2 X3 XE "
 
         def gather(q, buf, lk, c, n, key):
             off = T[lk][:, 128 * t + c // 16:128 * t + (c + n) // 16]
@@ -382,7 +420,7 @@ def rank_program(g, core, T, topo):
         gl = ("GL0a GL0b", "GL1a GL1b")
         gh = ("GH0a GH0b", "GH1a GH1b")
         for bk in (1, 2, 3):
-            mm(B[bk][:, 0:512], T.ZER[0:1, :], (T.ZR if t else T.X)[0:1, 0:512], True, False, "ZER ZR" if t else "ZER X0", "B%d" % bk)
+            mm(B[bk][:, 0:512], T.ZER[0:1, :], T.ZR[0:1, 0:512], True, False, "ZER ZR", "B%d" % bk)
         for hf in range(2):
             mm(B[6 + hf][:, 0:336], T.THL[:], T.DB[:], True, False, "THL DB DBa DBb DBc", "B%d" % (6 + hf))
 
@@ -490,60 +528,77 @@ def rank_program(g, core, T, topo):
                 add_sizes(1, range(2, 6))
             add(1, *p_, stop=i == len(MAXED) - 1)
         o = 16 if t == TV - 1 else 0
-        act(T.ES[:], T.WM[:, WW * t + 256:WW * t + WW].indirect(T.SV[:, o:o + 16]), r=wkey(t) + " SV%da SV%db" % (o, o), w="ES")
+        act(T.ES[:], landing(t)[:, 0:40].indirect(T.SV[:, o:o + 16]), r=wkey(t) + " SV%da SV%db" % (o, o), w="ES")
 
     def decode(t):
         last = t == TV - 1
         nh, c0 = T.NH[:], ZW * t
+        mm(B[0][:, 0:48], T.ONE[0:2, :], T.ZROW[0:2, 32:80], True, False, "ONE ZROW2 ZROW3 ZROW4", "B0")
+        mm(B[0][:, 0:48], IDB, T.OB[:, 0:48], False, False, "IDX OBa POSB OBz", "B0")
+        mm(B[5][:, 0:32], T.ONE[0:2, :], T.ZROW[0:2, 0:32], True, False, "ONE ZROW0 ZROW1", "B5")
         mm(B[4][:, 16:32], T.ES[:, 0:128], T.RR[:, 48:64], True, True, "ES RR4", "B4")
-        mm(B[5][:, 0:16], T.ONE[0:1, :], T.ZROW[0:1, 0:16], True, False, "ONE ZROW", "B5")
-        mm(B[5][:, 0:16], T.ES[:, 128:256], T.RR[:, 64:80], False, False, "ES RR5", "B5")
-        mm(B[0][:, 0:16], T.ONE[0:1, :], T.ZROW[0:1, 16:32], True, False, "ONE ZROWd", "B0")
-        mm(B[1][:, 128:144], IDB, T.POSB[:], True, False, "IDX POSB", "B1")
+        mm(B[5][:, 0:32], T.ES[:, 128:256], T.RR[:, 64:96], False, False, "ES RR5 RR6", "B5")
         for hf in range(2):
             c, bk = HALF * hf, "B%d" % (6 + hf)
             v(V.tensor_tensor_scan, T.S1[:, c:c + HALF], T.D0[:], B[6 + hf][:, 0:HALF], 0.0, A.mult, A.max, r=d0k, w="S1%d" % hf, b=bk)
+            if t == 0 and hf == 0:
+                ts(T.CV[:], T.I9[:], C["h168"], A.add, C["sel"], A.mult, r="I9a I9b h168 sel", w="CV")
         for hf in range(2):
             c, bk = HALF * hf, "B%d" % (6 + hf)
-            v(V.tensor_tensor_scan, T.U[:, 8 + c:8 + c + HALF], B[6 + hf][:, HALF:336], T.S1[:, c:c + HALF], 0.0, A.add, A.min, r="S1%d" % hf, w="U%d" % hf, b=bk)
-        cp(T.E[:], T.U[:].indirect(T.CV[:, 0:9]), r="U0 U1 Uz CV", w="E")
+            v(V.tensor_tensor_scan, T.U[:, 8 + c:8 + c + HALF], B[6 + hf][:, HALF:336], T.S1[:, c:c + HALF], 0.0, A.add, A.min,
+              r="S1%d" % hf, w="U%d" % hf, b=bk)
+        ts(T.E2[:], T.U[:].indirect(T.CV[:, 0:9]), 32, A.mult, 127.77, A.add, r="U0 U1 Uz CV", w="E2")
+        act(T.E[:], T.U[:].indirect(T.CV[:, 0:9]), r="U0 U1 Uz CV", w="E")
         o = 16 if last else 0
-        mm(B[0][:, 0:16], T.E[:, 16:144], T.RR[:, 16:32], False, True, "E RR3", "B0")
+        mm(B[0][:, 0:16], T.E2[:, 16:144], T.RB[:, 32:48], False, False, "E2 RB32", "B0")
+        mm(B[0][:, 16:48], T.E2[:, o:o + 128], T.RB[:, 16:48], False, True, "E2 RB16 RB32", "B0")
         mm(B[4][:, 0:16], T.E[:, o:o + 128], T.RR[:, 0:16], True, True, "E RR2", "B4")
-        ts(T.ZO[:], B[0][:, 0:16], C["zb"], A.add, r="zb", w="ZO", b="B0")
-        act(T.ZS[:, c0:c0 + 256], T.ZC[:].indirect(T.ZO[:]), r="ZC00 ZC01 ZC10 ZC11 ZCz ZO", w="Za")
+        mm(B[5][:, 0:32], T.E2[:, o:o + 128], T.RB[:, 48:80], False, False, "E2 RB48 RB64", "B5")
+        cp(T.OF[:], B[0][:, 0:48], w="OF", b="B0")
+        act(T.ZS[:, c0:c0 + 256], T.ZC[:].indirect(T.OF[:, 0:16]), F.Identity, scale=0.5, bias=96.0, r="ZC00 ZC01 ZC10 ZC11 ZCz OF", w="Za")
+        cp(T.T1[:], B[4][:, 0:16], w="T1", b="B4")
         ts(nh, B[4][:, 0:16], 1 << 21, A.is_ge, 4096, A.mult, w="NH", b="B4")
-        ts(T.HB[:], B[4][:, 0:16], 2.0 ** -17, A.mult, 127.77, A.add, w="HB", b="B4")
-        mm(B[1][:, 128:144], T.I256[:], T.HB[:], False, True, "I256 HB", "B1")
-        mm(B[5][:, 0:16], T.NIB[:], T.HB[:], False, False, "NIB HB", "B5")
-        mm(B[5][:, 0:16], T.J256[:], nh, False, True, "J256 NH", "B5")
+        ts(T.T2[:], T.T1[:], 15 + (1 << 21), A.bitwise_and, r="T1", w="T2")
+        mm(B[5][:, 0:16], T.J256[:], nh, False, False, "J256 NH", "B5")
+        mm(B[5][:, 16:32], T.J77[:], nh, False, True, "J77 NH", "B5")
         tt(T.A5[:], B[4][:, 16:32], nh, A.mult, r="NH", w="A5", b="B4")
+        ts(T.ZS[:, c0 + 256:c0 + ZW], T.T2[:], 4096, A.min, r="T2", w="Zb")
+        send("C%d" % t, nxt, T.ZM[:, c0 + 256:c0 + ZW], T.ZS[:, c0 + 256:c0 + ZW], r="Zb")
+        send("Z%d" % t, nxt, T.ZM[:, c0:c0 + 256], T.ZS[:, c0:c0 + 256], r="Za")
         tt(T.SUM[:], B[4][:, 0:16], T.A5[:], A.add, r="A5", w="SUM", b="B4")
+        if not last:
+            ts(T.S15[:], T.SUM[:], 15, A.bitwise_and, r="SUM", w="S15")
+        ts(T.SI[:], T.SUM[:], 4095, A.bitwise_and, r="SUM", w="SI")
         if last:
+            act(T.MF[:], popped(t)[0], F.Identity, bias=2048.0, r=popped(t)[1], w="MF")
             cp(T.NU[:], B[5][:, 0:16], w="NU", b="B5")
+            cp(T.FO[:, 24:40], B[5][:, 0:16], w="FOn", b="B5")
+            cp(T.FO[:, 8:24], T.SI[:], r="SI", w="FOs")
             act(T.MS[:], T.M01[:].indirect(T.NU[:]), r="M01 NU", w="MS")
         else:
-            ts(T.NU[:], B[5][:, 0:16], 1, A.add, 16, A.min, w="NU", b="B5")
-            act(T.N77[:], B[5][:, 0:16], scale=77.0, w="N77", b="B5")
-            empty_rows()
-        ts(T.S15[:], T.SUM[:], 15, A.bitwise_and, r="SUM", w="S15")
-        ts(T.SI[:], T.SUM[:], 4095, A.bitwise_and, r="SUM", w="SI")
-        tt(T.ZS[:, c0 + 256:c0 + ZW], T.S15[:], nh, A.max, r="S15 NH", w="Zb")
-        send("Z%d" % t, nxt, T.ZM[:, c0:c0 + ZW], T.ZS[:, c0:c0 + ZW], r="Za Zb")
-        if last:
-            pop_at()
+            for i in range(16):
+                mm(B[6][:, 0:1], T.ONE[:], T.NH[:, i:i + 1], i == 0, i == 15, "ONE NH", "B6")
+            act(T.WN[:], popped(t)[0], r=popped(t)[1], w="WN")
 
-    def columns(t, base):
-        rot, rk = (IDB, "IDX") if t == TV - 1 else (T.ROT[:], "ROTa ROTb")
-        mm(B[4][:, 32:48], IDB, T[base][:], True, False, "IDX " + base, "B4")
-        mm(B[4][:, 32:48], rot, T.ZM[:, ZW * t + 256:ZW * t + ZW], False, True, "ZM%d %s" % (t, rk), "B4")
-        cp(T.CX[:], B[4][:, 32:48], w="CX", b="B4")
+    def columns(t):
+        tail, n = T.ZM[:, ZW * t + 256:ZW * t + ZW], 2 if t == TV - 1 else 1
+        for k_ in range(n):
+            c = 32 if t % 2 else 16 * k_
+            mm(B[4][:, 32 + 16 * k_:48 + 16 * k_], IDB, T.BA[:, c:c + 16], True, False, "IDX BA%d" % (t % 2), "B4")
+            mm(B[4][:, 32 + 16 * k_:48 + 16 * k_], IDB if n == 2 else T.ROT[:], tail, False, True, "CM%d IDX ROTa ROTb" % t, "B4")
 
-    def xupdate(m, e0, e1, lo, xk):
-        win, cols = T.X[:, lo:8192], T.CX[:, e0 // 16:e1 // 16]
-        tt(T.XT[:, e0:e1], win.indirect(cols), T.ZM[:, ZW * m + e0:ZW * m + e1], A.add, r="ZM%d CX %s" % (m, xk), w="XT")
-        ts(T.XU[:, e0:e1], T.XT[:, e0:e1], 0.5, A.mult, 127.75, A.add, r="XT", w="XU")
-        tt(win.indirect(cols), T.XU[:, e0:e1], T.NEG[:, e0:e1], A.add, r="XU NEG CX", w=xk)
+    def columns_out(n):
+        cp(T.CX[:, 0:n], B[4][:, 32:32 + n], w="CX", b="B4")
+
+    def halves(ea):
+        act(T.XT[:, 0:ea], T.X[:].indirect(T.CX[:, 0:ea // 16]), F.Identity, scale=0.5, bias=31.75, r="CX " + XK, w="XTa")
+        ts(T.XT[:, ea:256], T.X[:].indirect(T.CX[:, ea // 16:16]), 0.5, A.mult, 31.75, A.add, r="CX " + XK, w="XTb")
+
+    def means(m):
+        v(V.tensor_tensor_scan, T.XU[:], T.XT[:], T.ZM[:, ZW * m:ZW * m + 256], 255.0, A.min, A.add, r="XTa XTb ZM%d" % m, w="XU")
+
+    def change(e0, e1, lo, cols, xk):
+        tt(T.X[:, lo:8192].indirect(T.CX[:, cols + e0 // 16:cols + e1 // 16]), T.XU[:, e0:e1], T.NEG[:, e0:e1], A.add, r="XU NEG CX", w=xk)
 
     for t in range(TV):
         bulk(t)
@@ -553,47 +608,46 @@ def rank_program(g, core, T, topo):
         if t == TV - 1:
             break
         u = t + 1
-        if t == 0:
-            iotas_between()
-        mm(B[0][:, 32:48], T.ONE[:], T.NH[:], True, True, "ONE NH", "B0")
-        col_of_ls(u)
-        tt(T.WN[:], T.SH[:].indirect(T.PU[:]), T.MS[:], A.add, r="PU MS " + shk, w="WN")
-        words_in()
-        letters("LSN")
-        high_out(u)
+        act(T.WX[:], T.MX2[:].indirect(T.OF[:, 32:48]), scale=8192.0, r="MX2 MXz OF", w="WX")
+        col_of_ls(u, lambda: later_consts(t), lambda: None, lambda: seeds_out(u))
+        lists(1, ["WN", "WX"], True)
+        lists(0, ["WN"], False)
+        list_out(1, u)
         send("H%d" % u, nxt, T.HM[:, 128 * u:128 * u + 128], slot(u)[0], r="HS%d" % u)
-        act(T.WS[:, WW * u + 280:WW * u + WW], B[5][:, 0:16], F.Relu, scale=-1.0, bias=15.0, w="Wn%d" % u, b="B5")
-        act(T.NJ[:], B[0][:, 32:48], F.Identity, scale=-2.0 ** -12, bias=-128.0, accum_out=T.NS[:], w="NS", b="B0")
-        act(T.AT[:], T.NS[:], F.Identity, scale=-1 / 16, bias=0.47, r="NS", w="AT")
-        act(T.AR[:], T.AT[:], F.Identity, scale=16.0, bias=T.NS[:], r="AT NS", w="AR")
-        act(T.BC[:], T.AR[:], F.Identity, scale=C["m0"], bias=C["thx"], r="AR m0 thx", w="BC")
-        act(T.THL[:], T.ONE[:], scale=T.BC[:], r="ONE BC", w="THL")
-        later_consts(t)
-        low_out(u)
+        columns(t)
+        letters()
+        act(T.WS[:, WW * u + 24:WW * u + 40], B[5][:, 0:16], F.Relu, scale=-1.0, bias=15.0, w="Wn%d" % u, b="B5")
+        act(T.AT[:], B[6][:, 0:1], F.Identity, scale=2.0 ** -12, bias=2055.52, w="AT", b="B6")
+        columns_out(16)
+        halves(128)
+        list_out(0, u)
         send("L%d" % u, nxt, T.LLM[:, 128 * u:128 * u + 128], slot(u)[1], r="LS%d" % u)
-        columns(t, "BS" if t % 2 else "BA")
         words_out(u)
-        send("W%d" % u, nxt, T.WM[:, WW * u:WW * u + WW], slot(u)[2], r="Ww%d Ws%d Wn%d Wz%d" % (u, u, u, u))
-        build_sh(u)
-        if t == 0:
-            iotas_after()
-        xupdate(t, 0, 256, 0, XK)
+        send("W%d" % u, nxt, landing(u), slot(u)[2], r="Ww%d Ws%d Wn%d Wz%d" % (u, u, u, u))
+        act(T.AR[:], B[6][:, 0:1], F.Identity, scale=-2.0 ** -12, bias=T.AT[:], r="AT", w="AR", b="B6")
+        act(T.THL[:], T.M0B[:], F.Identity, scale=T.AR[:], bias=C["thy"], r="M0B AR thy", w="THL")
+        means(t)
+        change(0, 256, 0, 0, XK)
+        moved_by_dma(u)
 
-    tt(T.YW[:], T.SH[:].indirect(T.PU[:]), T.MS[:], A.mult, r="PU MS " + shk, w="YW")
-    dma("oyw", T.yw[:], T.YW[:], r="YW")
-    cp(T.FO[:, 8:24], T.SI[:], r="SI", w="FOs")
-    cp(T.FO[:, 24:40], B[5][:, 0:16], w="FOn", b="B5")
     act(T.ES[:], T.FO[:].indirect(T.SV[:, 16:32]), r="FOz FOs FOn SV16a SV16b", w="ES")
     for k_ in range(2):
         mm(B[1][:, 16 * k_:16 * k_ + 16], T.ES[:, 128 * k_:128 * k_ + 128], T.RR[:, 32:48], True, True, "ES RR1", "B1")
+    tt(T.YW[:], T.MF[:], T.MS[:], A.mult, r="MF MS", w="YW")
+    dma("oyw", T.yw[:], T.YW[:], r="YW")
     act(T.YO[:], B[1][:, 0:32], w="YO", b="B1")
-    dma("oyn", T.ys[:], T.YO[:, 0:16], r="YO", q="a")
-    dma("oyn", T.yn[:], T.YO[:, 16:32], r="YO", q="a")
-    columns(TV - 1, "BL")
-    for k_ in range(2):
-        lo = 2048 * k_
-        xupdate(TV - 1, 128 * k_, 128 * k_ + 128, lo, "X1 XD XE" if k_ else XK)
-        dma("oyx", T.yx[:, lo:lo + 2048], T.X[:, lo:lo + 2048], r="X%d" % k_)
+    dma("oyn", T.ys[:], T.YO[:, 0:16], r="YO")
+    dma("oyn", T.yn[:], T.YO[:, 16:32], r="YO")
+    columns(TV - 1)
+    columns_out(32)
+    halves(128)
+    means(TV - 1)
+    for k_ in range(4):
+        lo = 1024 * k_
+        change(64 * k_, 64 * k_ + 64, lo, 16, " ".join("X%d" % i for i in range(k_, 4)) + " XD XE")
+        if k_ != 2:
+            lo = min(lo, 2048)
+            dma("oyx", T.yx[:, lo:1024 * k_ + 1024], T.X[:, lo:1024 * k_ + 1024], r="X%d X%d" % (lo // 1024, k_))
     for sem, n in tot.items():
         if known["g"].get(sem, 0) < n:
             g.wait_ge(T.sem[sem], n)

from concourse.bass import DstId, RemoteDMATransfer
from concourse.mybir import AluOpType as A, ActivationFunctionType as F

HS = (8, 5, 3, 2, 1)
BASE = {8: 1, 5: 9, 3: 14, 2: 17, 1: 19}
NPL, HALF = 21, 168
TV = 5
EMPTY = 4098
ZW, WW = 272, 296
SW = 4352
MAXED = [(8, 0), (8, 1)] + [(h, j) for h in (5, 3, 2) for j in range(h)]

bf, f16, f32, i32, u16 = "bfloat16", "float16", "float32", "int32", "uint16"
SCRATCH = {n: ("sbuf", [p, c], d) for n, p, c, d in [
    ("X", 128, 8192, bf), ("LS", 128, 1024, i32), ("LSN", 128, 1024, i32), ("SH", 128, TV * SW, f32),
    ("GL", 128, 2048, bf), ("GH", 128, 2048, bf), ("ZC", 128, 2064, bf), ("ZR", 128, 512, bf),
    ("DL", 128, 12 * 256, bf), ("DA", 128, 1536, bf), ("NEG", 128, 256, bf),
    ("ZS", 128, 5 * ZW, bf), ("ZM", 128, 5 * ZW, bf), ("HS", 128, 5 * 128, u16), ("HM", 128, 5 * 128, u16),
    ("LLS", 128, 5 * 128, u16), ("LLM", 128, 5 * 128, u16), ("WS", 128, 5 * WW, f32),
    ("WI", 128, 256, i32), ("WN", 128, 256, f16), ("WX", 128, 256, bf), ("MM", 128, 256, f16), ("MK", 128, 256, bf), ("MS", 128, 256, f32),
    ("MF", 128, 256, f32), ("EXF", 128, 144, f32), ("LOW", 128, 256, i32), ("MX2", 128, 32, bf), ("M0B", 128, 128, bf),
    ("IDX", 128, 160, bf), ("IZ", 128, 128, bf), ("IZR", 128, 128, bf), ("NIB", 128, 128, bf), ("RA", 128, 512, bf), ("ROT", 128, 128, bf),
    ("EXT", 128, 144, bf), ("EXR", 128, 128, bf), ("BA", 128, 48, bf), ("OB", 128, 48, bf), ("OF", 128, 48, u16),
    ("J256", 128, 128, bf), ("J77", 128, 128, bf), ("ONE", 128, 128, bf), ("THL", 128, 128, bf), ("ZER", 128, 128, bf),
    ("CQ", 128, HALF, bf), ("DB", 128, 336, bf), ("D0", 128, HALF, bf), ("M1", 128, HALF, bf), ("CP", 128, 176, bf),
    ("S1", 128, 336, bf), ("U", 128, 344, f32), ("E", 128, 144, f32), ("E2", 128, 144, bf), ("ES", 128, 256, f32),
    ("RR", 128, 96, f32), ("RB", 128, 80, bf), ("ZROW", 32, 80, bf), ("NH", 128, 16, bf), ("MT", 128, 32, f32), ("M01", 128, 32, f32),
    ("KF", 128, 16, f32), ("KN", 128, 8, bf), ("K2", 128, 8, bf), ("KB", 128, 8, bf), ("WP", 128, 8, bf), ("WQ", 128, 8, bf),
    ("II", 128, 160, i32), ("IG", 128, 16, i32), ("IP", 128, 4, i32), ("IQ", 128, 8, i32), ("IU", 128, 32, i32), ("I9", 128, 10, i32),
    ("IS", 128, 16, i32), ("IA", 128, 32, f32), ("COL", 128, 24, f32), ("POS", 128, 16, i32), ("POSU", 128, 16, u16),
    ("CV", 128, 10, u16), ("SV", 128, 32, u16), ("N77", 128, 16, f32), ("M10", 128, 32, f32),
    ("SI", 128, 16, i32), ("NP", 128, 16, i32), ("THI", 128, 1, i32), ("WTI", 128, 1, i32),
    ("NU", 128, 16, u16), ("A5", 128, 16, f32), ("SUM", 128, 16, i32),
    ("S15", 128, 16, i32), ("SU", 128, 16, u16), ("T1", 128, 16, i32), ("T2", 128, 16, i32), ("U7", 128, 16, i32), ("CU", 128, 16, u16),
    ("CX", 128, 32, u16), ("AT", 128, 1, bf), ("AR", 128, 1, f32),
    ("XT", 128, 256, bf), ("XU", 128, 256, bf), ("YW", 128, 256, f32), ("FO", 128, 40, f32), ("YO", 128, 32, f32),
]}
for _b in range(8):
    SCRATCH["B%d" % _b] = ("psum", [128, 512], f32)
_ARR = ["%s%d" % (n, t) for n in ("Z", "C", "H", "L", "W") for t in range(TV)] + ["LS"]
_DMA = ["small", "sm2", "ls", "wd", "x", "sh", "oyx", "oyw", "oyn"]
SEMAPHORES = ["qv", "qa", "qp", "qg", "loc"] + ["r" + n for n in _ARR] + ["d" + n for n in _DMA]


def rank_program(g, core, T, topo):
    rank, N = T.rank_of(core), len(T.cores)

    def helpers(r):
        c, to = T.cores[r], T.cores[(r - 1) % N]
        free = [h for h in topo.cores_of(c) if T.rank_of(h) is None and topo.may_write(h, to)]
        return [[h for h in free if topo.die(h) == d][0] for d in (topo.die(c), 1 - topo.die(c))]
    if rank is None:
        for r in range(N):
            if core in helpers(r):
                k, to = helpers(r).index(core), T.cores[(r - 1) % N]
                rid, pid = topo.addr(to)[:2]
                half = T.LSN[:, 512 * k:512 * k + 512]
                g.wait_ge(T.sem.rLS, len(topo.engines(T.cores[r], core)) // 2)
                g.remote_dma(half, half, T.sem.rLS, T.sem.loc, pid, rid, topo.mask(core, to))
                g.wait_ge(T.sem.loc, len(topo.engines(core, to)))
        return
    nxt, prv = T.cores[(rank + 1) % N], T.cores[(rank - 1) % N]
    V, P, S = g.vector, g.tensor, g.scalar
    Q = {"v": V, "a": S, "p": P, "g": g, "s": g.sync}
    B = [T["B%d" % b] for b in range(8)]

    tot = {}
    known = {q: {} for q in Q}
    lastw, readers, banks, ops = {}, {}, {}, []

    def need(q, deps):
        for o in sorted(deps, reverse=True):
            sem, val, snap, dma_ = ops[o]
            if known[q].get(sem, 0) >= val:
                continue
            if dma_:
                val = tot[sem]
            if sem == "q" + q:
                val = max(val, tot[sem] - 1)
            Q[q].wait_ge(T.sem[sem], val)
            for s_, v_ in snap.items():
                known[q][s_] = max(known[q].get(s_, 0), v_)
            known[q][sem] = val

    def deps_of(q, r, w, b):
        d = set()
        for k in r:
            d.update(lastw.get(k, ()))
        for k in w:
            d.update(lastw.get(k, ()))
            d.update(readers.get(k, ()))
        for k in b:
            d.update(o for q_, o in banks.get(k, {}).items() if q_ != q)
        return d

    def note(q, sem, inc, r, w, b, dma_=False):
        tot[sem] = tot.get(sem, 0) + inc
        o = len(ops)
        ops.append((sem, tot[sem], dict(known[q]) if q else {}, dma_))
        for k in w:
            lastw[k] = [o]
            readers[k] = []
        for k in r:
            readers.setdefault(k, []).append(o)
        for k in b:
            banks.setdefault(k, {})[q] = o
        return o

    def run(q, fn, *a, r="", w="", b="", **k):
        r, w, b = r.split(), w.split(), b.split()
        need(q, deps_of(q, r, w, b))
        sem = "q" + q
        fn(*a, **k).then_inc(T.sem[sem], 1)
        note(q, sem, 1, r, w, b)

    def v(fn, *a, **k):
        run("v", fn, *a, **k)

    def ts(out, in_, s1, op0, s2=None, op1=None, **k):
        if op1 is None:
            run("v", V.tensor_scalar, out, in_, s1, None, op0, **k)
        else:
            run("v", V.tensor_scalar, out, in_, s1, s2, op0, op1, **k)

    def tt(out, a, b_, op, **k):
        run("v", V.tensor_tensor, out, a, b_, op, **k)

    def cp(out, in_, **k):
        run("v", V.tensor_copy, out, in_, **k)

    def act(out, in_, func=F.Copy, r="", w="", b="", **k):
        run("a", S.activation, out, in_, func, r=r, w=w, b=b, **k)

    def mm(out, l, rh, start, stop, r, b):
        r, b = r.split(), b.split()
        need("p", deps_of("p", r, [], b))
        P.matmul(out, l, rh, start, stop).then_inc(T.sem.qp, 1)
        note("p", "qp", 1, r, [], b)

    def dma(sem, out, in_, r="", w="", q="s"):
        r, w = r.split(), w.split()
        need(q, deps_of(q, r, w, []))
        Q[q].dma_start(out, in_).then_inc(T.sem["d" + sem], 16)
        note(q, "d" + sem, 16, r, w, [], True)

    def send(name, dst, out, in_, r=""):
        need("g", deps_of("g", r.split(), [], []))
        rid, pid = topo.addr(dst)[:2]
        g.remote_dma(out, in_, T.sem["r" + name], T.sem.loc, pid, rid, topo.mask(core, dst))
        note("g", "loc", len(topo.engines(core, dst)), [], [], [])

    def arrive(name, senders, key):
        tot["r" + name] = sum(len(topo.engines(c, core)) for c in senders)
        lastw[key] = [len(ops)]
        ops.append(("r" + name, tot["r" + name], {}, False))

    def iota(out, pat, base, cm, key, r=""):
        run("g", g.iota, out, pat, base, cm, w=key, r=r, allow_small_or_imprecise_dtypes=True)

    for t in range(TV):
        arrive("Z%d" % t, [prv], "ZM%d" % t)
        arrive("C%d" % t, [prv], "CM%d" % t)
        if t > 0:
            for n_ in "HLW":
                arrive("%s%d" % (n_, t), [prv], "%sM%d" % (n_, t))
    arrive("LS", helpers((rank + 1) % N), "LSN")

    v(V.memset, T.THI[:], 0, w="THI")
    dma("small", T.SI[:], T.sd[:], w="SI")
    dma("small", T.NP[:], T.nl[:], w="NP")
    dma("sm2", T.THI[0:128:16, :], T.th[:], w="THI")
    dma("sm2", T.WTI[:], T.wt[:], w="WTI")
    dma("ls", T.LS[:], T.ls[:], w="LS")
    dma("wd", T.WI[1:128, :], T.wd[0:127, :], w="WIa")
    dma("wd", T.WI[0:1, :], T.wd[0:1, :], w="WIb")
    dma("x", T.X[:, 0:4096], T.x[:], w="X0 X1 X2 X3")
    XK = "X0 X1 X2 X3 XD XE"
    IDB = T.IDX[:, 16:144]
    C = {n: T.COL[:, i:i + 1] for i, n in enumerate("p15 s8 n24 lo sel h168 thx q1 q2 wts bw c0 q3 thy".split())}
    C.update(m0=T.M01[:, 1:2], nz=T.M10[:, 1:2], hi=T.M10[:, 8:9], lo8=T.M01[:, 8:9])

    def landing(u):
        c = SW * u + (4096 if u == TV - 1 else 256) - 40
        return T.SH[:, c:c + WW]

    def slot(u):
        k = "M" if u == 0 else "S"
        return T["H" + k][:, 128 * u:128 * u + 128], T["LL" + k][:, 128 * u:128 * u + 128], T.WS[:, WW * u:WW * u + WW] if u else landing(0), k

    def lists(b_, src, stop):
        for n_ in src:
            for w_ in range(2):
                c = 128 * (2 * b_ + w_)
                mm(B[2 - b_][:, 0:128], T.RA[:, c:c + 128], T[n_][:, w_:256:2], (n_, w_) == (src[0], 0), stop and (n_, w_) == (src[-1], 1),
                   "%s RA%d%d" % (n_, b_, w_), "B%d" % (2 - b_))

    def list_out(b_, u):
        ts(slot(u)[1 - b_], B[2 - b_][:, 0:128], 2048, A.add, EMPTY, A.min, w="%s%s%d" % ("LH"[b_], slot(u)[3], u), b="B%d" % (2 - b_))

    def col_of_ls(u, *between):
        cp(T.SU[:], T.S15[:], r="S15", w="SU")
        act(T.MK[:], T.RR[:, 32:48].indirect(T.SU[:]), r="RR1 SU", w="MK")
        tt(T.T1[:], T.SI[:], T.SI[:], A.mult, r="SI", w="T1")
        if u:
            tt(T.U7[:], B[5][:, 16:32], T.SI[:], A.add, r="SI", w="U7", b="B5")
        else:
            tt(T.U7[:], T.N77[:], T.SI[:], A.add, r="N77 SI", w="U7")
        ts(T.T2[:], T.T1[:], 5, A.arith_shift_right, r="T1", w="T2")
        between[0]()
        tt(T.T1[:], T.T2[:], T.U7[:], A.add, r="T2 U7", w="T1")
        between[1]()
        ts(T.T2[:], T.T1[:], 1023, A.bitwise_and, r="T1", w="T2")
        between[2]()
        cp(T.CU[:], T.T2[:], r="T2", w="CU")

    def letters():
        tt(T.MM[:], T.LSN[:].indirect(T.CU[:]), T.MK[:], A.mult, r="LSN CU MK", w="MM")
        for w_ in range(2):
            mm(B[2][:, 0:128], T.EXT[:, 16 - 8 * w_:144 - 8 * w_], T.MM[:, w_:256:2], False, w_ == 1, "MM EXT", "B2")

    def seeds_out(u):
        ts(slot(u)[2][:, 8:24], T.SI[:], 5, A.mult, -16, A.add, r="SI", w="Ws%d" % u)

    def words_out(u):
        iz, ex = ("IZ", T.EXT[:, 16:144]) if u == TV - 1 else ("IZR", T.EXR[:])
        mm(B[3][:, 0:256], T[iz][:], T.WN[:], True, u == 0, iz + " IZRa WN", "B3")
        if u:
            mm(B[3][:, 0:256], T[iz][:], T.WX[:], False, False, iz + " WX", "B3")
            mm(B[3][:, 0:256], ex, T.MM[:], False, True, "MM EXT EXR", "B3")
        act(slot(u)[2][:, 40:WW], B[3][:, 0:256], w="Ww%d" % u, b="B3")

    def wkey(u):
        return "WM%d" % u if u else "Ww0 Ws0 Wn0 Wz"

    def copy(u, h):
        c = SW * u + 256 * (h or 16)
        return T.SH[:, c:c + 256]

    def moved_by_dma(u):
        wk, push = "WM%d" % u if u else "Ww0 X0", int(u < TV - 1)
        for h in HS[:5 - push] + (0,) * push:
            d = (h - push) % 128
            dma("sh", copy(u, h)[0:128 - d, :], copy(u, push)[d:128, :], r=wk, w="SH%d" % h)
            dma("sh", copy(u, h)[128 - d:128, :], copy(u, push)[0:d, :], r=wk, w="SH%da" % h)

    def popped(u):
        return T.SH[:, SW * u:SW * u + SW].indirect(T.OF[:, 16:32]), "OF SH0 SH0a SH1 SH1a SH2 SH2a SH3 SH3a SH5 SH5a SH8 SH8a " + wkey(u)

    iota(T.IP[:], [[0, 4]], 0, 1, "IP")
    iota(T.IS[:], [[1, 16]], 0, 16, "IS")
    iota(T.IU[:], [[1, 32]], 0, 0, "IU")
    iota(T.IG[:, 1:9], [[-16, 8]], 0, 1, "IGa")
    iota(T.IG[:, 0:1], [[1, 1]], -112, 1, "IGb")
    iota(T.II[:], [[-1, 160]], 16, 1, "II")
    v(V.memset, T.D0[:], 1.0, w="D0")
    act(T.M1[:], T.D0[:], scale=-1.0, r="D0", w="M1")
    act(T.CQ[:], T.D0[:], scale=0.0, r="D0", w="CQ")
    act(T.EXF[:], T.D0[:, 0:144], scale=0.0, r="D0", w="EXF")
    v(V.memset, T.LOW[:], -2048, w="LOW")
    v(V.memset, T.CP[:], 0.0, w="CP")
    v(V.memset, T.X[:, 4096:4112], 32.0, w="XE")
    v(V.memset, T.ONE[:], 1.0, w="ONE")
    v(V.memset, T.ZER[:], 0.0, w="ZER")
    v(V.memset, T.ZR[:], 1.0, w="ZR")
    run("g", g.affine_select, T.DB[:, 0:HALF], T.M1[:], [[-16, 8], [0, NPL]], A.is_equal, 0.0, 0, 1, r="M1", w="DB")
    iota(T.DB[:, 0:HALF:NPL], [[0, 8]], 0, 0, "DBa", r="DB")
    iota(T.DB[:, 20:HALF:NPL], [[0, 8]], 32768, 0, "DBb", r="DB")
    cq = {0: 64, 1: -16, 8: 24, 9: -24, 13: 27, 14: -27, 16: 29, 17: -29, 18: 30, 19: 1, 20: 1}
    for q_, c in cq.items():
        iota(T.CQ[:, q_:HALF:NPL], [[0, 8]], c, 0, "CQ%d" % q_, r="CQ")
    cqk = "CQ " + " ".join("CQ%d" % q_ for q_ in cq)
    v(V.memset, T.ZR[:, 0:512:8], 0.0, w="ZR")
    ts(T.IQ[:, 0:1], T.IP[:, 0:1], 15, A.bitwise_and, r="IP IU", w="IQ0")
    ts(T.POS[:], T.IS[:], 255, A.bitwise_and, r="IS", w="POS")
    ts(T.IQ[:, 2:3], T.IP[:, 0:1], 7, A.bitwise_and, r="IP", w="IQ2")
    ts(T.IQ[:, 1:2], T.IP[:, 0:1], 4, A.arith_shift_right, r="IP", w="IQ1")
    cp(C["p15"], T.IQ[:, 0:1], r="IQ0", w="p15")
    cp(T.POSU[:], T.POS[:], r="POS", w="POSU")
    ts(T.IG[:, 0:9], T.IG[:, 0:9], 4, A.arith_shift_right, r="IGa IGb II", w="IG")
    ts(T.IDX[:], T.II[:], 0, A.is_equal, r="II", w="IDX")
    ts(T.M01[:], T.IU[:], C["p15"], A.is_gt, r="IU p15", w="M01 m0")
    ts(T.M10[:], T.IU[:], C["p15"], A.is_le, r="IU p15", w="hi nz")
    ts(T.RR[:, 32:48], T.IU[:, 0:16], C["p15"], A.is_equal, r="IU p15", w="RR1")
    ts(T.KF[:, 0:9], T.IG[:, 0:9], 0, A.is_equal, r="IG", w="KF")
    for b_ in (1, 0):
        for w_ in range(2):
            c, o = 128 * (2 * b_ + w_), 16 + 8 * (b_ - w_)
            act(T.RA[:, c:c + 128], T.IDX[:, o:o + 128], scale=C["hi" if b_ else "lo8"], r="IDX hi M01", w="RA%d%d" % (b_, w_))
    ts(T.S15[:], T.SI[:], 15, A.bitwise_and, r="SI", w="S15")
    ts(T.NU[:], T.NP[:], 1, A.add, 16, A.min, r="NP", w="NU")
    ts(T.N77[:], T.NP[:], 77, A.mult, r="NP", w="N77")
    ts(T.MT[:], T.M01[:], -EMPTY, A.mult, EMPTY - 2048, A.add, r="M01", w="MT")
    cp(T.EXF[:, 16:144:16], T.KF[:, 1:9], r="KF", w="EXF")
    col_of_ls(0, lambda: ts(C["q1"], T.IP[:, 0:1], 1, A.is_equal, 2.0 ** -5, A.mult, r="IP", w="q1"),
              lambda: ts(C["q2"], T.IP[:, 0:1], 2, A.is_equal, 2.0 ** -22, A.mult, r="IP", w="q2"),
              lambda: ts(C["bw"], C["m0"], -2048, A.mult, r="m0", w="bw"))
    act(T.MS[:], T.MT[:].indirect(T.NU[:]), r="MT NU", w="MS")
    act(T.IZ[:], IDB, scale=C["nz"], r="IDX nz", w="IZ")
    ts(C["wts"], T.WTI[:], 2.0 ** -22, A.mult, r="WTI", w="wts")
    ts(C["thx"], T.THI[:], C["q1"], A.add, C["q2"], A.add, r="THI q1 q2", w="thx")
    ts(C["q3"], C["q1"], C["q2"], A.add, 0, A.is_gt, r="q1 q2", w="q3")
    for k_, sc in (("KN", -1.0), ("K2", 2.0), ("KB", 1.0)):
        ts(T[k_][:], T.KF[:, 1:9], sc, A.mult, r="KF", w=k_)
    need("g", deps_of("g", ["LS", "LOW"], [], []))
    en, to = topo.engines(core, helpers(rank)[0]), [topo.addr(h) for h in helpers(rank)]
    g.remote_dma_fused([RemoteDMATransfer(dst_ids=[DstId(rid=to[k_ // 2][0], pnc=to[k_ // 2][1])], dma_engine_mask=sum(1 << e for e in en[k_::4]),
                                          remote_sem=T.sem.rLS, srcs=[T.LS[:, 256 * k_:256 * k_ + 256], T.LOW[:]],
                                          dsts=[T.LSN[:, 256 * k_:256 * k_ + 256]], alu_op=1) for k_ in range(4)], local_sem=T.sem.loc)
    note("g", "loc", len(en), [], [], [])
    tt(T.MF[:], T.LS[:].indirect(T.CU[:]), T.MK[:], A.mult, r="LS CU MK", w="MF")
    tt(T.WN[:], T.WI[:].indirect(T.POSU[:]), T.MS[:], A.add, r="WIa WIb POSU MS", w="WN")
    mm(B[3][:, 0:256], T.EXF[:, 16:144], T.MF[:], True, False, "MF EXF", "B3")
    mm(B[3][:, 0:256], T.IZ[:], T.WN[:], False, True, "IZ WN", "B3")
    act(T.THL[:], T.ONE[:], scale=C["thx"], r="ONE thx", w="THL")
    act(T.DB[:, HALF:336], T.CQ[:], scale=C["q3"], r="q3 " + cqk, w="DBc")
    act(T.IZR[:, 16:128], T.IDX[:, 16:128], r="IDX", w="IZRa")
    act(T.IZR[:, 0:16], T.IDX[:, 128:144], r="IDX", w="IZR")
    ts(T.WP[:], T.KF[:, 1:9], C["wts"], A.mult, r="KF wts", w="WP")
    ts(T.WQ[:], T.KF[:, 1:9], C["wts"], A.mult, -1, A.mult, r="KF wts", w="WQ")
    ts(T.WN[:], B[3][:, 0:256], C["bw"], A.add, r="bw", w="WN", b="B3")
    lists(1, ["WN"], True)
    lists(0, ["WN"], True)
    words_out(0)
    moved_by_dma(0)
    ts(T.NIB[:], IDB, -1, A.mult, r="IDX", w="NIB")
    for h in HS:
        ts(T.CP[:, 1 + BASE[h]:169:NPL], T.KF[:, 1:9], -1, A.mult, r="KF CP", w="CP%d" % h)
    cpk = "CP " + " ".join("CP%d" % h for h in HS)
    list_out(1, 0)
    list_out(0, 0)
    act(T.EXT[:], T.EXF[:], r="EXF", w="EXT")
    for c, sc, k_ in ((48, 2.0 ** -12, "RR4"), (64, -1.0, "RR5")):
        act(T.RR[:, c:c + 16], T.RR[:, 32:48], scale=sc, r="RR1", w=k_)
    iota(T.I9[:, 1:9], [[NPL, 8]], 28, 0, "I9a")
    iota(T.I9[:, 0:10:9], [[0, 2]], 28 + 7 * NPL, 0, "I9b")
    ts(C["s8"], C["p15"], 8, A.add, r="p15", w="s8")
    ts(C["n24"], C["p15"], 24, A.add, r="p15", w="n24")
    ts(C["h168"], C["hi"], HALF, A.mult, r="hi", w="h168")
    tt(C["sel"], T.IQ[:, 1:2], T.IQ[:, 2:3], A.is_equal, r="IQ1 IQ2", w="sel")
    ts(landing(0)[:, 24:40], T.NU[:], -1, A.mult, 16, A.add, r="NU", w="Wn0")
    seeds_out(0)
    ts(T.SV[:, 0:8], T.KF[:, 0:8], C["s8"], A.mult, r="KF s8", w="SV0a")
    ts(T.SV[:, 8:16], T.KF[:, 0:8], C["n24"], A.mult, r="KF n24", w="SV0b")
    ts(T.OB[:, 0:16], T.POS[:], 8, A.mult, r="POS", w="OBa")
    cp(T.OB[:, 16:32], T.POS[:], r="POS", w="POSB")
    ts(T.MX2[:, 0:16], T.IU[:, 0:16], C["p15"], A.add, 17, A.is_ge, r="IU p15", w="MX2")
    for c, sc, k_ in ((80, -77.0, "RR6"), (0, 2.0 ** 22, "RR2")):
        ts(T.RR[:, c:c + 16], T.RR[:, 32:48], sc, A.mult, r="RR1", w=k_)
    for c, sc in ((16, 256), (32, 1), (48, -1), (64, -77)):
        ts(T.RB[:, c:c + 16], T.RR[:, 32:48], sc, A.mult, r="RR1", w="RB%d" % c)

    def diagonal(out, n, base, val, key):
        run("g", g.affine_select, out, T.ZER[:, 0:n], [[-1, n]], A.not_equal, val, base, 1, r="ZER", w=key)
    iota(landing(0)[:, 0:8], [[0, 8]], 0, 0, "Wz")
    for q_ in (0, 1, 9, 14, 17, 19):
        iota(T.D0[:, q_:HALF:NPL], [[0, 8]], 0, 0, "D0%d" % q_, r="M1 CQ EXF")
    d0k = "D0 " + " ".join("D0%d" % q_ for q_ in (0, 1, 9, 14, 17, 19))
    for k_, (a, b_) in enumerate(((1024, 16), (77 * 1024, 77 * 16), (-1024, -1), (-1024 * 256, 0), (-1024, 0))):
        iota(T.ZROW[0:2, 16 * k_:16 * k_ + 16], [[0, 16]], a, b_ - a, "ZROW%d" % k_)
    iota(T.OB[:, 32:48], [[0, 16]], 0, 0, "OBz")
    iota(T.MX2[:, 16:32], [[0, 16]], 0, 0, "MXz")
    iota(T.U[:, 0:8], [[0, 8]], 0, 0, "Uz")
    iota(T.ZC[:, 2048:2064], [[0, 16]], 0, 0, "ZCz")
    diagonal(T.J77[:], 128, 0, 77 / 256, "J77")
    diagonal(T.J256[:], 128, 0, 1 / 256, "J256")
    iota(T.IA[:, 0:16], [[256, 16]], 0, 0, "IA0")
    iota(T.IA[:, 16:32], [[0, 4], [256, 4]], 0, 0, "IA1")
    diagonal(T.ROT[:, 0:112], 112, -16, 1.0, "ROTa")
    diagonal(T.ROT[:, 112:128], 16, 0, 1.0, "ROTb")
    iota(T.EXR[:], [[0, 128]], 0, 0, "EXR")
    iota(T.X[:, 4112:8192:16], [[0, 255]], 0, 0, "XD")
    iota(T.NEG[:], [[0, 256]], -128, 0, "NEG")
    for u in range(1, TV):
        iota(T.WS[:, WW * u:WW * u + 8], [[0, 8]], 0, 0, "Wz%d" % u)
    iota(T.FO[:, 0:8], [[0, 8]], 0, 0, "FOz")

    def late_consts():
        act(C["lo"], C["lo8"], F.Identity, scale=C["nz"], r="M01 nz", w="lo")
        act(C["c0"], C["p15"], scale=16.0, r="p15", w="c0")
        act(T.IZR[:], T.IZR[:], scale=C["nz"], r="nz IZRa", w="IZR")

    def later_consts(t):
        if t == 0:
            ts(T.RA[:, 0:256], T.RA[:, 0:256], C["lo"], A.mult, r="lo", w="RA00 RA01")
            ts(C["thy"], C["m0"], -2048, A.mult, C["thx"], A.add, r="m0 thx", w="thy")
            ts(T.M0B[:], T.ONE[:], C["m0"], A.mult, r="ONE m0", w="M0B")
            cp(T.EXR[:, 0:128:16], T.KF[:, 0:8], r="KF", w="EXR")
            act(T.BA[:, 0:32], T.IA[:, 0:32], F.Identity, bias=C["c0"], r="IA0 IA1 c0", w="BA0")
        if t == 1:
            act(T.BA[:, 32:48], T.OB[:, 16:32], scale=16.0, r="POSB", w="BA1")
        if t == 2:
            ts(T.SV[:, 16:24], T.KF[:, 1:9], C["s8"], A.mult, r="KF s8", w="SV16a")
            ts(T.SV[:, 24:32], T.KF[:, 1:9], C["n24"], A.mult, r="KF n24", w="SV16b")

    PD, PC = 0, HALF

    def place(o, hf, q_):
        return B[6 + hf][:, o + q_:o + HALF:NPL]

    def row(buf, hf, j):
        return buf[:, 1024 * hf + j:1024 * hf + 1024:8]

    def diff_at(hf, j):
        if j < 6:
            return (1 if hf == 0 else 3), 128 * (j - 2)
        return 2, 256 * hf + 128 * (j - 6)

    def bulk(t):
        win, xk = T.X[:, 0:4112], "X0 X1 X2 X3 XE "

        def gather(q, buf, lk, c, n, key):
            off = T[lk][:, 128 * t + c // 16:128 * t + (c + n) // 16]
            (cp if q == "v" else act)(buf[:, c:c + n], win.indirect(off), r=xk + lk[-2:] + str(t), w=key)
        for hf in range(2):
            gather("v", T.GH, "HM", 1024 * hf, 512, "GH%da" % hf)
            gather("a", T.GH, "HM", 1024 * hf + 512, 512, "GH%db" % hf)
        gather("v", T.GL, "LLM", 0, 512, "GL0a")
        gather("a", T.GL, "LLM", 512, 512, "GL0b")
        gather("a", T.GL, "LLM", 1024, 1024, "GL1a GL1b")
        gl = ("GL0a GL0b", "GL1a GL1b")
        gh = ("GH0a GH0b", "GH1a GH1b")
        for bk in (1, 2, 3):
            mm(B[bk][:, 0:512], T.ZER[0:1, :], T.ZR[0:1, 0:512], True, False, "ZER ZR", "B%d" % bk)
        for hf in range(2):
            mm(B[6 + hf][:, 0:336], T.THL[:], T.DB[:], True, False, "THL DB DBa DBb DBc", "B%d" % (6 + hf))

        def highs(hf):
            for j in range(2):
                mm(B[0][:, 256 * hf + 128 * j:256 * hf + 128 * j + 128], IDB, row(T.GH, hf, j), True, True, "IDX " + gh[hf], "B0")

        def highd(hf):
            for j in range(2, 8):
                bk, c = diff_at(hf, j)
                mm(B[bk][:, c:c + 128], IDB, row(T.GH, hf, j), False, False, "IDX " + gh[hf], "B%d" % bk)

        def sums(hf, buf, j, places, key):
            for q_ in places:
                mm(place(PD, hf, q_), row(buf, hf, j), T.KN[:], False, False, key + " KN", "B%d" % (6 + hf))

        def highsums(hf):
            sums(hf, T.GH, 0, (BASE[8], BASE[5] + 3), gh[hf])
            sums(hf, T.GH, 1, (BASE[8] + 1, BASE[5] + 4), gh[hf])

        def lows(hf):
            for j in range(3):
                mm(B[4 + hf][:, 128 * j:128 * j + 128], IDB, row(T.GL, hf, j), True, True, "IDX " + gl[hf], "B%d" % (4 + hf))

        def lowd(hf):
            for j in range(2, 8):
                bk, c = diff_at(hf, j)
                mm(B[bk][:, c:c + 128], T.NIB[:], row(T.GL, hf, j), False, j == 5 or (hf, j) == (1, 7), "NIB " + gl[hf], "B%d" % bk)

        def lowsums(hf):
            o = B[6 + hf][:, 0:HALF]
            mm(o, row(T.GL, hf, 0), T.CP[:, 1:169], False, False, gl[hf] + " " + cpk, "B%d" % (6 + hf))
            mm(o, row(T.GL, hf, 1), T.CP[:, 0:168], False, False, gl[hf] + " " + cpk, "B%d" % (6 + hf))
            for j in range(1, 8):
                pl = [BASE[h] + j - h for h in (5, 3, 2, 1) if 0 <= j - h < h] + [BASE[h] + j for h in (5, 3) if 1 < j < h]
                sums(hf, T.GL, j, pl, gl[hf])

        def zc(hf):
            for k_ in range(2):
                c = 1024 * hf + 512 * k_
                v(V.tensor_tensor_scan, T.ZC[:, c:c + 512], T.ZR[:], T.GL[:, c:c + 512], 0.0, A.mult, A.max,
                  r="ZR " + gl[hf].split()[k_], w="ZC%d%d" % (hf, k_))

        def seeds(hf):
            zk, bk = "ZC%d0 ZC%d1 " % (hf, hf), "B%d" % (6 + hf)
            mm(place(PD, hf, BASE[1]), row(T.ZC, hf, 1), T.K2[:], False, False, zk + "K2", bk)
            for h, q_, wk in [(h, BASE[h] + h - 1, "WQ") for h in HS] + [(h, BASE[h] + h, "WP") for h in HS] + [(1, 1, "WP")]:
                mm(place(PC, hf, q_), row(T.ZC, hf, h - 1), T[wk][:], False, False, zk + wk, bk)

        def pair(hf, h, j):
            c = 256 * MAXED.index((h, j)) + 128 * hf
            if j + h >= 8:
                k_ = j + h - 8
                a, bk, o = B[0][:, 256 * hf + 128 * k_:256 * hf + 128 * k_ + 128], "B0", j
            else:
                a, bk, o = B[4 + hf][:, 128 * j:128 * j + 128], "B%d" % (4 + hf), j + h
            tt(T.DL[:, c:c + 128], a, row(T.GL, hf, o), A.max, r=gl[hf], w="DL%d%d%d" % (hf, h, j), b=bk)

        def add(hf, h, j, stop=False):
            c = 256 * MAXED.index((h, j)) + 128 * hf
            mm(place(PD, hf, BASE[h] + j), T.DL[:, c:c + 128], T.K2[:], False, stop, "K2 DL%d%d%d" % (hf, h, j), "B%d" % (6 + hf))

        def sizes(bk):
            act(T.DA[:, 512 * (bk - 1):512 * bk], B[bk][:, 0:512], F.Abs, w="DA%d" % bk, b="B%d" % bk)

        def add_sizes(hf, js):
            for j in js:
                bk, c = diff_at(hf, j)
                c += 512 * (bk - 1)
                mm(place(PD, hf, BASE[8] + j), T.DA[:, c:c + 128], T.KB[:], False, False, "KB DA%d" % bk, "B%d" % (6 + hf))

        up = [p_ for p_ in MAXED if sum(p_) >= 8]
        dn = [p_ for p_ in MAXED if sum(p_) < 8]
        for hf in range(2):
            highs(hf)
            highd(hf)
            highsums(hf)
        lows(0)
        lowd(0)
        sizes(1)
        zc(0)
        for p_ in up + dn:
            pair(0, *p_)
        lowsums(0)
        seeds(0)
        for p_ in up:
            add(0, *p_)
        lows(1)
        lowd(1)
        sizes(2)
        sizes(3)
        lowsums(1)
        for p_ in dn[:-1]:
            add(0, *p_)
        zc(1)
        add_sizes(0, range(2, 6))
        seeds(1)
        add_sizes(0, (6, 7))
        add(0, *dn[-1], stop=True)
        add_sizes(1, (6, 7))
        for p_ in up + dn:
            pair(1, *p_)
        for i, p_ in enumerate(up + dn):
            if i == 6:
                add_sizes(1, range(2, 6))
            add(1, *p_, stop=i == len(MAXED) - 1)
        o = 16 if t == TV - 1 else 0
        act(T.ES[:], landing(t)[:, 0:40].indirect(T.SV[:, o:o + 16]), r=wkey(t) + " SV%da SV%db" % (o, o), w="ES")

    def decode(t):
        last = t == TV - 1
        nh, c0 = T.NH[:], ZW * t
        mm(B[0][:, 0:48], T.ONE[0:2, :], T.ZROW[0:2, 32:80], True, False, "ONE ZROW2 ZROW3 ZROW4", "B0")
        mm(B[0][:, 0:48], IDB, T.OB[:, 0:48], False, False, "IDX OBa POSB OBz", "B0")
        mm(B[5][:, 0:32], T.ONE[0:2, :], T.ZROW[0:2, 0:32], True, False, "ONE ZROW0 ZROW1", "B5")
        mm(B[4][:, 16:32], T.ES[:, 0:128], T.RR[:, 48:64], True, True, "ES RR4", "B4")
        mm(B[5][:, 0:32], T.ES[:, 128:256], T.RR[:, 64:96], False, False, "ES RR5 RR6", "B5")
        for hf in range(2):
            c, bk = HALF * hf, "B%d" % (6 + hf)
            v(V.tensor_tensor_scan, T.S1[:, c:c + HALF], T.D0[:], B[6 + hf][:, 0:HALF], 0.0, A.mult, A.max, r=d0k, w="S1%d" % hf, b=bk)
            if t == 0 and hf == 0:
                ts(T.CV[:], T.I9[:], C["h168"], A.add, C["sel"], A.mult, r="I9a I9b h168 sel", w="CV")
        for hf in range(2):
            c, bk = HALF * hf, "B%d" % (6 + hf)
            v(V.tensor_tensor_scan, T.U[:, 8 + c:8 + c + HALF], B[6 + hf][:, HALF:336], T.S1[:, c:c + HALF], 0.0, A.add, A.min,
              r="S1%d" % hf, w="U%d" % hf, b=bk)
        ts(T.E2[:], T.U[:].indirect(T.CV[:, 0:9]), 32, A.mult, 127.77, A.add, r="U0 U1 Uz CV", w="E2")
        act(T.E[:], T.U[:].indirect(T.CV[:, 0:9]), r="U0 U1 Uz CV", w="E")
        o = 16 if last else 0
        mm(B[0][:, 0:16], T.E2[:, 16:144], T.RB[:, 32:48], False, False, "E2 RB32", "B0")
        mm(B[0][:, 16:48], T.E2[:, o:o + 128], T.RB[:, 16:48], False, True, "E2 RB16 RB32", "B0")
        mm(B[4][:, 0:16], T.E[:, o:o + 128], T.RR[:, 0:16], True, True, "E RR2", "B4")
        mm(B[5][:, 0:32], T.E2[:, o:o + 128], T.RB[:, 48:80], False, False, "E2 RB48 RB64", "B5")
        cp(T.OF[:], B[0][:, 0:48], w="OF", b="B0")
        act(T.ZS[:, c0:c0 + 256], T.ZC[:].indirect(T.OF[:, 0:16]), F.Identity, scale=0.5, bias=96.0, r="ZC00 ZC01 ZC10 ZC11 ZCz OF", w="Za")
        cp(T.T1[:], B[4][:, 0:16], w="T1", b="B4")
        ts(nh, B[4][:, 0:16], 1 << 21, A.is_ge, 4096, A.mult, w="NH", b="B4")
        ts(T.T2[:], T.T1[:], 15 + (1 << 21), A.bitwise_and, r="T1", w="T2")
        mm(B[5][:, 0:16], T.J256[:], nh, False, False, "J256 NH", "B5")
        mm(B[5][:, 16:32], T.J77[:], nh, False, True, "J77 NH", "B5")
        tt(T.A5[:], B[4][:, 16:32], nh, A.mult, r="NH", w="A5", b="B4")
        ts(T.ZS[:, c0 + 256:c0 + ZW], T.T2[:], 4096, A.min, r="T2", w="Zb")
        send("C%d" % t, nxt, T.ZM[:, c0 + 256:c0 + ZW], T.ZS[:, c0 + 256:c0 + ZW], r="Zb")
        send("Z%d" % t, nxt, T.ZM[:, c0:c0 + 256], T.ZS[:, c0:c0 + 256], r="Za")
        tt(T.SUM[:], B[4][:, 0:16], T.A5[:], A.add, r="A5", w="SUM", b="B4")
        if not last:
            ts(T.S15[:], T.SUM[:], 15, A.bitwise_and, r="SUM", w="S15")
        ts(T.SI[:], T.SUM[:], 4095, A.bitwise_and, r="SUM", w="SI")
        if last:
            act(T.MF[:], popped(t)[0], F.Identity, bias=2048.0, r=popped(t)[1], w="MF")
            cp(T.NU[:], B[5][:, 0:16], w="NU", b="B5")
            cp(T.FO[:, 24:40], B[5][:, 0:16], w="FOn", b="B5")
            cp(T.FO[:, 8:24], T.SI[:], r="SI", w="FOs")
            act(T.MS[:], T.M01[:].indirect(T.NU[:]), r="M01 NU", w="MS")
        else:
            for i in range(16):
                mm(B[6][:, 0:1], T.ONE[:], T.NH[:, i:i + 1], i == 0, i == 15, "ONE NH", "B6")
            act(T.WN[:], popped(t)[0], r=popped(t)[1], w="WN")

    def columns(t):
        tail, n = T.ZM[:, ZW * t + 256:ZW * t + ZW], 2 if t == TV - 1 else 1
        for k_ in range(n):
            c = 32 if t % 2 else 16 * k_
            mm(B[4][:, 32 + 16 * k_:48 + 16 * k_], IDB, T.BA[:, c:c + 16], True, False, "IDX BA%d" % (t % 2), "B4")
            mm(B[4][:, 32 + 16 * k_:48 + 16 * k_], IDB if n == 2 else T.ROT[:], tail, False, True, "CM%d IDX ROTa ROTb" % t, "B4")

    def columns_out(n):
        cp(T.CX[:, 0:n], B[4][:, 32:32 + n], w="CX", b="B4")

    def halves(ea):
        act(T.XT[:, 0:ea], T.X[:].indirect(T.CX[:, 0:ea // 16]), F.Identity, scale=0.5, bias=31.75, r="CX " + XK, w="XTa")
        ts(T.XT[:, ea:256], T.X[:].indirect(T.CX[:, ea // 16:16]), 0.5, A.mult, 31.75, A.add, r="CX " + XK, w="XTb")

    def means(m):
        v(V.tensor_tensor_scan, T.XU[:], T.XT[:], T.ZM[:, ZW * m:ZW * m + 256], 255.0, A.min, A.add, r="XTa XTb ZM%d" % m, w="XU")

    def change(e0, e1, lo, cols, xk):
        tt(T.X[:, lo:8192].indirect(T.CX[:, cols + e0 // 16:cols + e1 // 16]), T.XU[:, e0:e1], T.NEG[:, e0:e1], A.add, r="XU NEG CX", w=xk)

    for t in range(TV):
        bulk(t)
        if t == 0:
            late_consts()
        decode(t)
        if t == TV - 1:
            break
        u = t + 1
        act(T.WX[:], T.MX2[:].indirect(T.OF[:, 32:48]), scale=8192.0, r="MX2 MXz OF", w="WX")
        col_of_ls(u, lambda: later_consts(t), lambda: None, lambda: seeds_out(u))
        lists(1, ["WN", "WX"], True)
        lists(0, ["WN"], False)
        list_out(1, u)
        send("H%d" % u, nxt, T.HM[:, 128 * u:128 * u + 128], slot(u)[0], r="HS%d" % u)
        columns(t)
        letters()
        act(T.WS[:, WW * u + 24:WW * u + 40], B[5][:, 0:16], F.Relu, scale=-1.0, bias=15.0, w="Wn%d" % u, b="B5")
        act(T.AT[:], B[6][:, 0:1], F.Identity, scale=2.0 ** -12, bias=2055.52, w="AT", b="B6")
        columns_out(16)
        halves(128)
        list_out(0, u)
        send("L%d" % u, nxt, T.LLM[:, 128 * u:128 * u + 128], slot(u)[1], r="LS%d" % u)
        words_out(u)
        send("W%d" % u, nxt, landing(u), slot(u)[2], r="Ww%d Ws%d Wn%d Wz%d" % (u, u, u, u))
        act(T.AR[:], B[6][:, 0:1], F.Identity, scale=-2.0 ** -12, bias=T.AT[:], r="AT", w="AR", b="B6")
        act(T.THL[:], T.M0B[:], F.Identity, scale=T.AR[:], bias=C["thy"], r="M0B AR thy", w="THL")
        means(t)
        change(0, 256, 0, 0, XK)
        moved_by_dma(u)

    act(T.ES[:], T.FO[:].indirect(T.SV[:, 16:32]), r="FOz FOs FOn SV16a SV16b", w="ES")
    for k_ in range(2):
        mm(B[1][:, 16 * k_:16 * k_ + 16], T.ES[:, 128 * k_:128 * k_ + 128], T.RR[:, 32:48], True, True, "ES RR1", "B1")
    tt(T.YW[:], T.MF[:], T.MS[:], A.mult, r="MF MS", w="YW")
    dma("oyw", T.yw[:], T.YW[:], r="YW")
    act(T.YO[:], B[1][:, 0:32], w="YO", b="B1")
    dma("oyn", T.ys[:], T.YO[:, 0:16], r="YO")
    dma("oyn", T.yn[:], T.YO[:, 16:32], r="YO")
    columns(TV - 1)
    columns_out(32)
    halves(128)
    means(TV - 1)
    for k_ in range(4):
        lo = 1024 * k_
        change(64 * k_, 64 * k_ + 64, lo, 16, " ".join("X%d" % i for i in range(k_, 4)) + " XD XE")
        if k_ != 2:
            lo = min(lo, 2048)
            dma("oyx", T.yx[:, lo:1024 * k_ + 1024], T.X[:, lo:1024 * k_ + 1024], r="X%d X%d" % (lo // 1024, k_))
    for sem, n in tot.items():
        if known["g"].get(sem, 0) < n:
            g.wait_ge(T.sem[sem], n)
